import numpy as np, ml_dtypes
CORES = [78,86,94,102,110,118]
N = 6
import mx_ref
BF = ml_dtypes.bfloat16
def entries(a):
    return np.ascontiguousarray(a.T).reshape(-1)
def table(e):
    return np.ascontiguousarray(np.reshape(e, (-1, 16)).T).astype(np.int32)
def cols(t, e):
    v = np.concatenate([t.reshape(128, -1, 4), np.zeros((128, 1, 4), BF)], axis=1)
    return np.ascontiguousarray(v[:, e]).reshape(128, -1)
def cut(t, i, w=512):
    return t[:, w * i:w * i + w]
def f(rng, *shape):
    return mx_ref.flush((rng.standard_normal(shape, dtype=np.float32) * np.exp2(rng.integers(-2, 3, shape[:-1] + (1,)))).astype(BF))
def wide(rng, *shape, cols=0):
    v = rng.standard_normal(shape, dtype=np.float32) * np.exp2(rng.integers(-12, 13, shape)).astype(np.float32)
    if cols: v *= np.repeat(np.exp2(rng.integers(-cols, cols + 1, shape[:-2] + (1, shape[-1] // 4))) * (rng.random(shape[:-2] + (1, shape[-1] // 4)) > 0.0625), 4, axis=-1).astype(np.float32)
    return mx_ref.flush(v.astype(BF))
T, V, M, CAPP, R, O = 384, 160, 256, 48, 3, 2
START = np.repeat(np.arange(N), V)
def loose(rng, at, to, who, but=-1):
    to = to.copy(); n = np.zeros((N, N), int); np.add.at(n, (at, to), 1)
    for i in rng.permutation(who):
        q = rng.integers(0, N)
        if q != but and n[:, q].sum() < M and (q == at[i] or n[at[i], q] < CAPP): n[at[i], to[i]] -= 1; n[at[i], q] += 1; to[i] = q
    return to
def turn(rng, at):
    to = at.copy(); far = 1 + rng.permutation(N - 1)
    for s in range(N):
        k = rng.permutation(np.flatnonzero(at == s))
        for i in range(min(N - 1, len(k) // CAPP)): to[k[CAPP * i:CAPP * i + CAPP]] = (s + far[i]) % N
    return to
def collect(rng, at, e):
    to = at.copy(); k = rng.permutation(np.flatnonzero(at == e))[M - (N - 1) * CAPP:]
    to[k] = (e + 1 + np.arange(len(k)) % (N - 1)) % N
    for s in range(N):
        if s != e: to[rng.permutation(np.flatnonzero(at == s))[:CAPP]] = e
    return to
def spill(rng, at, to, who, ranks):
    to = to.copy(); n = np.zeros((N, N), int); others = np.setdiff1d(np.arange(N * V), who); np.add.at(n, (at[others], to[others]), 1)
    for i in rng.permutation(who):
        q = ranks[np.argmin(np.where(n[at[i], ranks] < CAPP, n[:, ranks].sum(axis=0), N * V))]
        n[at[i], q] += 1; to[i] = q
    return to
def lists(rng, a, share=0.25):
    nx = rng.integers(0, N * T, (N, 2 * T)); free = [list(rng.permutation(2 * T)) for r in range(N)]
    way = np.zeros((R - 1, N * V), int)
    for k in range(R - 2, -1, -1):
        goal = a[k + 1] if k == R - 2 else a[k + 1] * T + way[k + 1] // 2
        known = {}
        for i in rng.permutation(N * V):
            s = int(a[k][i]); L = known.setdefault((s, int(goal[i])), [])
            if not L or rng.random() >= share:
                L.append(free[s].pop()); way[k, i] = L[-1]
            else: way[k, i] = L[rng.integers(0, len(L))]
        if k < R - 2: nx[a[k], way[k]] = goal
    nx[a[R - 2], way[R - 2]] = a[R - 1] * T + rng.integers(0, T, N * V)
    st = (way[0] // 2).reshape(N, V); bt = sum((way[k] % 2) << k for k in range(R - 1)).reshape(N, V)
    return {"nx": np.stack([table(e) for e in nx]), "st": np.stack([table(e) for e in st]), "bt": np.stack([table(e) for e in bt])}
def setup_inputs(rng):
    a = [START]
    for k in range(R - 1): a.append(loose(rng, a[k], a[k], np.arange(N * V)))
    return {"x": f(rng, N, 128, 4 * T), "w": f(rng, N, 128, R * O * 512), **lists(rng, a)}
def setup_inputs_through(rng):
    h = rng.integers(1, N); a = [START, START.copy(), (START + h) % N]
    for s in range(N):
        for g, k in enumerate(np.array_split(V * s + rng.permutation(V), -(-V // CAPP))): a[1][k] = (s + g) % N
    return {**setup_inputs(rng), **lists(rng, a)}
def setup_inputs_far(rng):
    a = [START]
    for k in range(R - 1): a.append(turn(rng, a[k]))
    a[R - 1] = loose(rng, a[R - 2], a[R - 1], np.flatnonzero(a[R - 1] == a[R - 2]))
    return {**setup_inputs(rng), **lists(rng, a)}
def setup_inputs_gather(rng):
    p = rng.permutation(N); home, end, bare = p[:3]; a = [START, START.copy()]
    for j, s in enumerate(p[2:]): a[1][rng.permutation(np.flatnonzero(START == s))[:min(CAPP, max(0, M - V - j * CAPP))]] = home
    to = collect(rng, a[1], end)
    to = spill(rng, a[1], to, np.flatnonzero(((a[1] == end) & (to != end)) | (to == bare)), np.append(p[3:], home))
    a.append(loose(rng, a[1], to, np.flatnonzero((to == a[1]) & (a[1] != end)), but=bare))
    return {**setup_inputs(rng), **lists(rng, a, share=0.75)}
def setup_inputs_stay(rng):
    p = rng.integers(0, N); a = [START, collect(rng, START, p)]
    a.append(loose(rng, a[1], a[1], np.flatnonzero(a[1] != p)))
    return {**setup_inputs(rng), **lists(rng, a)}
def setup_inputs_spread(rng):
    d = setup_inputs(rng); d["x"] = wide(rng, N, 128, 4 * T, cols=8); return d
def follow(nx, st, bt):
    n = np.concatenate([entries(t) for t in nx]); bits = np.concatenate([entries(t) for t in bt])
    at = [np.concatenate([entries(st[r]) + r * T for r in range(N)])]
    for k in range(R - 1): at.append(n[2 * at[k] + (bits >> k & 1)])
    return at
def check_inputs(d):
    b = []
    for name, top in (("nx", N * T), ("st", T), ("bt", 2 ** (R - 1))):
        if d[name].min() < 0 or d[name].max() >= top: b.append(name)
    if b: return b
    at = [t // T for t in follow(d["nx"], d["st"], d["bt"])]
    for k in range(R):
        if np.bincount(at[k], minlength=N).max() > M: b.append("walkers on a rank at step " + str(k))
    for k in range(R - 1):
        n = np.zeros((N, N), int); np.add.at(n, (at[k], at[k + 1]), 1); np.fill_diagonal(n, 0)
        if n.max() > CAPP: b.append("walkers from a rank to another from step " + str(k))
    return b
def reference(x, w, nx, st, bt):
    nodes = np.concatenate([x[r] for r in range(N)], axis=1)
    at = follow(nx, st, bt)
    y = np.zeros((N, 128, O * M), np.float32); ids = np.full((N, 2, M), -1, np.float32)
    for e in range(N):
        m = np.flatnonzero(at[R - 1] // T == e)
        ids[e, 0, :len(m)] = m // V; ids[e, 1, :len(m)] = m % V
        for k in range(R):
            c = np.full(M, -1); c[:len(m)] = at[k][m]
            q = mx_ref.quantize(cols(nodes, c))
            for o in range(O): y[e][:, M * o:M * o + M] += mx_ref.matmul(mx_ref.quantize(np.ascontiguousarray(cut(w[e], k * O + o))), q)
    return {"y": y, "id": ids}

@@ -1,0 +1,534 @@
+from concourse.bass import DstId, RemoteDMATransfer
+from concourse.mybir import dt, AluOpType, AxisListType, ActivationFunctionType
+
+N, TN, V, M, CAPP, NO = 6, 384, 160, 256, 48, 2
+REM = CAPP * (N - 1)
+N1 = REM + V
+ZC = 128
+BX, BA = ZC, ZC + TN
+BL = BA + N1
+BW = BL + 2 * REM
+T1 = REM + M
+FN0, FN1, FN2, FID = 8, 9, 10, 11
+
+_F, _I, _U, _C, _S = "float32", "int32", "uint16", "float8_e4m3fn_x4", "uint8"
+SCRATCH, POOL = {}, {}
+
+
+def _add(dtype, **shapes):
+    for name, shape in shapes.items():
+        SCRATCH[name] = ("sbuf", [128] + (list(shape) if isinstance(shape, tuple) else [shape]), dtype)
+
+
+def _pool(buf, dtype, **widths):
+    at = 0
+    for name, w in widths.items():
+        POOL[name] = (buf, at, w)
+        at += w
+    _add(dtype, **{buf: at})
+
+
+_add(_I, ci=8, st0=10, bt0=10, btg=10, stA=10, nxr=768, nxA=48)
+_add(_F, cc=48, oh=16, ones=V, iot=2304, nxT=776, ctab=776, ctb=768, ztab=400, tabA=16, io6=96, PM=96)
+_add(_F, Rt=(12, 2, 16), RT=384)
+_add(_F, n1r=V, nxa=V, nd0=(10, 32), nt0=(10, 32), S0=800, S0t=(15, 32))
+_add(_U, offe=10, offS=10, off0=10, offi=16, nxo=48)
+_add(_I, ai0=V)
+_add(_F, mk0=V, cn0=V, zd0=(10, 32), zt0=(10, 32), za0=(10, 4), zb0=(10, 2))
+_add(_F, L1=(6, 12), L1h=(3, 10), L2=(6, 12), L2h=(3, 10))
+_add(_U, offE=10, offA=10, offN=10)
+_add(_I, rr=V, ia=10)
+_add(_F, rk=V, nd1=(10, 32), nt1=(10, 32), M1b=V, mk1=V, cn1=V, z1=V, zd1=(10, 32), zt1=(10, 32), pay1=V, E0=V, E=V, S1=T1 + V,
+     S1d=(15, 32), S1t=(15, 32), X1=(5, 2, 3), Y1=(5, 2, 3), Z1=(5, 2, 3))
+_add(_F, xb=32, XA=96, XM=96, yb=32, YA=96, YM=96, fa1=(10, 8), fb1=(10, 4), fc1=(10, 2))
+_add(_U, off1=10, off2=30)
+_add(_F, r2=V, mk2=V, cn2=V, z2=V, zd2=(10, 32), zt2=(10, 32), ta2=(10, 2), pay2=V, S2=M + V, S2d=(16, 32), S2t=(16, 32),
+     ga=(16, 3), gb=(16, 3), gc=(16, 3), n01=(2, 16), X2=(4, 16), Y2=(4, 16), idtab=968, idt=M, yo0=M, yo1=M)
+_add(_U, off20=10, offF=64)
+_pool("pooli", _I, i0=40, si0=10, k0=10, h0=10)
+_pool("poolf", _F, e0=60, b1g=10, u0=10, x1=1, x2=1, p1=1, p2=1, q1=1, q2=1, pw0=16, L1a=10, L1b=10, L2a=10, L2b=10,
+      fd1=10, tb2=10, gd=16, ge2=16)
+_add("bfloat16", xt=4 * (ZC + TN), wt=3072)
+for _n, _w in (("x", ZC + TN), ("w", 768), ("w0", V), ("sl1", REM), ("A", N1 + TN), ("sl2", 2 * REM), ("B", BW),
+               ("p0", M), ("p1", M), ("p2", M)):
+    SCRATCH[_n + "q"] = ("sbuf", [128, _w], _C)
+    SCRATCH[_n + "s"] = ("sbuf", [128, _w], _S)
+SCRATCH["ps_0"] = ("psum", [128, 512], _F)
+SCRATCH["ps_1"] = ("psum", [128, 512], _F)
+
+SEMAPHORES = ["qv", "qs", "qp", "qk", "dst0", "dbt0", "dbtg", "dnx", "dstA", "dnxA", "dx", "dw", "dxA", "dxB", "dwA", "dwB", "dAB",
+              "did", "dy0", "dy1", "am1", "ac1", "am2", "ac2", "loc"]
+
+add, sub, mul, mx, mn = AluOpType.add, AluOpType.subtract, AluOpType.mult, AluOpType.max, AluOpType.min
+eq, ge, gt, lt, ne = AluOpType.is_equal, AluOpType.is_ge, AluOpType.is_gt, AluOpType.is_lt, AluOpType.not_equal
+shr, band = AluOpType.arith_shift_right, AluOpType.bitwise_and
+Copy, Ident = ActivationFunctionType.Copy, ActivationFunctionType.Identity
+
+
+def pos(a, q):
+    return q if q < a else q - 1
+
+
+def rank_program(g, core, T, topo):
+    me = T.rank_of(core)
+    if me is None:
+        return
+    others = [(me + 1 + k) % N for k in range(N - 1)]
+
+    eng = {"v": g.vector, "s": g.scalar, "p": g, "k": g.tensor, "y": g.sync}
+    know = {q: {} for q in eng}
+    count, wr, rd = {"loc": 0}, {}, {}
+
+    def need(q, evs):
+        for sem, val, snap in sorted(evs, key=lambda e: -len(e[2])):
+            if know[q].get(sem, 0) < val:
+                eng[q].wait_ge(T.sem[sem], val)
+                for a, b in list(snap.items()) + [(sem, val)]:
+                    if know[q].get(a, 0) < b:
+                        know[q][a] = b
+
+    def op(q, call, reads=(), writes=(), sem="", inc=1, total=None):
+        evs = []
+        for k in reads:
+            evs += wr.get(k, [])
+        for k in writes:
+            evs += wr.get(k, []) + rd.get(k, [])
+        best = {}
+        for e in evs:
+            if e[0] not in best or best[e[0]][1] < e[1]:
+                best[e[0]] = e
+        need(q, list(best.values()))
+        ins = call()
+        if sem is None:
+            return
+        sem = sem or "q" + q
+        ins.then_inc(T.sem[sem], inc)
+        count[sem] = count.get(sem, 0) + inc
+        ev = (sem, total or count[sem], dict(know[q]))
+        for k in writes:
+            wr[k] = [ev]
+            rd[k] = []
+        for k in reads:
+            rd.setdefault(k, []).append(ev)
+
+    def o(name, lo=None, hi=None, st=None, k=None, p=None):
+        ps = slice(None) if p is None else slice(p[0], p[1])
+        keys = (k,) if isinstance(k, str) else k or (name,)
+        if name in POOL:
+            name, at, w = POOL[name]
+            lo, hi = at + (lo or 0), at + (w if hi is None else hi)
+        return (keys, T[name][ps, slice(lo, hi, st)])
+
+    def o3(name, lo=None, hi=None, k=None, p=None):
+        ps = slice(None) if p is None else slice(p[0], p[1])
+        return ((k,) if isinstance(k, str) else k or (name,), T[name][ps, :, slice(lo, hi)])
+
+    def o1(name, j, k=None):
+        return ((k or name,), T[name][:, :, j])
+
+    def o2(name, j, k=None, p=None):
+        ps = slice(None) if p is None else slice(p[0], p[1])
+        return ((k or name,), T[name][ps, j, :])
+
+    def ci(j):
+        return o("ci", j, j + 1, k="ci%d" % j)
+
+    def cc(j):
+        return o("cc", j, j + 1, k="cc%d" % j)
+
+    def oh(j):
+        return o("oh", j, j + 1)
+
+    def ind(win, off):
+        return (win[0] + off[0], win[1].indirect(off[1]))
+
+    def cp(out, in_):
+        op("v", lambda: g.vector.tensor_copy(out[1], in_[1]), in_[0], out[0])
+
+    def ms(out, c):
+        op("v", lambda: g.vector.memset(out[1], c), (), out[0])
+
+    def tt(out, a, b, f):
+        op("v", lambda: g.vector.tensor_tensor(out[1], a[1], b[1], f), a[0] + b[0], out[0])
+
+    def ts(out, a, s1, f1, s2=None, f2=None):
+        rk = a[0] + (s1[0] if isinstance(s1, tuple) else ()) + (s2[0] if isinstance(s2, tuple) else ())
+        v1 = s1[1] if isinstance(s1, tuple) else s1
+        v2 = s2[1] if isinstance(s2, tuple) else s2
+        if f2 is None:
+            op("v", lambda: g.vector.tensor_scalar(out[1], a[1], v1, None, f1), rk, out[0])
+        else:
+            op("v", lambda: g.vector.tensor_scalar(out[1], a[1], v1, v2, f1, f2), rk, out[0])
+
+    def scan(out, d0, d1, init):
+        op("v", lambda: g.vector.tensor_tensor_scan(out[1], d0[1], d1[1], init[1], mul, add), d0[0] + d1[0] + init[0], out[0])
+
+    def red(out, in_):
+        op("v", lambda: g.vector.tensor_reduce(out[1], in_[1], AxisListType.X, add), in_[0], out[0])
+
+    def tr(out, in_):
+        op("v", lambda: g.vector.transpose(out[1], in_[1]), in_[0], out[0])
+
+    def act(out, in_, f=Copy, scale=None, bias=None):
+        kw, rk = {}, ()
+        for n, v in (("scale", scale), ("bias", bias)):
+            if isinstance(v, tuple):
+                rk, v = rk + v[0], v[1]
+            if v is not None:
+                kw[n] = v
+        op("s", lambda: g.scalar.activation(out[1], in_[1], f, **kw), in_[0] + rk, out[0])
+
+    def scatter(win, off, in_):
+        op("v", lambda: g.vector.tensor_copy(win[1].indirect(off[1]), in_[1]), win[0] + off[0] + in_[0], win[0])
+
+    def pick(outn, winn, off, wkeys, hi=None):
+        op("v", lambda: g.vector.tensor_copy(T[outn + "q"][:].bitcast(dt.uint32), T[winn + "q"][:, 0:hi].bitcast(dt.uint32).indirect(off[1])),
+           tuple(x + "q" for x in wkeys) + off[0], (outn + "q",))
+        op("s", lambda: g.scalar.activation(T[outn + "s"][:], T[winn + "s"][:, 0:hi].indirect(off[1]), Copy),
+           tuple(x + "s" for x in wkeys) + off[0], (outn + "s",))
+
+    def quant(outn, lo, hi, src, a, b, skeys, key):
+        op("v", lambda: g.vector.quantize_mx(T[outn + "q"][:, lo:hi], T[outn + "s"][:, lo:hi], T[src][:, 4 * a:4 * b]), skeys, (key + "q", key + "s"))
+
+    def wq(j):
+        quant("w", 128 * j, 128 * j + 128, "wt", 128 * j, 128 * j + 128, ("wt",), "w%d" % j)
+
+    def move(outn, at, srcn, lo, hi, rkey, key, sem):
+        op("y", lambda: g.sync.dma_start(T[outn + "q"][:, at:at + hi - lo].bitcast(dt.uint8), T[srcn + "q"][:, lo:hi].bitcast(dt.uint8)),
+           (rkey + "q",), (key + "q",), sem=sem, inc=16, total=32)
+        op("y", lambda: g.sync.dma_start(T[outn + "s"][:, at:at + hi - lo], T[srcn + "s"][:, lo:hi]), (rkey + "s",), (key + "s",), sem=sem, inc=16, total=32)
+
+    def fan(reads, src, dst, rsem):
+        def call():
+            trs = []
+            for k, q in enumerate(others[:4]):
+                c = T.cores[q]
+                rid, pid, _ = topo.addr(c)
+                m = sum(1 << e for e in topo.engines(core, c)[k::4])
+                trs.append(RemoteDMATransfer(dst_ids=[DstId(rid=rid, pnc=pid)], dma_engine_mask=m, remote_sem=T.sem[rsem], src=src(q), dst=dst(q)))
+            g.remote_dma_fused(trs, local_sem=T.sem.loc)
+            c = T.cores[others[4]]
+            rid, pid, _ = topo.addr(c)
+            g.remote_dma(dst(others[4]), src(others[4]), T.sem[rsem], T.sem.loc, pid, rid, topo.mask(core, c))
+        op("p", call, reads, (), sem=None)
+        count["loc"] += 16
+
+    def everyone(name, rsem):
+        fan((name + "o",), lambda q: T[name][:, me, 0:10], lambda q: T[name][:, me, 0:10], rsem)
+
+    def columns(name, land, at, w, rsem):
+        def src(n, q):
+            return T[n][:, w * pos(me, q):w * pos(me, q) + w]
+
+        def dst(n, q):
+            return T[n][:, at + w * pos(q, me):at + w * pos(q, me) + w]
+        fan((name + "q",), lambda q: src(name + "q", q).bitcast(dt.uint8), lambda q: dst(land + "q", q).bitcast(dt.uint8), rsem)
+        fan((name + "s",), lambda q: src(name + "s", q), lambda q: dst(land + "s", q), rsem)
+
+    for s_, v_, ks in (("am1", 16, ("L1i",)), ("ac1", 32, ("Alq", "Als")), ("am2", 16, ("L2i",)), ("ac2", 32, ("Blq", "Bls"))):
+        count[s_] = v_
+        for k in ks:
+            wr[k] = [(s_, v_, {})]
+
+    def dma(q, out, in_, sem, total=None):
+        op(q, lambda: eng[q].dma_start(out[1], in_[1]), in_[0], out[0], sem=sem, inc=16, total=total)
+
+    P = (0, 16)
+    dma("y", o("st0", p=P), ((), T.st[:]), "dst0")
+    dma("s", o("bt0", p=P), ((), T.bt[:]), "dbt0")
+    ms(o("nxr"), 0)
+    dma("y", o("nxr", p=(0, 1)), ((), T.nx[:]), "dnx")
+    dma("y", o("xt", 4 * ZC, 4 * (ZC + TN), k="xtx"), ((), T.x[:]), "dx")
+    ms(o("btg"), 0)
+    for k in range(8):
+        dma("y", o("stA", p=(16 * k, 16 * k + 16), k="stA%d" % k), ((), T.st[:]), "dstA", 128)
+    dma("y", o("btg", p=(16 * me, 16 * me + 16)), ((), T.bt[:]), "dbtg")
+    for k in range(8):
+        dma("y", o("nxA", p=(16 * k, 16 * k + 16), k="nxA%d" % k), ((), T.nx[:]), "dnxA", 128)
+    stA = (tuple("stA%d" % k for k in range(8)), T.stA[:])
+    nxA = (tuple("nxA%d" % k for k in range(8)), T.nxA[:])
+    dma("y", o("wt"), ((), T.w[:]), "dw")
+
+    def iota(out, pattern, base=0, mult=0):
+        op("p", lambda: g.iota(out[1], pattern, base, mult, allow_small_or_imprecise_dtypes=True), (), out[0])
+    iotk = ("iota", "iotb", "iotc", "iotd", "iote")
+    (R_M, R_E, R_B1, R_RM, R_B2, R_ZB, R_CB, R_RB, R_K1, R_K2, R_K3, R_J) = range(12)
+    allR = tuple("R%d" % c for c in range(12))
+    iota(ci(0), [[1, 1]], 0, 1)
+    iota(o("iot", 0, 512, k="iota"), [[1, 512]])
+    iota((("R%d" % R_J,), T.Rt[:, R_J, :, :]), [[0, 2], [1, 16]])
+    iota((allR[:R_J], T.Rt[:, 0:R_J, :, :]), [[0, 32 * R_J]])
+    (JF, J, G, OD, EV, OV, X1, X2, X3, X4, GM, GM2, BASE0, BASE1, J1, A1, A2, A3, A4, A5, X5, X6, GV) = range(23)
+    hh = 16 * (me % 2)
+    ms(o("offe"), 0)
+    ts(ci(1), ci(0), 31, band)
+    ts(ci(2), ci(0), 15, band)
+    ts(ci(3), ci(0), 4, shr)
+    ms(o("ones"), 1.0)
+    cp(cc(JF), ci(1))
+    cp(cc(J), ci(2))
+    cp(cc(G), ci(3))
+    ms(o3("nd0", 16 - hh, 32 - hh, "nd0z"), 0.0)
+
+    def R(c):
+        return o("RT", 32 * c, 32 * c + 1)
+
+    def rows(c, a, b, v):
+        act((("R%d" % c,), T.Rt[:, c, :, a:b]), o("iot", 0, 2 * (b - a), k="iota"), Ident, scale=0.0, bias=float(v))
+
+    def steps(c, a, b, m, v):
+        if b > a:
+            act((("R%d" % c,), T.Rt[:, c, :, a:b]), (("R%d" % R_J,), T.Rt[:, R_J, :, a:b]), Ident, scale=float(m), bias=float(v))
+    rows(R_M, 0, 16, 99)
+    rows(R_M, 8, 9, 0)
+    rows(R_M, 11, 12, -1)
+    steps(R_E, 0, 6, 1, 0)
+    for a_, b_, v_ in ((me, me + 1, 77), (6, 7, me), (7, 8, -1), (9, 16, 77), (11, 12, -1)):
+        rows(R_E, a_, b_, v_)
+    for c, w_, at_ in ((R_B1, CAPP, 0), (R_B2, 2 * CAPP, BL)):
+        steps(c, 0, me, w_, at_ - 1)
+        steps(c, me + 1, N, w_, at_ - w_ - 1)
+    for c, a_, b_, v_ in ((R_B1, 6, 7, REM - 1), (R_B1, 7, 8, T1 - 1), (R_B1, 8, 9, BA - 1), (R_RM, 0, 7, 1), (R_B2, 6, 7, -1), (R_B2, 7, 8, M - 1),
+                          (R_ZB, 0, 7, 1), (R_ZB, FN2, FN2 + 1, BX), (R_CB, FN1, FN1 + 1, BX - CAPP), (R_RB, 8, 10, 1), (R_RB, 11, 12, 1),
+                          (R_K1, 0, 6, 1000), (R_K2, me, me + 1, 1000), (R_K2, 8, 10, 1000000), (R_K3, 10, 16, 1000000)):
+        rows(c, a_, b_, v_)
+
+    def i0(j):
+        return o("i0", 10 * j, 10 * j + 10, k="i0%d" % j, p=P)
+
+    def e0(j):
+        return o("e0", 10 * j, 10 * j + 10, k="e0%d" % j, p=P)
+    ts(i0(1), o("st0", p=P), 3, shr)
+    ts(e0(1), o("st0", p=P), 96.0, mul)
+    ts(i0(0), o("bt0", p=P), 1, band)
+    ts(e0(3), i0(1), -767.0, mul)
+    ts(e0(2), i0(0), 48.0, mul)
+    tt(e0(4), e0(1), e0(3), add)
+    ts(cc(GM), cc(G), float(me), eq)
+    tt(e0(4), e0(4), e0(2), add)
+    ts(cc(X2), cc(JF), float(me), gt, -48.0, mul)
+    cp(o("offe", p=P), e0(4))
+    ts(cc(X3), cc(JF), float(me), eq, float(REM - CAPP * me), mul)
+    cp(o("n1r"), ind(o("nxr"), o("offe")))
+    op("p", lambda: g.partition_broadcast(T.nxa[:], T.n1r[0:1, :], 128), ("n1r",), ("nxa",))
+    ts(cc(X1), cc(JF), 48.0, mul, -1.0, add)
+    tt(cc(X2), cc(X2), cc(X3), add)
+    ts(cc(X4), cc(JF), 6.0, eq, 256.0, mul)
+    tt(cc(X1), cc(X1), cc(X2), add)
+    i4 = o("i0", 30, 40, k="i03")
+    ts(i4, o("btg"), 1, shr)
+    ts(cc(OD), cc(JF), 16.0, ge, 16.0, mul)
+    tt(cc(BASE0), cc(X1), cc(X4), add)
+    ts(o("b1g"), i4, 1.0, add, cc(GM), mul)
+    ts(cc(GM2), cc(GM), 2.0, mul)
+    ts(cc(EV), cc(JF), 16.0, lt)
+    ts(cc(OV), cc(JF), 16.0, ge)
+    ts(cc(GV), cc(G), float(V), mul)
+    ts(cc(A2), cc(G), float(me), gt, -48.0, mul)
+    cp(o3("nd0", hh, hh + 16, "nd0x"), o("nxa"))
+    ts(o("ai0"), o("nxa"), -191.5, add, 1.0 / TN, mul)
+    tr((("nt0",), T.nt0[:]), (("nd0x", "nd0z"), T.nd0[:]))
+    ts(o("mk0"), o("ai0"), cc(JF), eq)
+    ts(o("u0"), o1("nt0", 0), cc(GM2), mul)
+    scan(o("cn0"), o("ones"), o("mk0"), cc(BASE0))
+    tt((("L1o",), T.L1[:, me, 0:10]), o("u0"), o("b1g"), add)
+    everyone("L1", "am1")
+    iota(o("S0", 0, 480, k="S0"), [[0, 480]])
+    cp(o("nxo"), nxA)
+    tt(o3("zd0", 0, 16, "zd0l"), o("mk0"), o("cn0"), mul)
+    act(o3("zd0", 16, 32, "zd0h"), o3("zd0", 0, 16, "zd0l"))
+    ms(o("xt", 0, 4 * ZC, k="xtz"), 0.0)
+    tr((("zt0",), T.zt0[:]), (("zd0l", "zd0h"), T.zd0[:]))
+    ts(o("offS"), stA, float(ZC), add)
+    tt(o3("za0", 0, 4), o3("zt0", 0, 4), o3("zt0", 4, 8), add)
+    ts(o("oh"), o("iot", 0, 16, k="iota"), cc(J), eq)
+    tt(o3("zb0", 0, 2), o3("za0", 0, 2), o3("za0", 2, 4), add)
+    ts(cc(J1), cc(J), 1.0, add)
+    tt(o("si0"), o1("zb0", 0), o1("zb0", 1), add)
+    quant("x", 0, ZC + TN, "xt", 0, ZC + TN, ("xtx", "xtz"), "x")
+    ts(o("k0"), o("si0"), 496, band)
+    for n in ("nxT", "ctab"):
+        act(o(n, 0, 1, k=n + "z"), o("iot", 0, 1, k="iota"))
+        act(o(n, 769, 776, k=n + "y"), o("iot", 0, 7, k="iota"), scale=0.0)
+    act(o("iot", 512, 1024, k="iotb"), o("iot", 0, 512, k="iota"), Ident, bias=512.0)
+    act(o("iot", 1024, 1536, k="iotc"), o("iot", 0, 512, k="iota"), Ident, bias=1024.0)
+    act(o("iot", 1536, 2048, k="iotd"), o("iot", 0, 512, k="iota"), Ident, bias=1536.0)
+    act(o("iot", 2048, 2304, k="iote"), o("iot", 0, 256, k="iota"), Ident, bias=2048.0)
+    act(o("nxT", 1, 769, k="nxTa"), ind(o("iot", k=iotk), o("nxo")), Ident, bias=1.0)
+    tt(o("h0"), o("si0"), o("k0"), add)
+    pick("w0", "x", o("offS"), ("x",))
+    ts(o("off0"), o("h0"), cc(OD), add)
+    iota(o("ctb"), [[1, TN], [0, 2]])
+    iota(o("io6"), [[0, 6], [1, 16]])
+    move("A", N1, "x", ZC, ZC + TN, "x", "Ax", "dxA")
+    move("B", 0, "x", 0, ZC + TN, "x", "Bx", "dxB")
+    move("A", REM, "w0", 0, V, "w0", "Aw", "dwA")
+    move("B", BA + REM, "w0", 0, V, "w0", "Bw", "dwB")
+    scatter(o("S0"), o("off0"), o("iot", 1, V + 1, k="iota"))
+    act(cc(A1), cc(GM), scale=oh(8))
+    act(cc(A3), cc(G), Ident, scale=48.0, bias=cc(A2))
+    act(cc(X3), cc(GV), scale=oh(11))
+    act(cc(A4), cc(GM), Ident, scale=float(REM - CAPP * me), bias=cc(A3))
+    act(cc(A5), cc(A4), Ident, scale=oh(8), bias=cc(X3))
+    op("v", lambda: g.vector.transpose(T.S0t[:], T.S0[:, 0:480]), ("S0",), ("S0t",))
+    tt(o("pw0", 0, 15), o1("S0t", 0), o1("S0t", 16), add)
+    ts(o("offi", 0, 15), o("pw0", 0, 15), -1.0, add, 0.0, mx)
+    pick("sl1", "w0", o("offi", 0, 15), ("w0",))
+
+    def total(f, out):
+        tt((("%sh" % f,), T[f + "h"][:]), (("%si" % f, "%so" % f), T[f][:, 0:3, 0:10]), (("%si" % f, "%so" % f), T[f][:, 3:6, 0:10]), add)
+        tt(o(f + "a"), o2(f + "h", 0), o2(f + "h", 1), add)
+        tt(out, o(f + "a"), o2(f + "h", 2), add)
+
+    def before(c, b, A, PMb, x, mask, base, out):
+        ts(o(b), o("ones", 0, 32), c, mul)
+        tr(o(A, 0, 32, k=A), o(b))
+        act(o(A, 32, 64, k=A + "2", p=(64, 96)), o(A, 0, 32, k=A, p=(32, 64)))
+        cp(o(A, 32, 64, k=A + "1", p=(32, 64)), o(A, 0, 32, k=A, p=(0, 32)))
+        cp(o(A, 64, 96, k=A + "3", p=(64, 96)), o(A, 0, 32, k=A, p=(0, 32)))
+        tt(o(PMb), o(A, k=(A, A + "1", A + "2", A + "3")), o("PM"), mul)
+        red(o(x), o(PMb))
+        ts(out, o(x), mask, mul, base, add)
+
+    def quarters(y, xv, keys):
+        op("v", lambda: g.vector.tensor_tensor(T[y][0:32], T[xv][0:32], T[xv][32:64], add), keys, (y,))
+        op("v", lambda: g.vector.tensor_tensor(T[y][0:32], T[y][0:32], T[xv][64:96], add), keys + (y,), (y,))
+
+    def spread(off, zv, keys):
+        for q in range(4):
+            op("v", lambda: g.vector.tensor_copy(T[off][32 * q:32 * q + 32], T[zv][0:32]), keys, (off + "%d" % q,))
+        return tuple(off + "%d" % q for q in range(4))
+
+    total("L1", o("L1b"))
+    ts(o("offE"), o("L1b"), float(-2 * TN * me), add, float(2 * TN + 1), mn)
+    nxT = o("nxT", k=("nxTa", "nxTz", "nxTy"))
+    ts(o("ia"), o("L1b"), -(TN + 0.5), add, 0.5 / TN, mul)
+    cp(o("rk"), ind(nxT, o("offE")))
+    ts(o("offA"), o("ia"), 1.0, add)
+    ts(o3("nd1", 0, 16, "nd1l"), o("rk"), cc(EV), mul)
+    act(o3("nd1", 16, 32, "nd1h"), o("rk"), scale=cc(OV))
+    ts(o("rr"), o("rk"), -(TN + 1) / 2.0, add, 1.0 / TN, mul)
+    tr((("nt1",), T.nt1[:]), (("nd1l", "nd1h"), T.nd1[:]))
+    ts(o("PM"), o("io6"), cc(J), eq)
+    tt((("L2o",), T.L2[:, me, 0:10]), o1("nt1", 0), o1("nt1", 16), add)
+    everyone("L2", "am2")
+    columns("sl1", "A", 0, CAPP, "ac1")
+    iota(o("XA"), [[0, 96]])
+    iota(o("YA"), [[0, 96]])
+    iota(o("idtab", 0, 1, k="idz"), [[0, 1]], -1)
+    iota(o("idtab", 1, 961, k="idn"), [[0, N], [1, V]])
+    iota(o("idtab", 1, 961, k="idn", p=(0, 1)), [[1, N], [0, V]])
+
+    tr(o("RT"), (allR, T.Rt[:]))
+    act(cc(X5), cc(A1), Ident, scale=-1.0, bias=R(R_M))
+    act(cc(X6), cc(A1), Ident, scale=-1.0, bias=R(R_E))
+    act(cc(BASE1), cc(A5), Ident, bias=R(R_B1))
+    ts(o("PM", 0, 16, k="PM"), o("PM", 0, 16, k="PM"), cc(OV), mul)
+    ts(o("tabA"), o("iot", 0, 16, k="iota"), cc(J1), ne, R(R_K1), mul)
+    ts(o("pw0"), o("iot", 0, 16, k="iota"), float(me + 1), eq, R(R_K2), mul)
+    ms(o("PM", 16, 32, k="PM"), 0.0)
+    ts(o("mk1"), o("rr"), cc(X5), mn, cc(X6), eq)
+    tt(o("tabA"), o("tabA"), o("pw0"), add)
+    red(o("x1"), o("mk1"))
+
+    before(o("x1"), "xb", "XA", "XM", "p1", R(R_RM), cc(BASE1), o("q1"))
+    act(o("ctab", 1, 769, k="cta"), o("ctb"), Ident, scale=oh(FN1), bias=R(R_CB))
+    act(o("S1", 0, REM, k="S1"), o("iot", 0, REM, k="iota"), scale=0.0)
+    act(o("tabA"), o("tabA"), Ident, bias=R(R_K3))
+    scan(o("cn1"), o("ones"), o("mk1"), o("q1"))
+    tt(o("z1"), o("mk1"), o("cn1"), mul)
+    ts(o3("zd1", 0, 16, "zd1l"), o("z1"), cc(EV), mul)
+    act(o3("zd1", 16, 32, "zd1h"), o("z1"), scale=cc(OV))
+    tt(o("pay1"), ind(o("ctab", k=("cta", "ctabz", "ctaby")), o("offE")), o("cn1"), add)
+    tr((("zt1",), T.zt1[:]), (("zd1l", "zd1h"), T.zd1[:]))
+    tt(o3("fa1"), o3("zt1", 0, 8), o3("zt1", 16, 24), add)
+    tt(o3("fb1"), o3("fa1", 0, 4), o3("fa1", 4, 8), add)
+    tt(o3("fc1"), o3("fb1", 0, 2), o3("fb1", 2, 4), add)
+    act(o("M1b"), ind(o("tabA"), o("offA")))
+    act(o("E0"), o("pay1"), scale=R(R_RB))
+    tt(o("fd1"), o1("fc1", 0), o1("fc1", 1), add)
+    cp(o("off1"), o("fd1"))
+    scatter(o("S1"), o("off1"), o("pay1"))
+    act(o3("S1d", 16, 32, "S1dh"), o("S1", 0, REM))
+    cp(o3("S1d", 0, 16, "S1dl"), o("S1", 0, REM))
+    tt(o("E"), o("E0"), o("M1b"), mn)
+    tr((("S1t",), T.S1t[:]), (("S1dl", "S1dh"), T.S1d[:]))
+    for k, j in ((0, FN0), (1, FN1)):
+        tt((("X1%d" % k,), T.X1[:, :, k, :]), o1("S1t", j), o1("S1t", j + 16), add)
+    quarters("Y1", "X1", ("X10", "X11"))
+    ts((("Z1a",), T.Z1[0:32, :, 0, :]), (("Y1",), T.Y1[0:32, :, 0, :]), float(-BA), add)
+    ts((("Z1b",), T.Z1[0:32, :, 1, :]), (("Y1",), T.Y1[0:32, :, 1, :]), float(N1 - BX + CAPP), add)
+    k2 = spread("off2", "Z1", ("Z1a", "Z1b"))
+    act(o("ztab", 1, 385, k="zta"), o("iot", 0, TN, k="iota"), Ident, scale=oh(FN2), bias=R(R_ZB))
+    act(o("ztab", 0, 1, k="ztz"), oh(7))
+    act(o("ztab", 385, 386, k="zty"), oh(7))
+    act(o("S2", 0, M, k="S2"), o("iot", 0, M, k="iota"), scale=0.0)
+    pick("sl2", "A", (k2, T.off2[:]), ("Al", "Aw", "Ax"))
+    columns("sl2", "B", BL, 2 * CAPP, "ac2")
+    move("B", BA, "A", 0, REM, "Al", "Ba", "dAB")
+
+    total("L2", o("L2b"))
+    ts(o("offN"), o("L2b"), float(-TN * me), add, float(TN + 1), mn)
+    wq(0)
+    tt(o("r2"), ind(o("ztab", 0, 392, k=("zta", "ztz", "zty")), o("offN")), o("E"), add)
+    tt(o("mk2"), o("r2"), o("M1b"), gt)
+    red(o("x2"), o("mk2"))
+    before(o("x2"), "yb", "YA", "YM", "p2", R(R_RM), R(R_B2), o("q2"))
+    wq(1)
+    scan(o("cn2"), o("ones"), o("mk2"), o("q2"))
+    tt(o("z2"), o("mk2"), o("cn2"), mul)
+    wq(2)
+    ts(o3("zd2", 0, 16, "zd2l"), o("z2"), cc(EV), mul)
+    act(o3("zd2", 16, 32, "zd2h"), o("z2"), scale=cc(OV))
+    tt(o("pay2"), o("z2"), o("r2"), add)
+    tr((("zt2",), T.zt2[:]), (("zd2l", "zd2h"), T.zd2[:]))
+    tt(o3("ta2"), o3("zt2", 6, 8), o3("zt2", 22, 24), add)
+    wq(3)
+    tt(o("tb2"), o1("ta2", 0), o1("ta2", 1), add)
+    wq(4)
+    cp(o("off20"), o("tb2"))
+    wq(5)
+    scatter(o("S2"), o("off20"), o("pay2"))
+    act(o3("S2d", 16, 32, "S2dh"), o("S2", 0, M))
+    cp(o3("S2d", 0, 16, "S2dl"), o("S2", 0, M))
+    tr((("S2t",), T.S2t[:]), (("S2dl", "S2dh"), T.S2d[:]))
+    tt(o3("ga"), o3("S2t", 0, 3), o3("S2t", 3, 6), add)
+    tt(o3("gb"), o3("S2t", 16, 19), o3("S2t", 19, 22), add)
+    tt(o2("n01", 0, "n0"), o1("S2t", FN0), o1("S2t", FN0 + 16), add)
+    tt(o3("gc"), o3("ga"), o3("gb"), add)
+    tt(o2("n01", 1, "n1"), o1("S2t", FN1), o1("S2t", FN1 + 16), add)
+    tt(o("gd"), o1("gc", 0), o1("gc", 1), add)
+    tt(o2("X2", 2, "X22"), o1("S2t", FN2), o1("S2t", FN2 + 16), add)
+    tt(o("ge2"), o("gd"), o1("gc", 2), add)
+    tt(o2("X2", 3, "X23"), o1("S2t", FID), o1("S2t", FID + 16), add)
+    tt(o2("X2", 0, "X20"), o2("n01", 0, "n0"), o("ge2"), add)
+    tt(o2("X2", 1, "X21"), o2("n01", 1, "n1"), o("ge2"), add)
+    quarters("Y2", "X2", ("X20", "X21", "X22", "X23"))
+    q0 = (0, 32)
+    ts(o2("Y2", 0, "Y2n", p=q0), o2("Y2", 0, p=q0), -float(N), add)
+    ts(o2("Y2", 1, "Y2m", p=q0), o2("Y2", 1, p=q0), float(CAPP - N), add)
+    kF = spread("offF", "Y2", ("Y2", "Y2n", "Y2m"))
+    off = [(kF, T.offF[:, 16 * k:16 * k + 16]) for k in range(4)]
+
+    def product(k, last):
+        n = "p%d" % k
+        for oo in range(NO):
+            a = 128 * (k * NO + oo)
+            op("k", lambda: g.tensor.matmul_mx(T["ps_%d" % oo][:, 0:M], T.wq[:, a:a + 128], T.ws[:, a:a + 128], T[n + "q"][:], T[n + "s"][:], k == 2, last),
+               ("w%dq" % (k * NO + oo), "w%ds" % (k * NO + oo), n + "q", n + "s"), ("ps_%d" % oo,) if last else ())
+    pick("p2", "B", off[2], ("Bx",), ZC + TN)
+    product(2, False)
+    Bk = ("Bx", "Ba", "Bw", "Bl")
+    pick("p0", "B", off[0], Bk)
+    product(0, False)
+    pick("p1", "B", off[1], Bk)
+    product(1, True)
+    act(o("idt"), ind(o("idtab", k=("idz", "idn")), off[3]))
+    cp(o("yo0"), o("ps_0", 0, M))
+    act(o("yo1"), o("ps_1", 0, M))
+    dma("y", (("y0",), T.y[:, 0:M]), o("yo0"), "dy0")
+    dma("s", (("y1",), T.y[:, M:2 * M]), o("yo1"), "dy1")
+    op("y", lambda: g.sync.dma_start(T["id"][:], T.idt[0:2, :]), ("idt",), ("ido",), sem="did", inc=16)
+    for sem, c in count.items():
+        if know["p"].get(sem, 0) < c:
+            g.wait_ge(T.sem[sem], c)

@@ -3,13 +3,15 @@ from concourse.mybir import dt, AluOpType, AxisListType, ActivationFunctionType
 
 N, TN, V, M, CAPP, NO = 6, 384, 160, 256, 48, 2
 REM = CAPP * (N - 1)
-N1 = REM + V
-ZC = 128
-BX, BA = ZC, ZC + TN
-BL = BA + N1
+ZC = 16
+BA = ZC + TN
+BL = BA + REM
 BW = BL + 2 * REM
-T1 = REM + M
-FN0, FN1, FN2, FID = 8, 9, 10, 11
+K = 2048.0
+BIG = 4096.0
+R_N2, R_LAND, R_SLOT, R_OUT, R_C0, R_C1 = 0, 1, 7, 12, 14, 15
+R_ELSE, R_ID, R_C2 = 0, 12, 13
+NB = 11
 
 _F, _I, _U, _C, _S = "float32", "int32", "uint16", "float8_e4m3fn_x4", "uint8"
 SCRATCH, POOL = {}, {}
@@ -28,45 +30,31 @@ def _pool(buf, dtype, **widths):
     _add(dtype, **{buf: at})
 
 
-_add(_I, ci=8, st0=10, bt0=10, btg=10, stA=10, nxr=768, nxA=48)
-_add(_F, cc=48, oh=16, ones=V, iot=2304, nxT=776, ctab=776, ctb=768, ztab=400, tabA=16, io6=96, PM=96)
-_add(_F, Rt=(12, 2, 16), RT=384)
-_add(_F, n1r=V, nxa=V, nd0=(10, 32), nt0=(10, 32), S0=800, S0t=(15, 32))
-_add(_U, offe=10, offS=10, off0=10, offi=16, nxo=48)
-_add(_I, ai0=V)
-_add(_F, mk0=V, cn0=V, zd0=(10, 32), zt0=(10, 32), za0=(10, 4), zb0=(10, 2))
-_add(_F, L1=(6, 12), L1h=(3, 10), L2=(6, 12), L2h=(3, 10))
-_add(_U, offE=10, offA=10, offN=10)
-_add(_I, rr=V, ia=10)
-_add(_F, rk=V, nd1=(10, 32), nt1=(10, 32), M1b=V, mk1=V, cn1=V, z1=V, zd1=(10, 32), zt1=(10, 32), pay1=V, E0=V, E=V, S1=T1 + V,
-     S1d=(15, 32), S1t=(15, 32), X1=(5, 2, 3), Y1=(5, 2, 3), Z1=(5, 2, 3))
-_add(_F, xb=32, XA=96, XM=96, yb=32, YA=96, YM=96, fa1=(10, 8), fb1=(10, 4), fc1=(10, 2))
-_add(_U, off1=10, off2=30)
-_add(_F, r2=V, mk2=V, cn2=V, z2=V, zd2=(10, 32), zt2=(10, 32), ta2=(10, 2), pay2=V, S2=M + V, S2d=(16, 32), S2t=(16, 32),
-     ga=(16, 3), gb=(16, 3), gc=(16, 3), n01=(2, 16), X2=(4, 16), Y2=(4, 16), idtab=968, idt=M, yo0=M, yo1=M)
-_add(_U, off20=10, offF=64)
-_pool("pooli", _I, i0=40, si0=10, k0=10, h0=10)
-_pool("poolf", _F, e0=60, b1g=10, u0=10, x1=1, x2=1, p1=1, p2=1, q1=1, q2=1, pw0=16, L1a=10, L1b=10, L2a=10, L2b=10,
-      fd1=10, tb2=10, gd=16, ge2=16)
-_add("bfloat16", xt=4 * (ZC + TN), wt=3072)
-for _n, _w in (("x", ZC + TN), ("w", 768), ("w0", V), ("sl1", REM), ("A", N1 + TN), ("sl2", 2 * REM), ("B", BW),
-               ("p0", M), ("p1", M), ("p2", M)):
+_add(_I, st0=10, bt0=10, b1t=16, nxr=768, nxA=48, r1i=16, vi=12, sli=10)
+_add(_F, cc=48, oh=16, ramp=480, Kt=192, KT=192, K2=(2, 16), KU=32, tq1=(5, 2, 3), Fm=8, Fb=8, Ft=8, F=2304, TAB=776, capT=776,
+     ztab=1160, ptab=736, rs=32 * NB, mD=64, D=64, DT=72, idtab=968, idt=M, yo0=M, yo1=M)
+_add(_F, zp0=192, zp1=192, zp2=192, Tz=32 * NB, SS=32 * NB, Ts=544, S0=416, S1=416, S2=448,
+     G0=V, G1=V, G2=V, cn0=V, cn1=V, cn2=V, strow=V, Mt=V, cap1=V, E=V, cap2=V,
+     L1o=16, L1=88, L2=(6, 20), L2h=(3, 11), Ha=64, Hb=64, tq=64, yq=64)
+_add(_U, selA=32, selB=16, selP=2, selL=2, offr=10, off0=16, offi=16, nxo=48, offE=16, off1=16, off2=32,
+     offN=10, offS=10, off20=10, offF=64)
+_pool("poolu", _U, offe=10, offSt=10)
+_pool("pooli", _I, ia=10, ib=10)
+_pool("poolf", _F, e1=10, e2=10, e3=10, e4=10, e5=10, x1=1, tot=1, L2a=11, in2=1, pa=16, pb=16)
+_add("bfloat16", xt=4 * BA, wt=3072)
+for _n, _w in (("x", BA), ("w", 768), ("sl1", REM), ("A", BL), ("sl2", 2 * REM), ("B", BW), ("p0", M), ("p1", M), ("p2", M)):
     SCRATCH[_n + "q"] = ("sbuf", [128, _w], _C)
     SCRATCH[_n + "s"] = ("sbuf", [128, _w], _S)
 SCRATCH["ps_0"] = ("psum", [128, 512], _F)
 SCRATCH["ps_1"] = ("psum", [128, 512], _F)
 
-SEMAPHORES = ["qv", "qs", "qp", "qk", "dst0", "dbt0", "dbtg", "dnx", "dstA", "dnxA", "dx", "dw", "dxA", "dxB", "dwA", "dwB", "dAB",
+SEMAPHORES = ["qv", "qs", "qp", "qk", "dst0", "dbt0", "dnx", "dnxA", "dx", "dw", "dxA", "dxB", "dAB", "dL1",
               "did", "dy0", "dy1", "am1", "ac1", "am2", "ac2", "loc"]
 
 add, sub, mul, mx, mn = AluOpType.add, AluOpType.subtract, AluOpType.mult, AluOpType.max, AluOpType.min
-eq, ge, gt, lt, ne = AluOpType.is_equal, AluOpType.is_ge, AluOpType.is_gt, AluOpType.is_lt, AluOpType.not_equal
+eq, ge, gt, le = AluOpType.is_equal, AluOpType.is_ge, AluOpType.is_gt, AluOpType.is_le
 shr, band = AluOpType.arith_shift_right, AluOpType.bitwise_and
 Copy, Ident = ActivationFunctionType.Copy, ActivationFunctionType.Identity
-
-
-def pos(a, q):
-    return q if q < a else q - 1
 
 
 def rank_program(g, core, T, topo):
@@ -74,6 +62,9 @@ def rank_program(g, core, T, topo):
     if me is None:
         return
     others = [(me + 1 + k) % N for k in range(N - 1)]
+
+    def pos(a, q):
+        return (q - a - 1) % N
 
     eng = {"v": g.vector, "s": g.scalar, "p": g, "k": g.tensor, "y": g.sync}
     know = {q: {} for q in eng}
@@ -119,22 +110,14 @@ def rank_program(g, core, T, topo):
             lo, hi = at + (lo or 0), at + (w if hi is None else hi)
         return (keys, T[name][ps, slice(lo, hi, st)])
 
-    def o3(name, lo=None, hi=None, k=None, p=None):
-        ps = slice(None) if p is None else slice(p[0], p[1])
-        return ((k,) if isinstance(k, str) else k or (name,), T[name][ps, :, slice(lo, hi)])
+    def blk(name, lo, hi, st, k):
+        return ((k,) if isinstance(k, str) else k, T[name][:, lo:hi:st, :])
 
-    def o1(name, j, k=None):
-        return ((k or name,), T[name][:, :, j])
+    names = {}
 
-    def o2(name, j, k=None, p=None):
-        ps = slice(None) if p is None else slice(p[0], p[1])
-        return ((k or name,), T[name][ps, j, :])
-
-    def ci(j):
-        return o("ci", j, j + 1, k="ci%d" % j)
-
-    def cc(j):
-        return o("cc", j, j + 1, k="cc%d" % j)
+    def cc(n):
+        j = names.setdefault(n, len(names))
+        return o("cc", j, j + 1, k="cc" + n)
 
     def oh(j):
         return o("oh", j, j + 1)
@@ -160,8 +143,9 @@ def rank_program(g, core, T, topo):
         else:
             op("v", lambda: g.vector.tensor_scalar(out[1], a[1], v1, v2, f1, f2), rk, out[0])
 
-    def scan(out, d0, d1, init):
-        op("v", lambda: g.vector.tensor_tensor_scan(out[1], d0[1], d1[1], init[1], mul, add), d0[0] + d1[0] + init[0], out[0])
+    def scan(out, d0, d1, init, f0, f1):
+        ik, iv = init if isinstance(init, tuple) else ((), init)
+        op("v", lambda: g.vector.tensor_tensor_scan(out[1], d0[1], d1[1], iv, f0, f1), d0[0] + d1[0] + ik, out[0])
 
     def red(out, in_):
         op("v", lambda: g.vector.tensor_reduce(out[1], in_[1], AxisListType.X, add), in_[0], out[0])
@@ -169,14 +153,22 @@ def rank_program(g, core, T, topo):
     def tr(out, in_):
         op("v", lambda: g.vector.transpose(out[1], in_[1]), in_[0], out[0])
 
-    def act(out, in_, f=Copy, scale=None, bias=None):
-        kw, rk = {}, ()
+    def act(out, in_, scale=None, bias=None, acc=None):
+        kw, rk, wk = {}, (), out[0]
         for n, v in (("scale", scale), ("bias", bias)):
             if isinstance(v, tuple):
                 rk, v = rk + v[0], v[1]
             if v is not None:
                 kw[n] = v
-        op("s", lambda: g.scalar.activation(out[1], in_[1], f, **kw), in_[0] + rk, out[0])
+        if acc:
+            kw["accum_out"], wk = acc[1], wk + acc[0]
+        op("s", lambda: g.scalar.activation(out[1], in_[1], Copy if bias is None else Ident, **kw), in_[0] + rk, wk)
+
+    def fill(out, n, v=0.0):
+        act(out, o("ramp", 0, n), scale=0.0, bias=v)
+
+    def iota(out, pattern, base=0, mult=0):
+        op("p", lambda: g.iota(out[1], pattern, base, mult, allow_small_or_imprecise_dtypes=True), (), out[0])
 
     def scatter(win, off, in_):
         op("v", lambda: g.vector.tensor_copy(win[1].indirect(off[1]), in_[1]), win[0] + off[0] + in_[0], win[0])
@@ -187,16 +179,13 @@ def rank_program(g, core, T, topo):
         op("s", lambda: g.scalar.activation(T[outn + "s"][:], T[winn + "s"][:, 0:hi].indirect(off[1]), Copy),
            tuple(x + "s" for x in wkeys) + off[0], (outn + "s",))
 
-    def quant(outn, lo, hi, src, a, b, skeys, key):
-        op("v", lambda: g.vector.quantize_mx(T[outn + "q"][:, lo:hi], T[outn + "s"][:, lo:hi], T[src][:, 4 * a:4 * b]), skeys, (key + "q", key + "s"))
+    def quant(outn, lo, hi, src, skeys, key):
+        op("v", lambda: g.vector.quantize_mx(T[outn + "q"][:, lo:hi], T[outn + "s"][:, lo:hi], T[src][:, 4 * lo:4 * hi]), skeys, (key + "q", key + "s"))
 
-    def wq(j):
-        quant("w", 128 * j, 128 * j + 128, "wt", 128 * j, 128 * j + 128, ("wt",), "w%d" % j)
-
-    def move(outn, at, srcn, lo, hi, rkey, key, sem):
-        op("y", lambda: g.sync.dma_start(T[outn + "q"][:, at:at + hi - lo].bitcast(dt.uint8), T[srcn + "q"][:, lo:hi].bitcast(dt.uint8)),
+    def move(outn, srcn, lo, hi, rkey, key, sem):
+        op("y", lambda: g.sync.dma_start(T[outn + "q"][:, lo:hi].bitcast(dt.uint8), T[srcn + "q"][:, lo:hi].bitcast(dt.uint8)),
            (rkey + "q",), (key + "q",), sem=sem, inc=16, total=32)
-        op("y", lambda: g.sync.dma_start(T[outn + "s"][:, at:at + hi - lo], T[srcn + "s"][:, lo:hi]), (rkey + "s",), (key + "s",), sem=sem, inc=16, total=32)
+        op("y", lambda: g.sync.dma_start(T[outn + "s"][:, lo:hi], T[srcn + "s"][:, lo:hi]), (rkey + "s",), (key + "s",), sem=sem, inc=16, total=32)
 
     def fan(reads, src, dst, rsem):
         def call():
@@ -212,9 +201,6 @@ def rank_program(g, core, T, topo):
             g.remote_dma(dst(others[4]), src(others[4]), T.sem[rsem], T.sem.loc, pid, rid, topo.mask(core, c))
         op("p", call, reads, (), sem=None)
         count["loc"] += 16
-
-    def everyone(name, rsem):
-        fan((name + "o",), lambda q: T[name][:, me, 0:10], lambda q: T[name][:, me, 0:10], rsem)
 
     def columns(name, land, at, w, rsem):
         def src(n, q):
@@ -233,297 +219,274 @@ def rank_program(g, core, T, topo):
     def dma(q, out, in_, sem, total=None):
         op(q, lambda: eng[q].dma_start(out[1], in_[1]), in_[0], out[0], sem=sem, inc=16, total=total)
 
-    P = (0, 16)
-    dma("y", o("st0", p=P), ((), T.st[:]), "dst0")
-    dma("s", o("bt0", p=P), ((), T.bt[:]), "dbt0")
+    Tz = (("Tze", "Tzo"), T.Tz[:])
+    Ts = (("Tse", "Tso"), T.Ts[:])
+
+    def turn(zp):
+        tr(o("Tz", 0, 192, k="Tze"), o(zp, 0, 192, k=(zp, zp + "p", zp + "r")))
+        tr(o("Tz", 192, 352, k="Tzo"), o(zp, 16, 176))
+
+    def turn_slots(win, even):
+        tr(o("Ts", 256, 256 + 32 * even, k="Tse"), o(win, 0, 32 * even))
+        tr(o("Ts", 0, 256, k="Tso"), o(win, 16, 272))
+
+    def pads(zp):
+        ms(o(zp, 0, 16, k=zp + "p"), 0.0)
+        ms(o(zp, 176, 192, k=zp + "r"), 0.0)
+
+    def sums():
+        scan(o("SS"), o("rs", k=("rs", "rs0", "rs1")), Tz, 0.0, mul, add)
+
+    def gather_lists(off, row, rows):
+        n = 16 * rows
+        cp(o("Ha", 0, n), ind(Ts, o("selA", row, row + rows)))
+        tt(o("Hb", 0, n), ind(Ts, o("selA", 16 + row, 16 + row + rows)), o("Ha", 0, n), add)
+        if rows == 2:
+            n = 30
+            for k in range(2):
+                tt((("tq%d" % k,), T.tq1[0:64, :, k, :]), o("Hb", 16 * k, 16 * k + 15, p=(0, 64)), o("Hb", 16 * k, 16 * k + 15, p=(64, 128)), add)
+            tq = [(("tq0", "tq1"), T.tq1[32 * h:32 * h + 32]) for h in range(2)]
+        else:
+            tt(o("tq", 0, n, p=(0, 64)), o("Hb", 0, n, p=(0, 64)), o("Hb", 0, n, p=(64, 128)), add)
+            tq = [o("tq", 0, n, p=(32 * h, 32 * h + 32)) for h in range(2)]
+        for h in range(2):
+            tt(o("yq", 0, n, k="yq%d" % h, p=(32 * h, 32 * h + 32)), tq[0], tq[1], add)
+        for h in range(2):
+            cp(o(off, 0, n, k=off + "%d" % h, p=(64 * h, 64 * h + 64)), o("yq", 0, n, k=("yq0", "yq1"), p=(0, 64)))
+        return (off + "0", off + "1")
+
+    Q = 32 * (me // 2)
+    PQ = (Q, Q + 32)
     ms(o("nxr"), 0)
-    dma("y", o("nxr", p=(0, 1)), ((), T.nx[:]), "dnx")
-    dma("y", o("xt", 4 * ZC, 4 * (ZC + TN), k="xtx"), ((), T.x[:]), "dx")
-    ms(o("btg"), 0)
-    for k in range(8):
-        dma("y", o("stA", p=(16 * k, 16 * k + 16), k="stA%d" % k), ((), T.st[:]), "dstA", 128)
-    dma("y", o("btg", p=(16 * me, 16 * me + 16)), ((), T.bt[:]), "dbtg")
+    for h in range(2):
+        dma("y", o("st0", p=(Q + 16 * h, Q + 16 * h + 16), k="st%d" % h), ((), T.st[:]), "dst0", 32)
+        dma("s", o("bt0", p=(Q + 16 * h, Q + 16 * h + 16), k="bt%d" % h), ((), T.bt[:]), "dbt0", 32)
+    st = o("st0", p=PQ, k=("st0", "st1"))
+    bt = o("bt0", p=PQ, k=("bt0", "bt1"))
+    dma("y", o("nxr", p=(16 * me, 16 * me + 1)), ((), T.nx[:]), "dnx")
+    dma("y", o("xt", 4 * ZC, 4 * BA, k="xtx"), ((), T.x[:]), "dx")
     for k in range(8):
         dma("y", o("nxA", p=(16 * k, 16 * k + 16), k="nxA%d" % k), ((), T.nx[:]), "dnxA", 128)
-    stA = (tuple("stA%d" % k for k in range(8)), T.stA[:])
     nxA = (tuple("nxA%d" % k for k in range(8)), T.nxA[:])
     dma("y", o("wt"), ((), T.w[:]), "dw")
 
-    def iota(out, pattern, base=0, mult=0):
-        op("p", lambda: g.iota(out[1], pattern, base, mult, allow_small_or_imprecise_dtypes=True), (), out[0])
-    iotk = ("iota", "iotb", "iotc", "iotd", "iote")
-    (R_M, R_E, R_B1, R_RM, R_B2, R_ZB, R_CB, R_RB, R_K1, R_K2, R_K3, R_J) = range(12)
-    allR = tuple("R%d" % c for c in range(12))
-    iota(ci(0), [[1, 1]], 0, 1)
-    iota(o("iot", 0, 512, k="iota"), [[1, 512]])
-    iota((("R%d" % R_J,), T.Rt[:, R_J, :, :]), [[0, 2], [1, 16]])
-    iota((allR[:R_J], T.Rt[:, 0:R_J, :, :]), [[0, 32 * R_J]])
-    (JF, J, G, OD, EV, OV, X1, X2, X3, X4, GM, GM2, BASE0, BASE1, J1, A1, A2, A3, A4, A5, X5, X6, GV) = range(23)
-    hh = 16 * (me % 2)
-    ms(o("offe"), 0)
-    ts(ci(1), ci(0), 31, band)
-    ts(ci(2), ci(0), 15, band)
-    ts(ci(3), ci(0), 4, shr)
-    ms(o("ones"), 1.0)
-    cp(cc(JF), ci(1))
-    cp(cc(J), ci(2))
-    cp(cc(G), ci(3))
-    ms(o3("nd0", 16 - hh, 32 - hh, "nd0z"), 0.0)
-
-    def R(c):
-        return o("RT", 32 * c, 32 * c + 1)
-
-    def rows(c, a, b, v):
-        act((("R%d" % c,), T.Rt[:, c, :, a:b]), o("iot", 0, 2 * (b - a), k="iota"), Ident, scale=0.0, bias=float(v))
-
-    def steps(c, a, b, m, v):
-        if b > a:
-            act((("R%d" % c,), T.Rt[:, c, :, a:b]), (("R%d" % R_J,), T.Rt[:, R_J, :, a:b]), Ident, scale=float(m), bias=float(v))
-    rows(R_M, 0, 16, 99)
-    rows(R_M, 8, 9, 0)
-    rows(R_M, 11, 12, -1)
-    steps(R_E, 0, 6, 1, 0)
-    for a_, b_, v_ in ((me, me + 1, 77), (6, 7, me), (7, 8, -1), (9, 16, 77), (11, 12, -1)):
-        rows(R_E, a_, b_, v_)
-    for c, w_, at_ in ((R_B1, CAPP, 0), (R_B2, 2 * CAPP, BL)):
-        steps(c, 0, me, w_, at_ - 1)
-        steps(c, me + 1, N, w_, at_ - w_ - 1)
-    for c, a_, b_, v_ in ((R_B1, 6, 7, REM - 1), (R_B1, 7, 8, T1 - 1), (R_B1, 8, 9, BA - 1), (R_RM, 0, 7, 1), (R_B2, 6, 7, -1), (R_B2, 7, 8, M - 1),
-                          (R_ZB, 0, 7, 1), (R_ZB, FN2, FN2 + 1, BX), (R_CB, FN1, FN1 + 1, BX - CAPP), (R_RB, 8, 10, 1), (R_RB, 11, 12, 1),
-                          (R_K1, 0, 6, 1000), (R_K2, me, me + 1, 1000), (R_K2, 8, 10, 1000000), (R_K3, 10, 16, 1000000)):
-        rows(c, a_, b_, v_)
-
-    def i0(j):
-        return o("i0", 10 * j, 10 * j + 10, k="i0%d" % j, p=P)
-
-    def e0(j):
-        return o("e0", 10 * j, 10 * j + 10, k="e0%d" % j, p=P)
-    ts(i0(1), o("st0", p=P), 3, shr)
-    ts(e0(1), o("st0", p=P), 96.0, mul)
-    ts(i0(0), o("bt0", p=P), 1, band)
-    ts(e0(3), i0(1), -767.0, mul)
-    ts(e0(2), i0(0), 48.0, mul)
-    tt(e0(4), e0(1), e0(3), add)
-    ts(cc(GM), cc(G), float(me), eq)
-    tt(e0(4), e0(4), e0(2), add)
-    ts(cc(X2), cc(JF), float(me), gt, -48.0, mul)
-    cp(o("offe", p=P), e0(4))
-    ts(cc(X3), cc(JF), float(me), eq, float(REM - CAPP * me), mul)
-    cp(o("n1r"), ind(o("nxr"), o("offe")))
-    op("p", lambda: g.partition_broadcast(T.nxa[:], T.n1r[0:1, :], 128), ("n1r",), ("nxa",))
-    ts(cc(X1), cc(JF), 48.0, mul, -1.0, add)
-    tt(cc(X2), cc(X2), cc(X3), add)
-    ts(cc(X4), cc(JF), 6.0, eq, 256.0, mul)
-    tt(cc(X1), cc(X1), cc(X2), add)
-    i4 = o("i0", 30, 40, k="i03")
-    ts(i4, o("btg"), 1, shr)
-    ts(cc(OD), cc(JF), 16.0, ge, 16.0, mul)
-    tt(cc(BASE0), cc(X1), cc(X4), add)
-    ts(o("b1g"), i4, 1.0, add, cc(GM), mul)
-    ts(cc(GM2), cc(GM), 2.0, mul)
-    ts(cc(EV), cc(JF), 16.0, lt)
-    ts(cc(OV), cc(JF), 16.0, ge)
-    ts(cc(GV), cc(G), float(V), mul)
-    ts(cc(A2), cc(G), float(me), gt, -48.0, mul)
-    cp(o3("nd0", hh, hh + 16, "nd0x"), o("nxa"))
-    ts(o("ai0"), o("nxa"), -191.5, add, 1.0 / TN, mul)
-    tr((("nt0",), T.nt0[:]), (("nd0x", "nd0z"), T.nd0[:]))
-    ts(o("mk0"), o("ai0"), cc(JF), eq)
-    ts(o("u0"), o1("nt0", 0), cc(GM2), mul)
-    scan(o("cn0"), o("ones"), o("mk0"), cc(BASE0))
-    tt((("L1o",), T.L1[:, me, 0:10]), o("u0"), o("b1g"), add)
-    everyone("L1", "am1")
-    iota(o("S0", 0, 480, k="S0"), [[0, 480]])
-    cp(o("nxo"), nxA)
-    tt(o3("zd0", 0, 16, "zd0l"), o("mk0"), o("cn0"), mul)
-    act(o3("zd0", 16, 32, "zd0h"), o3("zd0", 0, 16, "zd0l"))
+    def rows(first, *pieces):
+        ks, at = (), first
+        for pat, base, mult in pieces:
+            n = pat[0][1] * pat[1][1]
+            ks += ("Kt%d" % at,)
+            iota(o("Kt", at, at + n, k=ks[-1]), pat, base, mult)
+            at += n
+        return o("Kt", first, at, k=ks)
+    Ka = rows(0, ([[0, 2], [1, 16]], 0, 0), ([[16, 2], [0, 16]], 0, 1), ([[32, 8], [-160, 2]], 192, 0), ([[32, 8], [192, 2]], 16, 0))
+    iota(o("ramp"), [[1, 480]])
+    Kb = rows(96, ([[32, 8], [288, 2]], 0, 0), ([[32, 8], [-256, 2]], 256, 0), ([[80, 2], [8, 16]], 0, 5), ([[16, 2], [1, 16]], 16, 0))
+    iota(o("rs"), [[0, 32 * NB]], 1)
+    J, G16, B0b = (o("KT", 32 * b, 32 * b + 1, k="KTa") for b in range(3))
+    B0, SL, P16 = (o("KT", 32 * b, 32 * b + 1, k="KTb") for b in range(3, 6))
+    r16 = o("Kt", 0, 16, k="Kt0")
+    ms(o("poolu", k=("offe", "offSt")), 0)
+    ms(o("b1t"), 0)
+    tr(o("KT", 0, 96, k="KTa"), Ka)
+    pads("zp0")
+    ts(cc("GM"), G16, 16.0 * me, eq)
+    ts(o("oh"), r16, J, eq)
     ms(o("xt", 0, 4 * ZC, k="xtz"), 0.0)
-    tr((("zt0",), T.zt0[:]), (("zd0l", "zd0h"), T.zd0[:]))
-    ts(o("offS"), stA, float(ZC), add)
-    tt(o3("za0", 0, 4), o3("zt0", 0, 4), o3("zt0", 4, 8), add)
-    ts(o("oh"), o("iot", 0, 16, k="iota"), cc(J), eq)
-    tt(o3("zb0", 0, 2), o3("za0", 0, 2), o3("za0", 2, 4), add)
-    ts(cc(J1), cc(J), 1.0, add)
-    tt(o("si0"), o1("zb0", 0), o1("zb0", 1), add)
-    quant("x", 0, ZC + TN, "xt", 0, ZC + TN, ("xtx", "xtz"), "x")
-    ts(o("k0"), o("si0"), 496, band)
-    for n in ("nxT", "ctab"):
-        act(o(n, 0, 1, k=n + "z"), o("iot", 0, 1, k="iota"))
-        act(o(n, 769, 776, k=n + "y"), o("iot", 0, 7, k="iota"), scale=0.0)
-    act(o("iot", 512, 1024, k="iotb"), o("iot", 0, 512, k="iota"), Ident, bias=512.0)
-    act(o("iot", 1024, 1536, k="iotc"), o("iot", 0, 512, k="iota"), Ident, bias=1024.0)
-    act(o("iot", 1536, 2048, k="iotd"), o("iot", 0, 512, k="iota"), Ident, bias=1536.0)
-    act(o("iot", 2048, 2304, k="iote"), o("iot", 0, 256, k="iota"), Ident, bias=2048.0)
-    act(o("nxT", 1, 769, k="nxTa"), ind(o("iot", k=iotk), o("nxo")), Ident, bias=1.0)
-    tt(o("h0"), o("si0"), o("k0"), add)
-    pick("w0", "x", o("offS"), ("x",))
-    ts(o("off0"), o("h0"), cc(OD), add)
-    iota(o("ctb"), [[1, TN], [0, 2]])
-    iota(o("io6"), [[0, 6], [1, 16]])
-    move("A", N1, "x", ZC, ZC + TN, "x", "Ax", "dxA")
-    move("B", 0, "x", 0, ZC + TN, "x", "Bx", "dxB")
-    move("A", REM, "w0", 0, V, "w0", "Aw", "dwA")
-    move("B", BA + REM, "w0", 0, V, "w0", "Bw", "dwB")
-    scatter(o("S0"), o("off0"), o("iot", 1, V + 1, k="iota"))
-    act(cc(A1), cc(GM), scale=oh(8))
-    act(cc(A3), cc(G), Ident, scale=48.0, bias=cc(A2))
-    act(cc(X3), cc(GV), scale=oh(11))
-    act(cc(A4), cc(GM), Ident, scale=float(REM - CAPP * me), bias=cc(A3))
-    act(cc(A5), cc(A4), Ident, scale=oh(8), bias=cc(X3))
-    op("v", lambda: g.vector.transpose(T.S0t[:], T.S0[:, 0:480]), ("S0",), ("S0t",))
-    tt(o("pw0", 0, 15), o1("S0t", 0), o1("S0t", 16), add)
-    ts(o("offi", 0, 15), o("pw0", 0, 15), -1.0, add, 0.0, mx)
-    pick("sl1", "w0", o("offi", 0, 15), ("w0",))
+    ms(o("L1", 60, 88, k="L1z"), 0.0)
+    ts(o("selB"), r16, B0b, add, 32.0 * NB - 1, mn)
+    if me < N - 1:
+        tt(o("Fm", me + 1, N, k="Fm1"), o("oh", R_LAND + me + 1, R_LAND + N), o("oh", R_SLOT, R_OUT - me), add)
+    tt(o("Fm", 0, me + 1, k="Fm0"), o("oh", R_LAND, R_LAND + me + 1), o("oh", R_OUT - me, R_OUT + 1), add)
+    Fm = o("Fm", 0, N, k=("Fm0", "Fm1"))
+    selZ = o("selB", 0, 1)
+    pads("zp1")
+    pads("zp2")
+    act(cc("FS"), oh(R_N2), scale=K)
+    act(cc("own"), cc("GM"), scale=oh(R_C0))
+    act(cc("b0"), oh(R_C1), scale=K, bias=cc("FS"))
+    act(cc("FA"), oh(R_N2), scale=K * TN)
+    act(cc("b1"), oh(R_C0), bias=cc("b0"))
+    act(cc("base0"), J, scale=float(CAPP), bias=float(15 - CAPP * R_SLOT))
+    act(cc("b2"), cc("own"), scale=K - 1, bias=cc("b1"))
+    act(cc("k1"), oh(R_N2), scale=1.0 - BIG, bias=BIG)
+    act(o("Ft", 0, N), o("Kt", 0, N, k="Kt0"), scale=cc("FA"), bias=cc("b2"))
+    act(cc("cs"), oh(R_C1), scale=1.0 / K)
+    act(cc("k2"), cc("own"), scale=1.0 - BIG, bias=cc("k1"))
+    act(cc("ms"), cc("own"), scale=1.0 / K)
+    act(cc("k3"), oh(R_C1), scale=ZC / K - BIG, bias=cc("k2"))
+    act(cc("mb"), cc("own"), scale=-1.0, bias=1.0)
 
-    def total(f, out):
-        tt((("%sh" % f,), T[f + "h"][:]), (("%si" % f, "%so" % f), T[f][:, 0:3, 0:10]), (("%si" % f, "%so" % f), T[f][:, 3:6, 0:10]), add)
-        tt(o(f + "a"), o2(f + "h", 0), o2(f + "h", 1), add)
-        tt(out, o(f + "a"), o2(f + "h", 2), add)
+    ts(o("ia", p=PQ), st, 3, shr)
+    ts(o("e1", p=PQ), st, 96.0, mul)
+    ts(o("ib", p=PQ), bt, 1, band)
+    ts(o("e2", p=PQ), o("ia", p=PQ), -767.0, mul)
+    ts(o("e3", p=PQ), o("ib", p=PQ), 48.0, mul)
+    tt(o("e4", p=PQ), o("e1", p=PQ), o("e2", p=PQ), add)
+    ts(o("b1t", 0, 10, p=PQ), bt, 1, shr)
+    tt(o("e5", p=PQ), o("e4", p=PQ), o("e3", p=PQ), add)
+    tt(o("Fb", 0, N), Fm, o("Ft", 0, N), add)
+    cp(o("offe", p=PQ), o("e5", p=PQ))
+    ts(o("offSt", p=PQ), st, float(ZC), add)
+    ts(o("zp0", 16, 176), ind(o("nxr"), o("offe")), 2.0, mul, 1.0, add)
+    ts(cc("pr0"), J, float(R_LAND), ge)
+    turn("zp0")
+    ts(cc("pr"), J, float(R_OUT - 1), le, cc("pr0"), mul)
+    tt(o("L1o"), ind(Tz, selZ), o("b1t"), add)
+    fan(("L1o",), lambda q: T.L1o[:, 0:10], lambda q: T.L1[:, 10 * me:10 * me + 10], "am1")
+    dma("y", o("L1", 10 * me, 10 * me + 10, k="L1m"), o("L1o", 0, 10), "dL1")
 
-    def before(c, b, A, PMb, x, mask, base, out):
-        ts(o(b), o("ones", 0, 32), c, mul)
-        tr(o(A, 0, 32, k=A), o(b))
-        act(o(A, 32, 64, k=A + "2", p=(64, 96)), o(A, 0, 32, k=A, p=(32, 64)))
-        cp(o(A, 32, 64, k=A + "1", p=(32, 64)), o(A, 0, 32, k=A, p=(0, 32)))
-        cp(o(A, 64, 96, k=A + "3", p=(64, 96)), o(A, 0, 32, k=A, p=(0, 32)))
-        tt(o(PMb), o(A, k=(A, A + "1", A + "2", A + "3")), o("PM"), mul)
-        red(o(x), o(PMb))
-        ts(out, o(x), mask, mul, base, add)
-
-    def quarters(y, xv, keys):
-        op("v", lambda: g.vector.tensor_tensor(T[y][0:32], T[xv][0:32], T[xv][32:64], add), keys, (y,))
-        op("v", lambda: g.vector.tensor_tensor(T[y][0:32], T[y][0:32], T[xv][64:96], add), keys + (y,), (y,))
-
-    def spread(off, zv, keys):
-        for q in range(4):
-            op("v", lambda: g.vector.tensor_copy(T[off][32 * q:32 * q + 32], T[zv][0:32]), keys, (off + "%d" % q,))
-        return tuple(off + "%d" % q for q in range(4))
-
-    total("L1", o("L1b"))
-    ts(o("offE"), o("L1b"), float(-2 * TN * me), add, float(2 * TN + 1), mn)
-    nxT = o("nxT", k=("nxTa", "nxTz", "nxTy"))
-    ts(o("ia"), o("L1b"), -(TN + 0.5), add, 0.5 / TN, mul)
-    cp(o("rk"), ind(nxT, o("offE")))
-    ts(o("offA"), o("ia"), 1.0, add)
-    ts(o3("nd1", 0, 16, "nd1l"), o("rk"), cc(EV), mul)
-    act(o3("nd1", 16, 32, "nd1h"), o("rk"), scale=cc(OV))
-    ts(o("rr"), o("rk"), -(TN + 1) / 2.0, add, 1.0 / TN, mul)
-    tr((("nt1",), T.nt1[:]), (("nd1l", "nd1h"), T.nd1[:]))
-    ts(o("PM"), o("io6"), cc(J), eq)
-    tt((("L2o",), T.L2[:, me, 0:10]), o1("nt1", 0), o1("nt1", 16), add)
-    everyone("L2", "am2")
-    columns("sl1", "A", 0, CAPP, "ac1")
-    iota(o("XA"), [[0, 96]])
-    iota(o("YA"), [[0, 96]])
+    iota((("K2b",), T.K2[:]), [[0, 32]])
+    for a_, n_, s_, v_ in ((R_LAND, me, -96, 96 * (me - 1) - 1), (R_LAND + me, N - me, -96, 96 * (N - 1) - 1), (R_SLOT, N, CAPP, 15)):
+        if n_:
+            iota((("K2b",), T.K2[:, :, a_:a_ + n_]), [[0, 2], [s_, n_]], v_)
+    iota(o("S1", 0, 272), [[0, 272]])
     iota(o("idtab", 0, 1, k="idz"), [[0, 1]], -1)
+
+    for k in range(N):
+        act(o("F", TN * k, TN * k + TN, k="F%d" % k), o("ramp", 0, TN), scale=cc("FS"), bias=o("Fb", k, k + 1))
+    ts(o("r1i"), ind(Tz, selZ), -float(TN), add, 0.5 / TN, mul)
+    tr(o("KT", 96, 192, k="KTb"), Kb)
+    cp(o("offr"), o("r1i", 0, 10))
+    ms(o("rs", 0, None, 16, k=("rs", "rs0")), 0.0)
+    cp(o("G0"), ind(Fm, o("offr")))
+    cp(o("nxo"), nxA)
+    act(o("strow"), ind(o("ramp"), o("offSt")))
+    fill(o("S0", 0, 288), 288)
+    act(o("TAB", 1, 769, k="TABa"), ind(o("F", k=tuple("F%d" % k for k in range(N))), o("nxo")))
+    scan(o("cn0"), o("G0"), o("G0"), cc("base0"), add, mx)
+    ms(o("rs", R_SLOT, None, 16, k=("rs", "rs1")), 0.0)
+    tt(o("zp0", 16, 176), o("G0"), o("cn0"), mul)
+    quant("x", 0, BA, "xt", ("xtx", "xtz"), "x")
+    move("A", "x", 0, BA, "x", "Ax", "dxA")
+    move("B", "x", 0, BA, "x", "Bx", "dxB")
+    turn("zp0")
+    ts(o("selL", 0, 1), SL, 0.125, mul)
+    sums()
+    ts(o("selA"), o("ramp", 0, 32), B0, add)
+    cp(o("off0"), ind(o("SS"), o("selB", R_OUT, R_OUT + 1)))
+    ts(o("mD", 0, 32, k="mD0"), o("Kt", 0, 32, k="Kt0"), J, eq, cc("pr"), mul)
+    scatter(o("S0"), o("off0", 0, 10), o("strow"))
+    ts(o("mD", 32, 64, k="mD1"), o("ramp", 0, 32), P16, eq, cc("pr"), mul)
+    turn_slots("S0", 9)
+    ts(o("selP", 0, 1), B0b, float(R_LAND + me), add, 32.0 * NB - 1, mn)
+    cp(o("offi", k="offi"), ind(Ts, o("selA", 16 * (me % 2), 16 * (me % 2) + 1)))
+    ki = ("offi",)
+    for q in range(4):
+        if 32 * q != Q:
+            ki += ("offi%d" % q,)
+            op("v", lambda: g.vector.tensor_copy(T.offi[32 * q:32 * q + 32, 0:16], T.offi[Q:Q + 32, 0:16]), ("offi",), ki[-1:])
+    for c in (0, 769):
+        act(o("TAB", c, c + 1, k="TAB%d" % c), oh(R_OUT))
+    for b in range(2):
+        act(o("capT", 1 + b, 769, 2, k="capT%d" % b), o("ramp", 0, TN), scale=cc("cs"), bias=cc("k3"))
+    act(o("capT", 0, 770, 769, k="capT2"), o("ramp", 0, 2), scale=0.0, bias=cc("k3"))
+    act(o("Mt"), o("strow"), scale=cc("ms"), bias=cc("mb"))
+    ts(cc("wrap"), G16, 16.0 * me, le, float(CAPP * N), mul)
+    pick("sl1", "x", (ki, T.offi[:, 0:15]), ("x",))
+    columns("sl1", "A", BA, CAPP, "ac1")
+    tr(o("KU"), (("K2b",), T.K2[:]))
+    act(cc("c1"), G16, scale=CAPP / 16.0, bias=cc("wrap"))
+    act(cc("c2"), cc("c1"), bias=float(BA - 1 - CAPP * (me + 1)))
+    act(o("DT", 64, 65, k="DTb"), cc("c2"), scale=oh(R_C0), bias=o("KU", 0, 1))
+
+    ts(o("offE"), ind(o("L1", k=("L1i", "L1m", "L1z")), o("selL", 0, 1)), float(-2 * TN * me), add, float(2 * TN + 1), mn)
+    offE = o("offE", 0, 10)
+    act(o("G1"), ind(o("TAB", k=("TABa", "TAB0", "TAB769")), offE), acc=o("x1"))
+    tt(o("cap1"), ind(o("capT", k=("capT0", "capT1", "capT2")), offE), o("Mt"), mul)
+    ts(o("D"), o("mD", k=("mD0", "mD1")), o("x1"), mul)
+    tr(o("DT", 0, 64), o("D"))
+    red(o("tot"), o("DT", 0, 32))
+    pre = (("pre",), T.L2[:, me, 0:1])
+    red(pre, o("DT", 32, 65, k=("DT", "DTb")))
+    ts((("pre1",), T.L2[32:64, me, 0:1]), (("pre",), T.L2[32:64, me, 0:1]), o("tot", p=(0, 32)), add)
+    ts((("pre2",), T.L2[64:96, me, 0:1]), (("pre",), T.L2[64:96, me, 0:1]), o("tot", p=(0, 32)), add, o("tot", p=(32, 64)), add)
+    pre = (("pre", "pre1", "pre2"), pre[1])
+    scan(o("cn1"), o("G1"), o("cap1"), pre, add, mn)
+    tt(o("zp1", 16, 176), o("G1"), o("cn1"), mul)
+    turn("zp1")
+    sums()
+    cp((("L2o",), T.L2[:, me, 1:17]), ind(o("SS"), o("selB", R_SLOT - 1, R_SLOT)))
+    cp(o("off1"), ind(o("SS"), o("selB", R_OUT, R_OUT + 1)))
+    fan(("L2o",) + pre[0], lambda q: T.L2[:, me, 0:11], lambda q: T.L2[:, me, 0:11], "am2")
     iota(o("idtab", 1, 961, k="idn"), [[0, N], [1, V]])
-    iota(o("idtab", 1, 961, k="idn", p=(0, 1)), [[1, N], [0, V]])
+    act(cc("o34"), oh(R_C0), bias=oh(R_C1))
+    act(cc("za"), oh(R_ELSE), bias=oh(R_ID))
+    act(cc("z1"), oh(R_LAND + me), bias=oh(R_ID))
+    act(cc("es"), cc("o34"), scale=1.0 / K)
+    act(cc("z2"), cc("o34"), scale=K, bias=cc("z1"))
+    act(cc("p1"), cc("o34"), scale=BL / K)
+    act(cc("z3"), oh(R_C2), scale=float(ZC), bias=cc("z2"))
+    act(cc("p2"), oh(R_C1), scale=CAPP / K, bias=cc("p1"))
+    act(cc("e1"), cc("o34"), scale=-BIG, bias=BIG)
+    act(cc("i1"), oh(R_ELSE), scale=287.0)
+    act(cc("i0"), G16, scale=V / 16.0)
+    act(cc("e2"), oh(R_C2), scale=1.0 - BIG, bias=cc("e1"))
+    act(cc("i2"), oh(R_LAND + me), scale=float(15 + N - 96 * 15), bias=cc("i1"))
+    act(o("ptab", 0, 480, k="pt0"), o("ramp"), scale=cc("es"), bias=cc("p2"))
+    act(cc("i3"), cc("i0"), scale=oh(R_ID), bias=cc("i2"))
+    fill(o("ptab", 480, 736, k="pt1"), 256)
+    low = me < N // 2
+    at = TN * me + 1 if low else 1
+    act(o("ztab", at, at + TN, k="zt0"), o("ramp", 0, TN), scale=oh(R_C2), bias=cc("z3"))
+    zk = ("zt0",)
+    for a_, b_ in ((0, at), (at + TN, at + TN + (1 if low else TN * (N - 1 - me)))):
+        while a_ < b_:
+            n_ = min(b_ - a_, 480)
+            zk += ("zt%d" % (a_ + 1),)
+            fill(o("ztab", a_, a_ + n_, k=zk[-1]), n_, cc("za"))
+            a_ += n_
+    fill(o("S2", 0, 288), 288)
+    act(o("E"), o("zp1", 16, 176), scale=cc("es"), bias=cc("e2"))
 
-    tr(o("RT"), (allR, T.Rt[:]))
-    act(cc(X5), cc(A1), Ident, scale=-1.0, bias=R(R_M))
-    act(cc(X6), cc(A1), Ident, scale=-1.0, bias=R(R_E))
-    act(cc(BASE1), cc(A5), Ident, bias=R(R_B1))
-    ts(o("PM", 0, 16, k="PM"), o("PM", 0, 16, k="PM"), cc(OV), mul)
-    ts(o("tabA"), o("iot", 0, 16, k="iota"), cc(J1), ne, R(R_K1), mul)
-    ts(o("pw0"), o("iot", 0, 16, k="iota"), float(me + 1), eq, R(R_K2), mul)
-    ms(o("PM", 16, 32, k="PM"), 0.0)
-    ts(o("mk1"), o("rr"), cc(X5), mn, cc(X6), eq)
-    tt(o("tabA"), o("tabA"), o("pw0"), add)
-    red(o("x1"), o("mk1"))
-
-    before(o("x1"), "xb", "XA", "XM", "p1", R(R_RM), cc(BASE1), o("q1"))
-    act(o("ctab", 1, 769, k="cta"), o("ctb"), Ident, scale=oh(FN1), bias=R(R_CB))
-    act(o("S1", 0, REM, k="S1"), o("iot", 0, REM, k="iota"), scale=0.0)
-    act(o("tabA"), o("tabA"), Ident, bias=R(R_K3))
-    scan(o("cn1"), o("ones"), o("mk1"), o("q1"))
-    tt(o("z1"), o("mk1"), o("cn1"), mul)
-    ts(o3("zd1", 0, 16, "zd1l"), o("z1"), cc(EV), mul)
-    act(o3("zd1", 16, 32, "zd1h"), o("z1"), scale=cc(OV))
-    tt(o("pay1"), ind(o("ctab", k=("cta", "ctabz", "ctaby")), o("offE")), o("cn1"), add)
-    tr((("zt1",), T.zt1[:]), (("zd1l", "zd1h"), T.zd1[:]))
-    tt(o3("fa1"), o3("zt1", 0, 8), o3("zt1", 16, 24), add)
-    tt(o3("fb1"), o3("fa1", 0, 4), o3("fa1", 4, 8), add)
-    tt(o3("fc1"), o3("fb1", 0, 2), o3("fb1", 2, 4), add)
-    act(o("M1b"), ind(o("tabA"), o("offA")))
-    act(o("E0"), o("pay1"), scale=R(R_RB))
-    tt(o("fd1"), o1("fc1", 0), o1("fc1", 1), add)
-    cp(o("off1"), o("fd1"))
-    scatter(o("S1"), o("off1"), o("pay1"))
-    act(o3("S1d", 16, 32, "S1dh"), o("S1", 0, REM))
-    cp(o3("S1d", 0, 16, "S1dl"), o("S1", 0, REM))
-    tt(o("E"), o("E0"), o("M1b"), mn)
-    tr((("S1t",), T.S1t[:]), (("S1dl", "S1dh"), T.S1d[:]))
-    for k, j in ((0, FN0), (1, FN1)):
-        tt((("X1%d" % k,), T.X1[:, :, k, :]), o1("S1t", j), o1("S1t", j + 16), add)
-    quarters("Y1", "X1", ("X10", "X11"))
-    ts((("Z1a",), T.Z1[0:32, :, 0, :]), (("Y1",), T.Y1[0:32, :, 0, :]), float(-BA), add)
-    ts((("Z1b",), T.Z1[0:32, :, 1, :]), (("Y1",), T.Y1[0:32, :, 1, :]), float(N1 - BX + CAPP), add)
-    k2 = spread("off2", "Z1", ("Z1a", "Z1b"))
-    act(o("ztab", 1, 385, k="zta"), o("iot", 0, TN, k="iota"), Ident, scale=oh(FN2), bias=R(R_ZB))
-    act(o("ztab", 0, 1, k="ztz"), oh(7))
-    act(o("ztab", 385, 386, k="zty"), oh(7))
-    act(o("S2", 0, M, k="S2"), o("iot", 0, M, k="iota"), scale=0.0)
-    pick("sl2", "A", (k2, T.off2[:]), ("Al", "Aw", "Ax"))
+    scatter(o("S1"), o("off1", 0, 10), o("zp1", 16, 176))
+    turn_slots("S1", 8)
+    k2 = gather_lists("off2", R_C0, 2)
+    pick("sl2", "A", (k2, T.off2[:, 0:30]), ("Al", "Ax"))
     columns("sl2", "B", BL, 2 * CAPP, "ac2")
-    move("B", BA, "A", 0, REM, "Al", "Ba", "dAB")
+    move("B", "A", BA, BL, "Al", "Ba", "dAB")
+    iota(o("idtab", 1, 961, k="idn", p=(0, 1)), [[1, N], [0, V]])
+    quant("w", 0, 384, "wt", ("wt",), "w0")
+    quant("w", 384, 768, "wt", ("wt",), "w1")
 
-    total("L2", o("L2b"))
-    ts(o("offN"), o("L2b"), float(-TN * me), add, float(TN + 1), mn)
-    wq(0)
-    tt(o("r2"), ind(o("ztab", 0, 392, k=("zta", "ztz", "zty")), o("offN")), o("E"), add)
-    tt(o("mk2"), o("r2"), o("M1b"), gt)
-    red(o("x2"), o("mk2"))
-    before(o("x2"), "yb", "YA", "YM", "p2", R(R_RM), R(R_B2), o("q2"))
-    wq(1)
-    scan(o("cn2"), o("ones"), o("mk2"), o("q2"))
-    tt(o("z2"), o("mk2"), o("cn2"), mul)
-    wq(2)
-    ts(o3("zd2", 0, 16, "zd2l"), o("z2"), cc(EV), mul)
-    act(o3("zd2", 16, 32, "zd2h"), o("z2"), scale=cc(OV))
-    tt(o("pay2"), o("z2"), o("r2"), add)
-    tr((("zt2",), T.zt2[:]), (("zd2l", "zd2h"), T.zd2[:]))
-    tt(o3("ta2"), o3("zt2", 6, 8), o3("zt2", 22, 24), add)
-    wq(3)
-    tt(o("tb2"), o1("ta2", 0), o1("ta2", 1), add)
-    wq(4)
-    cp(o("off20"), o("tb2"))
-    wq(5)
-    scatter(o("S2"), o("off20"), o("pay2"))
-    act(o3("S2d", 16, 32, "S2dh"), o("S2", 0, M))
-    cp(o3("S2d", 0, 16, "S2dl"), o("S2", 0, M))
-    tr((("S2t",), T.S2t[:]), (("S2dl", "S2dh"), T.S2d[:]))
-    tt(o3("ga"), o3("S2t", 0, 3), o3("S2t", 3, 6), add)
-    tt(o3("gb"), o3("S2t", 16, 19), o3("S2t", 19, 22), add)
-    tt(o2("n01", 0, "n0"), o1("S2t", FN0), o1("S2t", FN0 + 16), add)
-    tt(o3("gc"), o3("ga"), o3("gb"), add)
-    tt(o2("n01", 1, "n1"), o1("S2t", FN1), o1("S2t", FN1 + 16), add)
-    tt(o("gd"), o1("gc", 0), o1("gc", 1), add)
-    tt(o2("X2", 2, "X22"), o1("S2t", FN2), o1("S2t", FN2 + 16), add)
-    tt(o("ge2"), o("gd"), o1("gc", 2), add)
-    tt(o2("X2", 3, "X23"), o1("S2t", FID), o1("S2t", FID + 16), add)
-    tt(o2("X2", 0, "X20"), o2("n01", 0, "n0"), o("ge2"), add)
-    tt(o2("X2", 1, "X21"), o2("n01", 1, "n1"), o("ge2"), add)
-    quarters("Y2", "X2", ("X20", "X21", "X22", "X23"))
-    q0 = (0, 32)
-    ts(o2("Y2", 0, "Y2n", p=q0), o2("Y2", 0, p=q0), -float(N), add)
-    ts(o2("Y2", 1, "Y2m", p=q0), o2("Y2", 1, p=q0), float(CAPP - N), add)
-    kF = spread("offF", "Y2", ("Y2", "Y2n", "Y2m"))
+    L2k = ("L2i", "L2o") + pre[0]
+    tt((("L2h",), T.L2h[:]), (L2k, T.L2[:, 0:3, 0:11]), (L2k, T.L2[:, 3:6, 0:11]), add)
+    tt(o("L2a"), (("L2h",), T.L2h[:, 0, :]), (("L2h",), T.L2h[:, 1, :]), add)
+    tt(o("vi", 0, 11), o("L2a"), (("L2h",), T.L2h[:, 2, :]), add)
+    if low:
+        ts(o("offN"), o("vi", 1, 11), 1.0 / K, mul, float(at + TN), mn)
+    else:
+        ts(o("offN"), o("vi", 1, 11), 1.0 / K, mul, float(-TN * me), add)
+    ts(o("sli"), o("vi", 1, 11), int(K) - 1, band)
+    act(o("G2"), ind(o("ztab", k=zk), o("offN")))
+    ts(o("in2"), o("vi", 0, 1), oh(R_LAND + me), mul, cc("i3"), add)
+    cp(o("offS"), o("sli"))
+    tt(o("cap2"), ind(o("ptab", k=("pt0", "pt1")), o("offS")), o("E"), mx)
+    scan(o("cn2"), o("G2"), o("cap2"), o("in2"), add, mn)
+    tt(o("zp2", 16, 176), o("G2"), o("cn2"), mul)
+    turn("zp2")
+    cp(o("pa"), ind(Tz, o("selB", R_ELSE, R_ELSE + 1)))
+    tt(o("pb"), ind(Tz, o("selP", 0, 1)), o("pa"), add)
+    cp(o("off20"), o("pb", 0, 10))
+    scatter(o("S2"), o("off20"), o("zp2", 16, 176))
+    turn_slots("S2", 9)
+    kF = gather_lists("offF", R_ID, 4)
     off = [(kF, T.offF[:, 16 * k:16 * k + 16]) for k in range(4)]
 
     def product(k, last):
         n = "p%d" % k
         for oo in range(NO):
             a = 128 * (k * NO + oo)
+            wk = "w%d" % (a // 384)
             op("k", lambda: g.tensor.matmul_mx(T["ps_%d" % oo][:, 0:M], T.wq[:, a:a + 128], T.ws[:, a:a + 128], T[n + "q"][:], T[n + "s"][:], k == 2, last),
-               ("w%dq" % (k * NO + oo), "w%ds" % (k * NO + oo), n + "q", n + "s"), ("ps_%d" % oo,) if last else ())
-    pick("p2", "B", off[2], ("Bx",), ZC + TN)
+               (wk + "q", wk + "s", n + "q", n + "s"), ("ps_%d" % oo,) if last else ())
+    pick("p2", "B", off[1], ("Bx",), BA)
     product(2, False)
-    Bk = ("Bx", "Ba", "Bw", "Bl")
-    pick("p0", "B", off[0], Bk)
+    Bk = ("Bx", "Ba", "Bl")
+    pick("p0", "B", off[2], Bk)
     product(0, False)
-    pick("p1", "B", off[1], Bk)
+    pick("p1", "B", off[3], Bk)
     product(1, True)
-    act(o("idt"), ind(o("idtab", k=("idz", "idn")), off[3]))
+    act(o("idt"), ind(o("idtab", k=("idz", "idn")), off[0]))
     cp(o("yo0"), o("ps_0", 0, M))
     act(o("yo1"), o("ps_1", 0, M))
     dma("y", (("y0",), T.y[:, 0:M]), o("yo0"), "dy0")

@@ -8,7 +8,8 @@ BA = ZC + TN
 BL = BA + REM
 BW = BL + 2 * REM
 K = 2048.0
-BIG = 4096.0
+LIFT = 4096.0
+BIG = 8192.0
 R_N2, R_LAND, R_SLOT, R_OUT, R_C0, R_C1 = 0, 1, 7, 12, 14, 15
 R_ELSE, R_ID, R_C2 = 0, 12, 13
 NB = 11
@@ -34,13 +35,13 @@ _add(_I, st0=10, bt0=10, b1t=16, nxr=768, nxA=48, r1i=16, vi=12, sli=10)
 _add(_F, cc=48, oh=16, ramp=480, Kt=192, KT=192, K2=(2, 16), KU=32, tq1=(5, 2, 3), Fm=8, Fb=8, Ft=8, F=2304, TAB=776, capT=776,
      ztab=1160, ptab=736, rs=32 * NB, mD=64, D=64, DT=72, idtab=968, idt=M, yo0=M, yo1=M)
 _add(_F, zp0=192, zp1=192, zp2=192, Tz=32 * NB, SS=32 * NB, Ts=544, S0=416, S1=416, S2=448,
-     G0=V, G1=V, G2=V, cn0=V, cn1=V, cn2=V, strow=V, Mt=V, cap1=V, E=V, cap2=V,
+     G0=V, G1=V, G2=V, cn0=V, cn1=V, cn2=V, strow=V, Mt=V, cap1=V, E=V, cap2=V, zl=V,
      L1o=16, L1=88, L2=(6, 20), L2h=(3, 11), Ha=64, Hb=64, tq=64, yq=64)
 _add(_U, selA=32, selB=16, selP=2, selL=2, offr=10, off0=16, offi=16, nxo=48, offE=16, off1=16, off2=32,
-     offN=10, offS=10, off20=10, offF=64)
+     offN=10, offS=10, off20=16, offF=64)
 _pool("poolu", _U, offe=10, offSt=10)
 _pool("pooli", _I, ia=10, ib=10)
-_pool("poolf", _F, e1=10, e2=10, e3=10, e4=10, e5=10, x1=1, tot=1, L2a=11, in2=1, pa=16, pb=16)
+_pool("poolf", _F, e1=10, e2=10, e3=10, e4=10, e5=10, x1=1, tot=1, L2a=11, in2=1, jl=16, pb=16)
 _add("bfloat16", xt=4 * BA, wt=3072)
 for _n, _w in (("x", BA), ("w", 768), ("sl1", REM), ("A", BL), ("sl2", 2 * REM), ("B", BW), ("p0", M), ("p1", M), ("p2", M)):
     SCRATCH[_n + "q"] = ("sbuf", [128, _w], _C)
@@ -68,7 +69,11 @@ def rank_program(g, core, T, topo):
 
     eng = {"v": g.vector, "s": g.scalar, "p": g, "k": g.tensor, "y": g.sync}
     know = {q: {} for q in eng}
-    count, wr, rd = {"loc": 0}, {}, {}
+    count, wr, rd, jobs = {"loc": 0}, {}, {}, []
+    across = set()
+
+    def side(f, out, *args):
+        jobs.append((out[0], lambda: f(out, *args)))
 
     def need(q, evs):
         for sem, val, snap in sorted(evs, key=lambda e: -len(e[2])):
@@ -79,11 +84,15 @@ def rank_program(g, core, T, topo):
                         know[q][a] = b
 
     def op(q, call, reads=(), writes=(), sem="", inc=1, total=None):
+        while any(k in job[0] for job in jobs for k in tuple(reads) + tuple(writes)):
+            jobs.pop(0)[1]()
         evs = []
         for k in reads:
             evs += wr.get(k, [])
         for k in writes:
             evs += wr.get(k, []) + rd.get(k, [])
+        if q == "v" and jobs and count["qv"] not in across and any(e[0] == "qv" and e[1] == count["qv"] for e in evs):
+            jobs.pop(0)[1]()
         best = {}
         for e in evs:
             if e[0] not in best or best[e[0]][1] < e[1]:
@@ -129,7 +138,7 @@ def rank_program(g, core, T, topo):
         op("v", lambda: g.vector.tensor_copy(out[1], in_[1]), in_[0], out[0])
 
     def ms(out, c):
-        op("v", lambda: g.vector.memset(out[1], c), (), out[0])
+        op("v", lambda: g.vector.memset(out[1], c), ("rs",) if out[0][0] in ("rs0", "rs1") else (), out[0])
 
     def tt(out, a, b, f):
         op("v", lambda: g.vector.tensor_tensor(out[1], a[1], b[1], f), a[0] + b[0], out[0])
@@ -180,12 +189,13 @@ def rank_program(g, core, T, topo):
            tuple(x + "s" for x in wkeys) + off[0], (outn + "s",))
 
     def quant(outn, lo, hi, src, skeys, key):
-        op("v", lambda: g.vector.quantize_mx(T[outn + "q"][:, lo:hi], T[outn + "s"][:, lo:hi], T[src][:, 4 * lo:4 * hi]), skeys, (key + "q", key + "s"))
+        ks = (key + "q", key + "s")
+        jobs.append((ks, lambda: op("v", lambda: g.vector.quantize_mx(T[outn + "q"][:, lo:hi], T[outn + "s"][:, lo:hi], T[src][:, 4 * lo:4 * hi]), skeys, ks)))
 
-    def move(outn, srcn, lo, hi, rkey, key, sem):
+    def move(outn, srcn, lo, hi, rkeys, key, sem):
         op("y", lambda: g.sync.dma_start(T[outn + "q"][:, lo:hi].bitcast(dt.uint8), T[srcn + "q"][:, lo:hi].bitcast(dt.uint8)),
-           (rkey + "q",), (key + "q",), sem=sem, inc=16, total=32)
-        op("y", lambda: g.sync.dma_start(T[outn + "s"][:, lo:hi], T[srcn + "s"][:, lo:hi]), (rkey + "s",), (key + "s",), sem=sem, inc=16, total=32)
+           tuple(k + "q" for k in rkeys), (key + "q",), sem=sem, inc=16, total=32)
+        op("y", lambda: g.sync.dma_start(T[outn + "s"][:, lo:hi], T[srcn + "s"][:, lo:hi]), tuple(k + "s" for k in rkeys), (key + "s",), sem=sem, inc=16, total=32)
 
     def fan(reads, src, dst, rsem):
         def call():
@@ -226,13 +236,13 @@ def rank_program(g, core, T, topo):
         tr(o("Tz", 0, 192, k="Tze"), o(zp, 0, 192, k=(zp, zp + "p", zp + "r")))
         tr(o("Tz", 192, 352, k="Tzo"), o(zp, 16, 176))
 
-    def turn_slots(win, even):
-        tr(o("Ts", 256, 256 + 32 * even, k="Tse"), o(win, 0, 32 * even))
-        tr(o("Ts", 0, 256, k="Tso"), o(win, 16, 272))
+    def turn_slots(win, even, at=0):
+        tr(o("Ts", 256, 256 + 32 * even, k="Tse"), o(win, at, at + 32 * even))
+        tr(o("Ts", 0, 256, k="Tso"), o(win, at + 16, at + 272))
 
     def pads(zp):
-        ms(o(zp, 0, 16, k=zp + "p"), 0.0)
-        ms(o(zp, 176, 192, k=zp + "r"), 0.0)
+        side(ms, o(zp, 0, 16, k=zp + "p"), 0.0)
+        side(ms, o(zp, 176, 192, k=zp + "r"), 0.0)
 
     def sums():
         scan(o("SS"), o("rs", k=("rs", "rs0", "rs1")), Tz, 0.0, mul, add)
@@ -249,11 +259,10 @@ def rank_program(g, core, T, topo):
         else:
             tt(o("tq", 0, n, p=(0, 64)), o("Hb", 0, n, p=(0, 64)), o("Hb", 0, n, p=(64, 128)), add)
             tq = [o("tq", 0, n, p=(32 * h, 32 * h + 32)) for h in range(2)]
-        for h in range(2):
-            tt(o("yq", 0, n, k="yq%d" % h, p=(32 * h, 32 * h + 32)), tq[0], tq[1], add)
-        for h in range(2):
-            cp(o(off, 0, n, k=off + "%d" % h, p=(64 * h, 64 * h + 64)), o("yq", 0, n, k=("yq0", "yq1"), p=(0, 64)))
-        return (off + "0", off + "1")
+        across.update((count["qv"], count["qv"] + 4))
+        for h in range(4):
+            tt(o(off, 0, n, k=off + "%d" % h, p=(32 * h, 32 * h + 32)), tq[0], tq[1], add)
+        return tuple(off + "%d" % h for h in range(4))
 
     Q = 32 * (me // 2)
     PQ = (Q, Q + 32)
@@ -280,41 +289,41 @@ def rank_program(g, core, T, topo):
         return o("Kt", first, at, k=ks)
     Ka = rows(0, ([[0, 2], [1, 16]], 0, 0), ([[16, 2], [0, 16]], 0, 1), ([[32, 8], [-160, 2]], 192, 0), ([[32, 8], [192, 2]], 16, 0))
     iota(o("ramp"), [[1, 480]])
-    Kb = rows(96, ([[32, 8], [288, 2]], 0, 0), ([[32, 8], [-256, 2]], 256, 0), ([[80, 2], [8, 16]], 0, 5), ([[16, 2], [1, 16]], 16, 0))
     iota(o("rs"), [[0, 32 * NB]], 1)
     J, G16, B0b = (o("KT", 32 * b, 32 * b + 1, k="KTa") for b in range(3))
     B0, SL, P16 = (o("KT", 32 * b, 32 * b + 1, k="KTb") for b in range(3, 6))
     r16 = o("Kt", 0, 16, k="Kt0")
     ms(o("poolu", k=("offe", "offSt")), 0)
     ms(o("b1t"), 0)
+    ms(o("zp0", 0, 16, k="zp0p"), 0.0)
     tr(o("KT", 0, 96, k="KTa"), Ka)
-    pads("zp0")
-    ts(cc("GM"), G16, 16.0 * me, eq)
-    ts(o("oh"), r16, J, eq)
+    ms(o("zp0", 176, 192, k="zp0r"), 0.0)
     ms(o("xt", 0, 4 * ZC, k="xtz"), 0.0)
-    ms(o("L1", 60, 88, k="L1z"), 0.0)
-    ts(o("selB"), r16, B0b, add, 32.0 * NB - 1, mn)
+    ts(o("oh"), r16, J, eq)
+    ts(cc("GM"), G16, 16.0 * me, eq)
     if me < N - 1:
-        tt(o("Fm", me + 1, N, k="Fm1"), o("oh", R_LAND + me + 1, R_LAND + N), o("oh", R_SLOT, R_OUT - me), add)
-    tt(o("Fm", 0, me + 1, k="Fm0"), o("oh", R_LAND, R_LAND + me + 1), o("oh", R_OUT - me, R_OUT + 1), add)
+        side(tt, o("Fm", me + 1, N, k="Fm1"), o("oh", R_LAND + me + 1, R_LAND + N), o("oh", R_SLOT, R_OUT - me), add)
+    side(tt, o("Fm", 0, me + 1, k="Fm0"), o("oh", R_LAND, R_LAND + me + 1), o("oh", R_OUT - me, R_OUT + 1), add)
+    side(ts, o("selB"), r16, B0b, add, 32.0 * NB - 1, mn)
+    side(ts, cc("pr0"), J, float(R_LAND), ge)
+    side(ts, cc("wrap"), G16, 16.0 * me, le, float(CAPP * N), mul)
+    side(ts, cc("pr"), J, float(R_OUT - 1), le, cc("pr0"), mul)
     Fm = o("Fm", 0, N, k=("Fm0", "Fm1"))
     selZ = o("selB", 0, 1)
-    pads("zp1")
-    pads("zp2")
     act(cc("FS"), oh(R_N2), scale=K)
-    act(cc("own"), cc("GM"), scale=oh(R_C0))
+    act(cc("b1"), cc("GM"), scale=K - 1, bias=1.0)
     act(cc("b0"), oh(R_C1), scale=K, bias=cc("FS"))
     act(cc("FA"), oh(R_N2), scale=K * TN)
-    act(cc("b1"), oh(R_C0), bias=cc("b0"))
+    act(cc("b2"), cc("b1"), scale=oh(R_C0), bias=cc("b0"))
     act(cc("base0"), J, scale=float(CAPP), bias=float(15 - CAPP * R_SLOT))
-    act(cc("b2"), cc("own"), scale=K - 1, bias=cc("b1"))
-    act(cc("k1"), oh(R_N2), scale=1.0 - BIG, bias=BIG)
     act(o("Ft", 0, N), o("Kt", 0, N, k="Kt0"), scale=cc("FA"), bias=cc("b2"))
+    act(cc("own"), cc("GM"), scale=oh(R_C0))
+    act(cc("k1"), oh(R_N2), scale=1.0 - BIG, bias=BIG)
     act(cc("cs"), oh(R_C1), scale=1.0 / K)
     act(cc("k2"), cc("own"), scale=1.0 - BIG, bias=cc("k1"))
     act(cc("ms"), cc("own"), scale=1.0 / K)
-    act(cc("k3"), oh(R_C1), scale=ZC / K - BIG, bias=cc("k2"))
     act(cc("mb"), cc("own"), scale=-1.0, bias=1.0)
+    act(cc("k3"), oh(R_C1), scale=ZC / K - BIG, bias=cc("k2"))
 
     ts(o("ia", p=PQ), st, 3, shr)
     ts(o("e1", p=PQ), st, 96.0, mul)
@@ -323,86 +332,98 @@ def rank_program(g, core, T, topo):
     ts(o("e3", p=PQ), o("ib", p=PQ), 48.0, mul)
     tt(o("e4", p=PQ), o("e1", p=PQ), o("e2", p=PQ), add)
     ts(o("b1t", 0, 10, p=PQ), bt, 1, shr)
-    tt(o("e5", p=PQ), o("e4", p=PQ), o("e3", p=PQ), add)
-    tt(o("Fb", 0, N), Fm, o("Ft", 0, N), add)
-    cp(o("offe", p=PQ), o("e5", p=PQ))
-    ts(o("offSt", p=PQ), st, float(ZC), add)
+    tt(o("offe", p=PQ), o("e4", p=PQ), o("e3", p=PQ), add)
     ts(o("zp0", 16, 176), ind(o("nxr"), o("offe")), 2.0, mul, 1.0, add)
-    ts(cc("pr0"), J, float(R_LAND), ge)
+    tt(o("Fb", 0, N), Fm, o("Ft", 0, N), add)
+    side(ts, o("offSt", p=PQ), st, float(ZC), add)
     turn("zp0")
-    ts(cc("pr"), J, float(R_OUT - 1), le, cc("pr0"), mul)
     tt(o("L1o"), ind(Tz, selZ), o("b1t"), add)
     fan(("L1o",), lambda q: T.L1o[:, 0:10], lambda q: T.L1[:, 10 * me:10 * me + 10], "am1")
     dma("y", o("L1", 10 * me, 10 * me + 10, k="L1m"), o("L1o", 0, 10), "dL1")
 
-    iota((("K2b",), T.K2[:]), [[0, 32]])
-    for a_, n_, s_, v_ in ((R_LAND, me, -96, 96 * (me - 1) - 1), (R_LAND + me, N - me, -96, 96 * (N - 1) - 1), (R_SLOT, N, CAPP, 15)):
-        if n_:
-            iota((("K2b",), T.K2[:, :, a_:a_ + n_]), [[0, 2], [s_, n_]], v_)
+    Kb = rows(96, ([[32, 8], [288, 2]], 0, 0), ([[32, 8], [-256, 2]], 256, 0), ([[80, 2], [8, 16]], 0, 5), ([[16, 2], [1, 16]], 16, 0))
+    K2 = ()
+    for a_, b_, s_, v_ in ((0, R_LAND + me, -96, 96 * me - 1), (R_LAND + me, R_SLOT, -96, 96 * (N - 1) - 1), (R_SLOT, 16, CAPP, 15)):
+        K2 += ("K2%d" % a_,)
+        iota((K2[-1:], T.K2[:, :, a_:b_]), [[0, 2], [s_, b_ - a_]], v_)
     iota(o("S1", 0, 272), [[0, 272]])
     iota(o("idtab", 0, 1, k="idz"), [[0, 1]], -1)
 
-    for k in range(N):
+    def Fk(k):
         act(o("F", TN * k, TN * k + TN, k="F%d" % k), o("ramp", 0, TN), scale=cc("FS"), bias=o("Fb", k, k + 1))
-    ts(o("r1i"), ind(Tz, selZ), -float(TN), add, 0.5 / TN, mul)
-    tr(o("KT", 96, 192, k="KTb"), Kb)
-    cp(o("offr"), o("r1i", 0, 10))
-    ms(o("rs", 0, None, 16, k=("rs", "rs0")), 0.0)
-    cp(o("G0"), ind(Fm, o("offr")))
-    cp(o("nxo"), nxA)
+    for k in range(4):
+        Fk(k)
     act(o("strow"), ind(o("ramp"), o("offSt")))
     fill(o("S0", 0, 288), 288)
-    act(o("TAB", 1, 769, k="TABa"), ind(o("F", k=tuple("F%d" % k for k in range(N))), o("nxo")))
+    Fk(4)
+    Fk(5)
+    ts(o("r1i"), ind(Tz, selZ), -float(TN), add, 0.5 / TN, mul)
+    side(ms, o("rs", 0, None, 16, k=("rs0",)), 0.0)
+    side(cp, o("nxo"), nxA)
+    side(ms, o("rs", R_SLOT, None, 16, k=("rs1",)), 0.0)
+    xk = ("x0", "x1", "x2")
+    for k, (a_, b_) in enumerate(((0, 136), (136, 268), (268, BA))):
+        quant("x", a_, b_, "xt", ("xtx", "xtz"), xk[k])
+    cp(o("offr"), o("r1i", 0, 10))
+    cp(o("G0"), ind(Fm, o("offr")))
     scan(o("cn0"), o("G0"), o("G0"), cc("base0"), add, mx)
-    ms(o("rs", R_SLOT, None, 16, k=("rs", "rs1")), 0.0)
+    act(o("TAB", 1, 769, k="TABa"), ind(o("F", k=tuple("F%d" % k for k in range(N))), o("nxo")))
     tt(o("zp0", 16, 176), o("G0"), o("cn0"), mul)
-    quant("x", 0, BA, "xt", ("xtx", "xtz"), "x")
-    move("A", "x", 0, BA, "x", "Ax", "dxA")
-    move("B", "x", 0, BA, "x", "Bx", "dxB")
     turn("zp0")
-    ts(o("selL", 0, 1), SL, 0.125, mul)
     sums()
-    ts(o("selA"), o("ramp", 0, 32), B0, add)
     cp(o("off0"), ind(o("SS"), o("selB", R_OUT, R_OUT + 1)))
-    ts(o("mD", 0, 32, k="mD0"), o("Kt", 0, 32, k="Kt0"), J, eq, cc("pr"), mul)
+    move("A", "x", 0, BA, xk, "Ax", "dxA")
+    move("B", "x", 0, BA, xk, "Bx", "dxB")
+    side(tr, o("KT", 96, 192, k="KTb"), Kb)
+    side(ts, o("selA"), o("ramp", 0, 32), B0, add)
+    side(ms, o("L1", 60, 88, k="L1z"), 0.0)
+    side(tr, o("KU"), (K2, T.K2[:]))
+    side(ts, o("selL", 0, 1), SL, 0.125, mul)
+    side(ts, o("mD", 0, 32, k="mD0"), o("Kt", 0, 32, k="Kt0"), J, eq, cc("pr"), mul)
+    side(ts, o("mD", 32, 64, k="mD1"), o("ramp", 0, 32), P16, eq, cc("pr"), mul)
+    pads("zp1")
     scatter(o("S0"), o("off0", 0, 10), o("strow"))
-    ts(o("mD", 32, 64, k="mD1"), o("ramp", 0, 32), P16, eq, cc("pr"), mul)
     turn_slots("S0", 9)
-    ts(o("selP", 0, 1), B0b, float(R_LAND + me), add, 32.0 * NB - 1, mn)
     cp(o("offi", k="offi"), ind(Ts, o("selA", 16 * (me % 2), 16 * (me % 2) + 1)))
     ki = ("offi",)
     for q in range(4):
         if 32 * q != Q:
             ki += ("offi%d" % q,)
             op("v", lambda: g.vector.tensor_copy(T.offi[32 * q:32 * q + 32, 0:16], T.offi[Q:Q + 32, 0:16]), ("offi",), ki[-1:])
-    for c in (0, 769):
-        act(o("TAB", c, c + 1, k="TAB%d" % c), oh(R_OUT))
+    act(cc("c1"), G16, scale=CAPP / 16.0, bias=cc("wrap"))
+    act(o("TAB", 0, 770, 769, k="TABz"), o("ramp", 0, 2), scale=0.0, bias=oh(R_OUT))
+    act(cc("c2"), cc("c1"), bias=float(BA - 1 - CAPP * (me + 1) - 15 - CAPP * (R_C0 - R_SLOT)))
     for b in range(2):
         act(o("capT", 1 + b, 769, 2, k="capT%d" % b), o("ramp", 0, TN), scale=cc("cs"), bias=cc("k3"))
     act(o("capT", 0, 770, 769, k="capT2"), o("ramp", 0, 2), scale=0.0, bias=cc("k3"))
+    act(cc("prn"), cc("pr"), scale=-LIFT)
+    act(cc("KUc"), cc("c2"), scale=oh(R_C0), bias=o("KU", 0, 1))
+    act(o("DT", 64, 65, k="DTb"), o("KU", 0, 1), scale=cc("pr"), bias=cc("prn"))
     act(o("Mt"), o("strow"), scale=cc("ms"), bias=cc("mb"))
-    ts(cc("wrap"), G16, 16.0 * me, le, float(CAPP * N), mul)
-    pick("sl1", "x", (ki, T.offi[:, 0:15]), ("x",))
+    act(cc("in1"), o("DT", 64, 65, k="DTb"), scale=-1.0, bias=cc("KUc"))
+    pick("sl1", "x", (ki, T.offi[:, 0:15]), xk)
     columns("sl1", "A", BA, CAPP, "ac1")
-    tr(o("KU"), (("K2b",), T.K2[:]))
-    act(cc("c1"), G16, scale=CAPP / 16.0, bias=cc("wrap"))
-    act(cc("c2"), cc("c1"), bias=float(BA - 1 - CAPP * (me + 1)))
-    act(o("DT", 64, 65, k="DTb"), cc("c2"), scale=oh(R_C0), bias=o("KU", 0, 1))
+    side(ts, o("selP", 0, 1), B0b, float(R_LAND + me), add, 32.0 * NB - 1, mn)
+    side(ts, o("jl"), r16, 16.0, mul, J, add)
+    pads("zp2")
+    for k in range(2 * 3):
+        quant("w", 128 * k, 128 * k + 128, "wt", ("wt",), "w%d" % k)
 
     ts(o("offE"), ind(o("L1", k=("L1i", "L1m", "L1z")), o("selL", 0, 1)), float(-2 * TN * me), add, float(2 * TN + 1), mn)
     offE = o("offE", 0, 10)
-    act(o("G1"), ind(o("TAB", k=("TABa", "TAB0", "TAB769")), offE), acc=o("x1"))
+    act(o("G1"), ind(o("TAB", k=("TABa", "TABz")), offE), acc=o("x1"))
     tt(o("cap1"), ind(o("capT", k=("capT0", "capT1", "capT2")), offE), o("Mt"), mul)
     ts(o("D"), o("mD", k=("mD0", "mD1")), o("x1"), mul)
+    scan(o("cn1"), o("G1"), o("cap1"), cc("in1"), add, mn)
     tr(o("DT", 0, 64), o("D"))
+    tt(o("zl"), o("G1"), o("cn1"), mul)
     red(o("tot"), o("DT", 0, 32))
     pre = (("pre",), T.L2[:, me, 0:1])
     red(pre, o("DT", 32, 65, k=("DT", "DTb")))
     ts((("pre1",), T.L2[32:64, me, 0:1]), (("pre",), T.L2[32:64, me, 0:1]), o("tot", p=(0, 32)), add)
     ts((("pre2",), T.L2[64:96, me, 0:1]), (("pre",), T.L2[64:96, me, 0:1]), o("tot", p=(0, 32)), add, o("tot", p=(32, 64)), add)
     pre = (("pre", "pre1", "pre2"), pre[1])
-    scan(o("cn1"), o("G1"), o("cap1"), pre, add, mn)
-    tt(o("zp1", 16, 176), o("G1"), o("cn1"), mul)
+    ts(o("zp1", 16, 176), o("zl"), pre, add, 0.0, mx)
     turn("zp1")
     sums()
     cp((("L2o",), T.L2[:, me, 1:17]), ind(o("SS"), o("selB", R_SLOT - 1, R_SLOT)))
@@ -410,7 +431,6 @@ def rank_program(g, core, T, topo):
     fan(("L2o",) + pre[0], lambda q: T.L2[:, me, 0:11], lambda q: T.L2[:, me, 0:11], "am2")
     iota(o("idtab", 1, 961, k="idn"), [[0, N], [1, V]])
     act(cc("o34"), oh(R_C0), bias=oh(R_C1))
-    act(cc("za"), oh(R_ELSE), bias=oh(R_ID))
     act(cc("z1"), oh(R_LAND + me), bias=oh(R_ID))
     act(cc("es"), cc("o34"), scale=1.0 / K)
     act(cc("z2"), cc("o34"), scale=K, bias=cc("z1"))
@@ -418,10 +438,9 @@ def rank_program(g, core, T, topo):
     act(cc("z3"), oh(R_C2), scale=float(ZC), bias=cc("z2"))
     act(cc("p2"), oh(R_C1), scale=CAPP / K, bias=cc("p1"))
     act(cc("e1"), cc("o34"), scale=-BIG, bias=BIG)
-    act(cc("i1"), oh(R_ELSE), scale=287.0)
     act(cc("i0"), G16, scale=V / 16.0)
     act(cc("e2"), oh(R_C2), scale=1.0 - BIG, bias=cc("e1"))
-    act(cc("i2"), oh(R_LAND + me), scale=float(15 + N - 96 * 15), bias=cc("i1"))
+    act(cc("i2"), oh(R_LAND + me), scale=V + 15 + N * (1 + LIFT) - 96 * 15)
     act(o("ptab", 0, 480, k="pt0"), o("ramp"), scale=cc("es"), bias=cc("p2"))
     act(cc("i3"), cc("i0"), scale=oh(R_ID), bias=cc("i2"))
     fill(o("ptab", 480, 736, k="pt1"), 256)
@@ -433,9 +452,9 @@ def rank_program(g, core, T, topo):
         while a_ < b_:
             n_ = min(b_ - a_, 480)
             zk += ("zt%d" % (a_ + 1),)
-            fill(o("ztab", a_, a_ + n_, k=zk[-1]), n_, cc("za"))
+            fill(o("ztab", a_, a_ + n_, k=zk[-1]), n_, oh(R_ID))
             a_ += n_
-    fill(o("S2", 0, 288), 288)
+    fill(o("S2", V, V + 288), 288)
     act(o("E"), o("zp1", 16, 176), scale=cc("es"), bias=cc("e2"))
 
     scatter(o("S1"), o("off1", 0, 10), o("zp1", 16, 176))
@@ -443,10 +462,8 @@ def rank_program(g, core, T, topo):
     k2 = gather_lists("off2", R_C0, 2)
     pick("sl2", "A", (k2, T.off2[:, 0:30]), ("Al", "Ax"))
     columns("sl2", "B", BL, 2 * CAPP, "ac2")
-    move("B", "A", BA, BL, "Al", "Ba", "dAB")
+    move("B", "A", BA, BL, ("Al",), "Ba", "dAB")
     iota(o("idtab", 1, 961, k="idn", p=(0, 1)), [[1, N], [0, V]])
-    quant("w", 0, 384, "wt", ("wt",), "w0")
-    quant("w", 384, 768, "wt", ("wt",), "w1")
 
     L2k = ("L2i", "L2o") + pre[0]
     tt((("L2h",), T.L2h[:]), (L2k, T.L2[:, 0:3, 0:11]), (L2k, T.L2[:, 3:6, 0:11]), add)
@@ -464,11 +481,9 @@ def rank_program(g, core, T, topo):
     scan(o("cn2"), o("G2"), o("cap2"), o("in2"), add, mn)
     tt(o("zp2", 16, 176), o("G2"), o("cn2"), mul)
     turn("zp2")
-    cp(o("pa"), ind(Tz, o("selB", R_ELSE, R_ELSE + 1)))
-    tt(o("pb"), ind(Tz, o("selP", 0, 1)), o("pa"), add)
-    cp(o("off20"), o("pb", 0, 10))
-    scatter(o("S2"), o("off20"), o("zp2", 16, 176))
-    turn_slots("S2", 9)
+    tt(o("off20"), ind(Tz, o("selP", 0, 1)), o("jl"), mx)
+    scatter(o("S2"), o("off20", 0, 10), o("zp2", 16, 176))
+    turn_slots("S2", 9, V)
     kF = gather_lists("offF", R_ID, 4)
     off = [(kF, T.offF[:, 16 * k:16 * k + 16]) for k in range(4)]
 
@@ -476,7 +491,7 @@ def rank_program(g, core, T, topo):
         n = "p%d" % k
         for oo in range(NO):
             a = 128 * (k * NO + oo)
-            wk = "w%d" % (a // 384)
+            wk = "w%d" % (k * NO + oo)
             op("k", lambda: g.tensor.matmul_mx(T["ps_%d" % oo][:, 0:M], T.wq[:, a:a + 128], T.ws[:, a:a + 128], T[n + "q"][:], T[n + "s"][:], k == 2, last),
                (wk + "q", wk + "s", n + "q", n + "s"), ("ps_%d" % oo,) if last else ())
     pick("p2", "B", off[1], ("Bx",), BA)

@@ -32,12 +32,12 @@ def _pool(buf, dtype, **widths):
 
 
 _add(_I, st0=10, bt0=10, b1t=16, nxr=768, nxA=48, r1i=16, vi=12, sli=10)
-_add(_F, cc=48, oh=16, ramp=480, Kt=192, KT=192, K2=(2, 16), KU=32, tq1=(5, 2, 3), Fm=8, Fb=8, Ft=8, F=2304, TAB=776, capT=776,
+_add(_F, cc=48, oh=16, ramp=480, Kt=192, KT=192, K2=(2, 16), KU=32, tq1=(5, 2, 3), Fm=8, Fb=8, Fc=8, Ft=16, F=2304, TAB=776, capT=776,
      ztab=1160, ptab=736, rs=32 * NB, mD=64, D=64, DT=72, idtab=968, idt=M, yo0=M, yo1=M)
 _add(_F, zp0=192, zp1=192, zp2=192, Tz=32 * NB, SS=32 * NB, Ts=544, S0=416, S1=416, S2=448,
      G0=V, G1=V, G2=V, cn0=V, cn1=V, cn2=V, strow=V, Mt=V, cap1=V, E=V, cap2=V, zl=V,
      L1o=16, L1=88, L2=(6, 20), L2h=(3, 11), Ha=64, Hb=64, tq=64, yq=64)
-_add(_U, selA=32, selB=16, selP=2, selL=2, offr=10, off0=16, offi=16, nxo=48, offE=16, off1=16, off2=32,
+_add(_U, selA=32, selB=16, selP=2, selL=2, offr=16, off0=16, offi=16, nxo=48, offE=16, off1=16, off2=32,
      offN=10, offS=10, off20=16, offF=64)
 _pool("poolu", _U, offe=10, offSt=10)
 _pool("pooli", _I, ia=10, ib=10)
@@ -46,11 +46,12 @@ _add("bfloat16", xt=4 * BA, wt=3072)
 for _n, _w in (("x", BA), ("w", 768), ("sl1", REM), ("A", BL), ("sl2", 2 * REM), ("B", BW), ("p0", M), ("p1", M), ("p2", M)):
     SCRATCH[_n + "q"] = ("sbuf", [128, _w], _C)
     SCRATCH[_n + "s"] = ("sbuf", [128, _w], _S)
+_add(_S, hsl1=REM, hsl2=2 * REM)
 SCRATCH["ps_0"] = ("psum", [128, 512], _F)
 SCRATCH["ps_1"] = ("psum", [128, 512], _F)
 
-SEMAPHORES = ["qv", "qs", "qp", "qk", "dst0", "dbt0", "dnx", "dnxA", "dx", "dw", "dxA", "dxB", "dAB", "dL1",
-              "did", "dy0", "dy1", "am1", "ac1", "am2", "ac2", "loc"]
+SEMAPHORES = ["qv", "qs", "qp", "qk", "dst0", "dbt0", "dnx", "dnxA", "dx", "dw", "left", "dAB", "dL1",
+              "did", "dy0", "dy1", "am1", "Aq", "As", "am2", "Bq", "Bs", "hsl1", "hsl2", "loc"]
 
 add, sub, mul, mx, mn = AluOpType.add, AluOpType.subtract, AluOpType.mult, AluOpType.max, AluOpType.min
 eq, ge, gt, le = AluOpType.is_equal, AluOpType.is_ge, AluOpType.is_gt, AluOpType.is_le
@@ -58,22 +59,67 @@ shr, band = AluOpType.arith_shift_right, AluOpType.bitwise_and
 Copy, Ident = ActivationFunctionType.Copy, ActivationFunctionType.Identity
 
 
+STAGES = (("sl1", "A", BA, CAPP), ("sl2", "B", BL, 2 * CAPP))
+
+
+HANDED = [0]
+
+
+def pos(a, q):
+    return (q - a - 1) % N
+
+
+def pieces(T, me, name, land, at, w):
+    return (lambda q: T[name][:, w * pos(me, q):w * pos(me, q) + w]), (lambda q: T[land][:, at + w * pos(q, me):at + w * pos(q, me) + w])
+
+
+def neighbour(T, topo, r):
+    c = T.cores[r]
+    able = [h for h in topo.cores_of(c) if h != c and all(topo.may_write(h, d) for d in T.cores if d != c)]
+    return min(able, key=lambda h: topo.die(h) != topo.die(c))
+
+
+def send_five(g, core, me, T, topo, src, dst, rsem, lsem):
+    others = [(me + 1 + k) % N for k in range(N - 1)]
+    trs = []
+    for k, q in enumerate(others[:4]):
+        c = T.cores[q]
+        rid, pid, _ = topo.addr(c)
+        m = sum(1 << e for e in topo.engines(core, c)[k::4])
+        trs.append(RemoteDMATransfer(dst_ids=[DstId(rid=rid, pnc=pid)], dma_engine_mask=m, remote_sem=T.sem[rsem], src=src(q), dst=dst(q)))
+    g.remote_dma_fused(trs, local_sem=T.sem[lsem])
+    c = T.cores[others[4]]
+    rid, pid, _ = topo.addr(c)
+    g.remote_dma(dst(others[4]), src(others[4]), T.sem[rsem], T.sem[lsem], pid, rid, topo.mask(core, c))
+
+
+def hand_on(g, core, r, T, topo):
+    c = T.cores[r]
+    inner = [e for e in topo.engines(c, core) if e not in topo.engines(c, T.cores[(r + 1) % N])]
+    for stage in HANDED:
+        name, land, at, w = STAGES[stage]
+        g.wait_ge(T.sem["h" + name], len(inner))
+        src, dst = pieces(T, r, "h" + name, land + "s", at, w)
+        send_five(g, core, r, T, topo, src, dst, land + "s", "loc")
+    g.wait_ge(T.sem.loc, 16 * len(HANDED))
+
+
 def rank_program(g, core, T, topo):
     me = T.rank_of(core)
     if me is None:
+        for r in range(N):
+            if HANDED and neighbour(T, topo, r) == core:
+                hand_on(g, core, r, T, topo)
         return
     others = [(me + 1 + k) % N for k in range(N - 1)]
 
-    def pos(a, q):
-        return (q - a - 1) % N
-
     eng = {"v": g.vector, "s": g.scalar, "p": g, "k": g.tensor, "y": g.sync}
     know = {q: {} for q in eng}
-    count, wr, rd, jobs = {"loc": 0}, {}, {}, []
+    count, wr, rd, jobs, room = {"loc": 0}, {}, {}, [], []
     across = set()
 
     def side(f, out, *args):
-        jobs.append((out[0], lambda: f(out, *args)))
+        jobs.append((out[0], lambda: f(out, *args), 1))
 
     def need(q, evs):
         for sem, val, snap in sorted(evs, key=lambda e: -len(e[2])):
@@ -91,8 +137,12 @@ def rank_program(g, core, T, topo):
             evs += wr.get(k, [])
         for k in writes:
             evs += wr.get(k, []) + rd.get(k, [])
-        if q == "v" and jobs and count["qv"] not in across and any(e[0] == "qv" and e[1] == count["qv"] for e in evs):
-            jobs.pop(0)[1]()
+        if q == "v" and jobs and not room and count["qv"] not in across and any(e[0] == "qv" and e[1] == count["qv"] for e in evs):
+            room.append(3)
+            while jobs and jobs[0][2] <= room[0]:
+                room[0] -= jobs[0][2]
+                jobs.pop(0)[1]()
+            room.pop()
         best = {}
         for e in evs:
             if e[0] not in best or best[e[0]][1] < e[1]:
@@ -182,49 +232,49 @@ def rank_program(g, core, T, topo):
     def scatter(win, off, in_):
         op("v", lambda: g.vector.tensor_copy(win[1].indirect(off[1]), in_[1]), win[0] + off[0] + in_[0], win[0])
 
-    def pick(outn, winn, off, wkeys, hi=None):
-        op("v", lambda: g.vector.tensor_copy(T[outn + "q"][:].bitcast(dt.uint32), T[winn + "q"][:, 0:hi].bitcast(dt.uint32).indirect(off[1])),
-           tuple(x + "q" for x in wkeys) + off[0], (outn + "q",))
-        op("s", lambda: g.scalar.activation(T[outn + "s"][:], T[winn + "s"][:, 0:hi].indirect(off[1]), Copy),
-           tuple(x + "s" for x in wkeys) + off[0], (outn + "s",))
+    def pick(outn, winn, off, wkeys, hi=None, part=(0, None), kinds="qs"):
+        a, b = part
+        key = outn + ("%d" % a if a else "")
+        if "q" in kinds:
+            op("v", lambda: g.vector.tensor_copy(T[outn + "q"][:, a:b].bitcast(dt.uint32), T[winn + "q"][:, 0:hi].bitcast(dt.uint32).indirect(off[1])),
+               tuple(x + "q" for x in wkeys) + off[0], (key + "q",))
+        if "s" in kinds:
+            op("s", lambda: g.scalar.activation(T[outn + "s"][:, a:b], T[winn + "s"][:, 0:hi].indirect(off[1]), Copy),
+               tuple(x + "s" for x in wkeys) + off[0], (key + "s",))
 
     def quant(outn, lo, hi, src, skeys, key):
         ks = (key + "q", key + "s")
-        jobs.append((ks, lambda: op("v", lambda: g.vector.quantize_mx(T[outn + "q"][:, lo:hi], T[outn + "s"][:, lo:hi], T[src][:, 4 * lo:4 * hi]), skeys, ks)))
+        jobs.append((ks, lambda: op("v", lambda: g.vector.quantize_mx(T[outn + "q"][:, lo:hi], T[outn + "s"][:, lo:hi], T[src][:, 4 * lo:4 * hi]), skeys, ks), 3))
 
     def move(outn, srcn, lo, hi, rkeys, key, sem):
         op("y", lambda: g.sync.dma_start(T[outn + "q"][:, lo:hi].bitcast(dt.uint8), T[srcn + "q"][:, lo:hi].bitcast(dt.uint8)),
            tuple(k + "q" for k in rkeys), (key + "q",), sem=sem, inc=16, total=32)
         op("y", lambda: g.sync.dma_start(T[outn + "s"][:, lo:hi], T[srcn + "s"][:, lo:hi]), tuple(k + "s" for k in rkeys), (key + "s",), sem=sem, inc=16, total=32)
 
-    def fan(reads, src, dst, rsem):
-        def call():
-            trs = []
-            for k, q in enumerate(others[:4]):
-                c = T.cores[q]
-                rid, pid, _ = topo.addr(c)
-                m = sum(1 << e for e in topo.engines(core, c)[k::4])
-                trs.append(RemoteDMATransfer(dst_ids=[DstId(rid=rid, pnc=pid)], dma_engine_mask=m, remote_sem=T.sem[rsem], src=src(q), dst=dst(q)))
-            g.remote_dma_fused(trs, local_sem=T.sem.loc)
-            c = T.cores[others[4]]
-            rid, pid, _ = topo.addr(c)
-            g.remote_dma(dst(others[4]), src(others[4]), T.sem[rsem], T.sem.loc, pid, rid, topo.mask(core, c))
-        op("p", call, reads, (), sem=None)
-        count["loc"] += 16
+    def fan(reads, src, dst, rsem, lsem="loc"):
+        op("p", lambda: send_five(g, core, me, T, topo, src, dst, rsem, lsem), reads, (), sem=None)
+        count[lsem] = count.get(lsem, 0) + 16
+        wr[lsem] = [(lsem, count[lsem], {})]
 
-    def columns(name, land, at, w, rsem):
-        def src(n, q):
-            return T[n][:, w * pos(me, q):w * pos(me, q) + w]
+    def columns(stage, keys):
+        name, land, at, w = STAGES[stage]
+        src, dst = pieces(T, me, name + "q", land + "q", at, w)
+        h = neighbour(T, topo, me)
+        rid, pid, _ = topo.addr(h)
+        inner = [e for e in topo.engines(core, h) if e not in topo.engines(core, T.cores[others[0]])]
+        for kind in ("sq", "qs")[stage]:
+            if kind == "q":
+                fan(tuple(k + "q" for k in keys), lambda q: src(q).bitcast(dt.uint8), lambda q: dst(q).bitcast(dt.uint8), land + "q")
+            elif stage not in HANDED:
+                fan(tuple(k + "s" for k in keys), *pieces(T, me, name + "s", land + "s", at, w), land + "s")
+            else:
+                op("p", lambda: g.remote_dma(T["h" + name][:], T[name + "s"][:], T.sem["h" + name], T.sem.loc, pid, rid, sum(1 << e for e in inner)),
+                   tuple(k + "s" for k in keys), (), sem=None)
+                count["loc"] = count.get("loc", 0) + len(inner)
 
-        def dst(n, q):
-            return T[n][:, at + w * pos(q, me):at + w * pos(q, me) + w]
-        fan((name + "q",), lambda q: src(name + "q", q).bitcast(dt.uint8), lambda q: dst(land + "q", q).bitcast(dt.uint8), rsem)
-        fan((name + "s",), lambda q: src(name + "s", q), lambda q: dst(land + "s", q), rsem)
-
-    for s_, v_, ks in (("am1", 16, ("L1i",)), ("ac1", 32, ("Alq", "Als")), ("am2", 16, ("L2i",)), ("ac2", 32, ("Blq", "Bls"))):
-        count[s_] = v_
-        for k in ks:
-            wr[k] = [(s_, v_, {})]
+    for s_, k in (("am1", "L1i"), ("Aq", "Alq"), ("As", "Als"), ("am2", "L2i"), ("Bq", "Blq"), ("Bs", "Bls")):
+        count[s_] = 16
+        wr[k] = [(s_, 16, {})]
 
     def dma(q, out, in_, sem, total=None):
         op(q, lambda: eng[q].dma_start(out[1], in_[1]), in_[0], out[0], sem=sem, inc=16, total=total)
@@ -277,7 +327,6 @@ def rank_program(g, core, T, topo):
     for k in range(8):
         dma("y", o("nxA", p=(16 * k, 16 * k + 16), k="nxA%d" % k), ((), T.nx[:]), "dnxA", 128)
     nxA = (tuple("nxA%d" % k for k in range(8)), T.nxA[:])
-    dma("y", o("wt"), ((), T.w[:]), "dw")
 
     def rows(first, *pieces):
         ks, at = (), first
@@ -289,137 +338,139 @@ def rank_program(g, core, T, topo):
         return o("Kt", first, at, k=ks)
     Ka = rows(0, ([[0, 2], [1, 16]], 0, 0), ([[16, 2], [0, 16]], 0, 1), ([[32, 8], [-160, 2]], 192, 0), ([[32, 8], [192, 2]], 16, 0))
     iota(o("ramp"), [[1, 480]])
-    iota(o("rs"), [[0, 32 * NB]], 1)
+    Kb = rows(96, ([[32, 8], [288, 2]], 0, 0), ([[32, 8], [-256, 2]], 256, 0), ([[80, 2], [8, 16]], 0, 5), ([[16, 2], [1, 16]], 16, 0))
+    K2 = ()
+    for a_, b_, s_, v_ in ((0, R_LAND + me, -96, 96 * me - 1), (R_LAND + me, R_SLOT, -96, 96 * (N - 1) - 1), (R_SLOT, 16, CAPP, 15)):
+        K2 += ("K2%d" % a_,)
+        iota((K2[-1:], T.K2[:, :, a_:b_]), [[0, 2], [s_, b_ - a_]], v_)
     J, G16, B0b = (o("KT", 32 * b, 32 * b + 1, k="KTa") for b in range(3))
     B0, SL, P16 = (o("KT", 32 * b, 32 * b + 1, k="KTb") for b in range(3, 6))
     r16 = o("Kt", 0, 16, k="Kt0")
     ms(o("poolu", k=("offe", "offSt")), 0)
     ms(o("b1t"), 0)
     ms(o("zp0", 0, 16, k="zp0p"), 0.0)
-    tr(o("KT", 0, 96, k="KTa"), Ka)
     ms(o("zp0", 176, 192, k="zp0r"), 0.0)
     ms(o("xt", 0, 4 * ZC, k="xtz"), 0.0)
-    ts(o("oh"), r16, J, eq)
-    ts(cc("GM"), G16, 16.0 * me, eq)
-    if me < N - 1:
-        side(tt, o("Fm", me + 1, N, k="Fm1"), o("oh", R_LAND + me + 1, R_LAND + N), o("oh", R_SLOT, R_OUT - me), add)
-    side(tt, o("Fm", 0, me + 1, k="Fm0"), o("oh", R_LAND, R_LAND + me + 1), o("oh", R_OUT - me, R_OUT + 1), add)
-    side(ts, o("selB"), r16, B0b, add, 32.0 * NB - 1, mn)
-    side(ts, cc("pr0"), J, float(R_LAND), ge)
-    side(ts, cc("wrap"), G16, 16.0 * me, le, float(CAPP * N), mul)
-    side(ts, cc("pr"), J, float(R_OUT - 1), le, cc("pr0"), mul)
+    ms(o("L1", 60, 88, k="L1z"), 0.0)
+    tr(o("KT", 0, 96, k="KTa"), Ka)
+    pads("zp1")
     Fm = o("Fm", 0, N, k=("Fm0", "Fm1"))
     selZ = o("selB", 0, 1)
-    act(cc("FS"), oh(R_N2), scale=K)
+
+    act(o("Ft", 8, 8 + N, k="Fa"), o("Kt", 0, N, k="Kt0"), scale=K * TN, bias=K)
+    ts(o("oh"), r16, J, eq)
+    ts(cc("GM"), G16, 16.0 * me, eq)
+    ts(o("ia", p=PQ), st, 3, shr)
+    ts(o("ib", p=PQ), bt, 1, band)
+    ts(o("e1", p=PQ), st, 96.0, mul)
+    act(o("Ft", 0, N), o("Ft", 8, 8 + N, k="Fa"), scale=oh(R_N2))
+    act(cc("b0"), oh(R_C1), scale=K)
     act(cc("b1"), cc("GM"), scale=K - 1, bias=1.0)
-    act(cc("b0"), oh(R_C1), scale=K, bias=cc("FS"))
-    act(cc("FA"), oh(R_N2), scale=K * TN)
-    act(cc("b2"), cc("b1"), scale=oh(R_C0), bias=cc("b0"))
+    act(cc("FS"), oh(R_N2), scale=K)
     act(cc("base0"), J, scale=float(CAPP), bias=float(15 - CAPP * R_SLOT))
-    act(o("Ft", 0, N), o("Kt", 0, N, k="Kt0"), scale=cc("FA"), bias=cc("b2"))
+    act(cc("b2"), cc("b1"), scale=oh(R_C0), bias=cc("b0"))
     act(cc("own"), cc("GM"), scale=oh(R_C0))
     act(cc("k1"), oh(R_N2), scale=1.0 - BIG, bias=BIG)
     act(cc("cs"), oh(R_C1), scale=1.0 / K)
     act(cc("k2"), cc("own"), scale=1.0 - BIG, bias=cc("k1"))
     act(cc("ms"), cc("own"), scale=1.0 / K)
     act(cc("mb"), cc("own"), scale=-1.0, bias=1.0)
-    act(cc("k3"), oh(R_C1), scale=ZC / K - BIG, bias=cc("k2"))
-
-    ts(o("ia", p=PQ), st, 3, shr)
-    ts(o("e1", p=PQ), st, 96.0, mul)
-    ts(o("ib", p=PQ), bt, 1, band)
+    if me < N - 1:
+        tt(o("Fm", me + 1, N, k="Fm1"), o("oh", R_LAND + me + 1, R_LAND + N), o("oh", R_SLOT, R_OUT - me), add)
+    tt(o("Fm", 0, me + 1, k="Fm0"), o("oh", R_LAND, R_LAND + me + 1), o("oh", R_OUT - me, R_OUT + 1), add)
     ts(o("e2", p=PQ), o("ia", p=PQ), -767.0, mul)
     ts(o("e3", p=PQ), o("ib", p=PQ), 48.0, mul)
-    tt(o("e4", p=PQ), o("e1", p=PQ), o("e2", p=PQ), add)
     ts(o("b1t", 0, 10, p=PQ), bt, 1, shr)
+    ts(o("selB"), r16, B0b, add, 32.0 * NB - 1, mn)
+    tt(o("e4", p=PQ), o("e1", p=PQ), o("e2", p=PQ), add)
+    tt(o("Fc", 0, N), Fm, o("Ft", 0, N), add)
+    ts(o("offSt", p=PQ), st, float(ZC), add)
+    ts(cc("pr0"), J, float(R_LAND), ge)
     tt(o("offe", p=PQ), o("e4", p=PQ), o("e3", p=PQ), add)
+    ts(o("Fb", 0, N), o("Fc", 0, N), cc("b2"), add)
+    ts(cc("wrap"), G16, 16.0 * me, le, float(CAPP * N), mul)
+    ts(cc("pr"), J, float(R_OUT - 1), le, cc("pr0"), mul)
     ts(o("zp0", 16, 176), ind(o("nxr"), o("offe")), 2.0, mul, 1.0, add)
-    tt(o("Fb", 0, N), Fm, o("Ft", 0, N), add)
-    side(ts, o("offSt", p=PQ), st, float(ZC), add)
+    side(ts, o("selP", 0, 1), B0b, float(R_LAND + me), add, 32.0 * NB - 1, mn)
+    side(ts, o("jl"), r16, 16.0, mul, J, add)
+    side(ts, o("mD", 0, 32, k="mD0"), o("Kt", 0, 32, k="Kt0"), J, eq, cc("pr"), mul)
+    pads("zp2")
     turn("zp0")
     tt(o("L1o"), ind(Tz, selZ), o("b1t"), add)
-    fan(("L1o",), lambda q: T.L1o[:, 0:10], lambda q: T.L1[:, 10 * me:10 * me + 10], "am1")
+    fan(("L1o",), lambda q: T.L1o[:, 0:10], lambda q: T.L1[:, 10 * me:10 * me + 10], "am1", "left")
     dma("y", o("L1", 10 * me, 10 * me + 10, k="L1m"), o("L1o", 0, 10), "dL1")
+    dma("y", o("wt"), (("left",), T.w[:]), "dw")
 
-    Kb = rows(96, ([[32, 8], [288, 2]], 0, 0), ([[32, 8], [-256, 2]], 256, 0), ([[80, 2], [8, 16]], 0, 5), ([[16, 2], [1, 16]], 16, 0))
-    K2 = ()
-    for a_, b_, s_, v_ in ((0, R_LAND + me, -96, 96 * me - 1), (R_LAND + me, R_SLOT, -96, 96 * (N - 1) - 1), (R_SLOT, 16, CAPP, 15)):
-        K2 += ("K2%d" % a_,)
-        iota((K2[-1:], T.K2[:, :, a_:b_]), [[0, 2], [s_, b_ - a_]], v_)
     iota(o("S1", 0, 272), [[0, 272]])
     iota(o("idtab", 0, 1, k="idz"), [[0, 1]], -1)
 
     def Fk(k):
         act(o("F", TN * k, TN * k + TN, k="F%d" % k), o("ramp", 0, TN), scale=cc("FS"), bias=o("Fb", k, k + 1))
-    for k in range(4):
+    for k in range(N):
         Fk(k)
-    act(o("strow"), ind(o("ramp"), o("offSt")))
-    fill(o("S0", 0, 288), 288)
-    Fk(4)
-    Fk(5)
-    ts(o("r1i"), ind(Tz, selZ), -float(TN), add, 0.5 / TN, mul)
-    side(ms, o("rs", 0, None, 16, k=("rs0",)), 0.0)
+    ts(o("offr"), ind(Tz, selZ), -float(TN), add, 0.5 / TN, mul)
     side(cp, o("nxo"), nxA)
+    side(tr, o("KT", 96, 192, k="KTb"), Kb)
+    side(tr, o("KU"), (K2, T.K2[:]))
+    jobs.append((("rs",), lambda: ms(o("rs"), 1.0), 3))
+    side(ts, o("selA"), o("ramp", 0, 32), B0, add)
+    side(ms, o("rs", 0, None, 16, k=("rs0",)), 0.0)
     side(ms, o("rs", R_SLOT, None, 16, k=("rs1",)), 0.0)
-    xk = ("x0", "x1", "x2")
-    for k, (a_, b_) in enumerate(((0, 136), (136, 268), (268, BA))):
-        quant("x", a_, b_, "xt", ("xtx", "xtz"), xk[k])
-    cp(o("offr"), o("r1i", 0, 10))
-    cp(o("G0"), ind(Fm, o("offr")))
-    scan(o("cn0"), o("G0"), o("G0"), cc("base0"), add, mx)
+    jobs.append((("S0",), lambda: ms(o("S0", 0, 288), 0.0), 3))
+    side(ts, o("selL", 0, 1), SL, 0.125, mul)
+    side(ts, o("mD", 32, 64, k="mD1"), o("ramp", 0, 32), P16, eq, cc("pr"), mul)
+    def own_codes(buf):
+        for a_, b_ in ((0, 136), (136, 268), (268, BA)):
+            quant(buf, a_, b_, "xt", ("xtx", "xtz"), "%s%d" % (buf, a_))
+        return (buf + "0", buf + "136", buf + "268")
+    xk = own_codes("x")
+    cp(o("G0"), ind(Fm, o("offr", 0, 10)))
+    act(cc("k3"), oh(R_C1), scale=ZC / K - BIG, bias=cc("k2"))
+    act(o("strow"), ind(o("ramp"), o("offSt")))
     act(o("TAB", 1, 769, k="TABa"), ind(o("F", k=tuple("F%d" % k for k in range(N))), o("nxo")))
+    act(cc("c1"), G16, scale=CAPP / 16.0, bias=cc("wrap"))
+    act(o("TAB", 0, 770, 769, k="TABz"), o("ramp", 0, 2), scale=0.0, bias=oh(R_OUT))
+    act(cc("prn"), cc("pr"), scale=-LIFT)
+    for b in range(2):
+        act(o("capT", 1 + b, 769, 2, k="capT%d" % b), o("ramp", 0, TN), scale=cc("cs"), bias=cc("k3"))
+    act(cc("c2"), cc("c1"), bias=float(BA - 1 - CAPP * (me + 1) - 15 - CAPP * (R_C0 - R_SLOT)))
+    act(o("capT", 0, 770, 769, k="capT2"), o("ramp", 0, 2), scale=0.0, bias=cc("k3"))
+    act(o("Mt"), o("strow"), scale=cc("ms"), bias=cc("mb"))
+
+    scan(o("cn0"), o("G0"), o("G0"), cc("base0"), add, mx)
     tt(o("zp0", 16, 176), o("G0"), o("cn0"), mul)
     turn("zp0")
     sums()
     cp(o("off0"), ind(o("SS"), o("selB", R_OUT, R_OUT + 1)))
-    move("A", "x", 0, BA, xk, "Ax", "dxA")
-    move("B", "x", 0, BA, xk, "Bx", "dxB")
-    side(tr, o("KT", 96, 192, k="KTb"), Kb)
-    side(ts, o("selA"), o("ramp", 0, 32), B0, add)
-    side(ms, o("L1", 60, 88, k="L1z"), 0.0)
-    side(tr, o("KU"), (K2, T.K2[:]))
-    side(ts, o("selL", 0, 1), SL, 0.125, mul)
-    side(ts, o("mD", 0, 32, k="mD0"), o("Kt", 0, 32, k="Kt0"), J, eq, cc("pr"), mul)
-    side(ts, o("mD", 32, 64, k="mD1"), o("ramp", 0, 32), P16, eq, cc("pr"), mul)
-    pads("zp1")
+    act(o("DT", 64, 65, k="DTb"), o("KU", 0, 1), scale=cc("pr"), bias=cc("prn"))
+    act(cc("KUc"), cc("c2"), scale=oh(R_C0), bias=o("KU", 0, 1))
+    act(cc("in1"), o("DT", 64, 65, k="DTb"), scale=-1.0, bias=cc("KUc"))
     scatter(o("S0"), o("off0", 0, 10), o("strow"))
     turn_slots("S0", 9)
+
+    ts(o("offE"), ind(o("L1", k=("L1i", "L1m", "L1z")), o("selL", 0, 1)), float(-2 * TN * me), add, float(2 * TN + 1), mn)
+    offE = o("offE", 0, 10)
     cp(o("offi", k="offi"), ind(Ts, o("selA", 16 * (me % 2), 16 * (me % 2) + 1)))
+    act(o("G1"), ind(o("TAB", k=("TABa", "TABz")), offE), acc=o("x1"))
+    tt(o("cap1"), ind(o("capT", k=("capT0", "capT1", "capT2")), offE), o("Mt"), mul)
     ki = ("offi",)
     for q in range(4):
         if 32 * q != Q:
             ki += ("offi%d" % q,)
             op("v", lambda: g.vector.tensor_copy(T.offi[32 * q:32 * q + 32, 0:16], T.offi[Q:Q + 32, 0:16]), ("offi",), ki[-1:])
-    act(cc("c1"), G16, scale=CAPP / 16.0, bias=cc("wrap"))
-    act(o("TAB", 0, 770, 769, k="TABz"), o("ramp", 0, 2), scale=0.0, bias=oh(R_OUT))
-    act(cc("c2"), cc("c1"), bias=float(BA - 1 - CAPP * (me + 1) - 15 - CAPP * (R_C0 - R_SLOT)))
-    for b in range(2):
-        act(o("capT", 1 + b, 769, 2, k="capT%d" % b), o("ramp", 0, TN), scale=cc("cs"), bias=cc("k3"))
-    act(o("capT", 0, 770, 769, k="capT2"), o("ramp", 0, 2), scale=0.0, bias=cc("k3"))
-    act(cc("prn"), cc("pr"), scale=-LIFT)
-    act(cc("KUc"), cc("c2"), scale=oh(R_C0), bias=o("KU", 0, 1))
-    act(o("DT", 64, 65, k="DTb"), o("KU", 0, 1), scale=cc("pr"), bias=cc("prn"))
-    act(o("Mt"), o("strow"), scale=cc("ms"), bias=cc("mb"))
-    act(cc("in1"), o("DT", 64, 65, k="DTb"), scale=-1.0, bias=cc("KUc"))
+    ts(o("D"), o("mD", k=("mD0", "mD1")), o("x1"), mul)
     pick("sl1", "x", (ki, T.offi[:, 0:15]), xk)
-    columns("sl1", "A", BA, CAPP, "ac1")
-    side(ts, o("selP", 0, 1), B0b, float(R_LAND + me), add, 32.0 * NB - 1, mn)
-    side(ts, o("jl"), r16, 16.0, mul, J, add)
-    pads("zp2")
+    columns(0, ("sl1",))
+    tr(o("DT", 0, 64), o("D"))
+    scan(o("cn1"), o("G1"), o("cap1"), cc("in1"), add, mn)
+    Ak = own_codes("A")
+    Bx = own_codes("B")
     for k in range(2 * 3):
         quant("w", 128 * k, 128 * k + 128, "wt", ("wt",), "w%d" % k)
-
-    ts(o("offE"), ind(o("L1", k=("L1i", "L1m", "L1z")), o("selL", 0, 1)), float(-2 * TN * me), add, float(2 * TN + 1), mn)
-    offE = o("offE", 0, 10)
-    act(o("G1"), ind(o("TAB", k=("TABa", "TABz")), offE), acc=o("x1"))
-    tt(o("cap1"), ind(o("capT", k=("capT0", "capT1", "capT2")), offE), o("Mt"), mul)
-    ts(o("D"), o("mD", k=("mD0", "mD1")), o("x1"), mul)
-    scan(o("cn1"), o("G1"), o("cap1"), cc("in1"), add, mn)
-    tr(o("DT", 0, 64), o("D"))
-    tt(o("zl"), o("G1"), o("cn1"), mul)
     red(o("tot"), o("DT", 0, 32))
     pre = (("pre",), T.L2[:, me, 0:1])
     red(pre, o("DT", 32, 65, k=("DT", "DTb")))
+    tt(o("zl"), o("G1"), o("cn1"), mul)
     ts((("pre1",), T.L2[32:64, me, 0:1]), (("pre",), T.L2[32:64, me, 0:1]), o("tot", p=(0, 32)), add)
     ts((("pre2",), T.L2[64:96, me, 0:1]), (("pre",), T.L2[64:96, me, 0:1]), o("tot", p=(0, 32)), add, o("tot", p=(32, 64)), add)
     pre = (("pre", "pre1", "pre2"), pre[1])
@@ -434,14 +485,14 @@ def rank_program(g, core, T, topo):
     act(cc("z1"), oh(R_LAND + me), bias=oh(R_ID))
     act(cc("es"), cc("o34"), scale=1.0 / K)
     act(cc("z2"), cc("o34"), scale=K, bias=cc("z1"))
-    act(cc("p1"), cc("o34"), scale=BL / K)
+    act(cc("p1"), cc("o34"), scale=float(BL))
     act(cc("z3"), oh(R_C2), scale=float(ZC), bias=cc("z2"))
-    act(cc("p2"), oh(R_C1), scale=CAPP / K, bias=cc("p1"))
+    act(cc("p2"), oh(R_C1), scale=float(CAPP), bias=cc("p1"))
     act(cc("e1"), cc("o34"), scale=-BIG, bias=BIG)
     act(cc("i0"), G16, scale=V / 16.0)
     act(cc("e2"), oh(R_C2), scale=1.0 - BIG, bias=cc("e1"))
     act(cc("i2"), oh(R_LAND + me), scale=V + 15 + N * (1 + LIFT) - 96 * 15)
-    act(o("ptab", 0, 480, k="pt0"), o("ramp"), scale=cc("es"), bias=cc("p2"))
+    act(o("ptab", 0, 480, k="pt0"), o("ramp"), scale=cc("o34"), bias=cc("p2"))
     act(cc("i3"), cc("i0"), scale=oh(R_ID), bias=cc("i2"))
     fill(o("ptab", 480, 736, k="pt1"), 256)
     low = me < N // 2
@@ -460,14 +511,16 @@ def rank_program(g, core, T, topo):
     scatter(o("S1"), o("off1", 0, 10), o("zp1", 16, 176))
     turn_slots("S1", 8)
     k2 = gather_lists("off2", R_C0, 2)
-    pick("sl2", "A", (k2, T.off2[:, 0:30]), ("Al", "Ax"))
-    columns("sl2", "B", BL, 2 * CAPP, "ac2")
     move("B", "A", BA, BL, ("Al",), "Ba", "dAB")
-    iota(o("idtab", 1, 961, k="idn", p=(0, 1)), [[1, N], [0, V]])
 
+    def third(k, kind):
+        pick("sl2", "A", (k2, T.off2[:, 10 * k:10 * k + 10]), ("Al",) + Ak, part=(V * k, V * k + V), kinds=kind)
     L2k = ("L2i", "L2o") + pre[0]
+    third(0, "q")
     tt((("L2h",), T.L2h[:]), (L2k, T.L2[:, 0:3, 0:11]), (L2k, T.L2[:, 3:6, 0:11]), add)
+    third(1, "q")
     tt(o("L2a"), (("L2h",), T.L2h[:, 0, :]), (("L2h",), T.L2h[:, 1, :]), add)
+    third(2, "q")
     tt(o("vi", 0, 11), o("L2a"), (("L2h",), T.L2h[:, 2, :]), add)
     if low:
         ts(o("offN"), o("vi", 1, 11), 1.0 / K, mul, float(at + TN), mn)
@@ -475,14 +528,18 @@ def rank_program(g, core, T, topo):
         ts(o("offN"), o("vi", 1, 11), 1.0 / K, mul, float(-TN * me), add)
     ts(o("sli"), o("vi", 1, 11), int(K) - 1, band)
     act(o("G2"), ind(o("ztab", k=zk), o("offN")))
+    for k in range(3):
+        third(k, "s")
+    columns(1, ("sl2", "sl2160", "sl2320"))
+    iota(o("idtab", 1, 961, k="idn", p=(0, 1)), [[1, N], [0, V]])
     ts(o("in2"), o("vi", 0, 1), oh(R_LAND + me), mul, cc("i3"), add)
     cp(o("offS"), o("sli"))
-    tt(o("cap2"), ind(o("ptab", k=("pt0", "pt1")), o("offS")), o("E"), mx)
-    scan(o("cn2"), o("G2"), o("cap2"), o("in2"), add, mn)
+    scan(o("cn2"), o("G2"), o("E"), o("in2"), add, mn)
     tt(o("zp2", 16, 176), o("G2"), o("cn2"), mul)
     turn("zp2")
+    tt(o("cap2"), ind(o("ptab", k=("pt0", "pt1")), o("offS")), o("zp2", 16, 176), mx)
     tt(o("off20"), ind(Tz, o("selP", 0, 1)), o("jl"), mx)
-    scatter(o("S2"), o("off20", 0, 10), o("zp2", 16, 176))
+    scatter(o("S2"), o("off20", 0, 10), o("cap2"))
     turn_slots("S2", 9, V)
     kF = gather_lists("offF", R_ID, 4)
     off = [(kF, T.offF[:, 16 * k:16 * k + 16]) for k in range(4)]
@@ -494,9 +551,9 @@ def rank_program(g, core, T, topo):
             wk = "w%d" % (k * NO + oo)
             op("k", lambda: g.tensor.matmul_mx(T["ps_%d" % oo][:, 0:M], T.wq[:, a:a + 128], T.ws[:, a:a + 128], T[n + "q"][:], T[n + "s"][:], k == 2, last),
                (wk + "q", wk + "s", n + "q", n + "s"), ("ps_%d" % oo,) if last else ())
-    pick("p2", "B", off[1], ("Bx",), BA)
+    pick("p2", "B", off[1], Bx, BA)
     product(2, False)
-    Bk = ("Bx", "Ba", "Bl")
+    Bk = Bx + ("Ba", "Bl")
     pick("p0", "B", off[2], Bk)
     product(0, False)
     pick("p1", "B", off[3], Bk)

@@ -33,25 +33,27 @@ def _pool(buf, dtype, **widths):
 
 _add(_I, st0=10, bt0=10, b1t=16, nxr=768, nxA=48, r1i=16, vi=12, sli=10)
 _add(_F, cc=48, oh=16, ramp=480, Kt=192, KT=192, K2=(2, 16), KU=32, tq1=(5, 2, 3), Fm=8, Fb=8, Fc=8, Ft=16, F=2304, TAB=776, capT=776,
-     ztab=1160, ptab=736, rs=32 * NB, mD=64, D=64, DT=72, idtab=968, idt=M, yo0=M, yo1=M)
+     ztab=1160, ptab=736, rs=96, mD=64, D=64, DT=72, idtab=968, idt=M, yo0=M, yo1=M)
 _add(_F, zp0=192, zp1=192, zp2=192, Tz=32 * NB, SS=32 * NB, Ts=544, S0=416, S1=416, S2=448,
      G0=V, G1=V, G2=V, cn0=V, cn1=V, cn2=V, strow=V, Mt=V, cap1=V, E=V, cap2=V, zl=V,
-     L1o=16, L1=88, L2=(6, 20), L2h=(3, 11), Ha=64, Hb=64, tq=64, yq=64)
-_add(_U, selA=32, selB=16, selP=2, selL=2, offr=16, off0=16, offi=16, nxo=48, offE=16, off1=16, off2=32,
+     L1o=16, L1=88, L2=(6, 20), L2h=(3, 11), Ha=64, Hb=64, tq=64)
+_add(_U, selA=32, selB=16, selP=2, selL=2, same=16, offr=16, off0=16, offi=16, nxo=48, offE=16, off1=16, off2=32,
      offN=10, offS=10, off20=16, offF=64)
 _pool("poolu", _U, offe=10, offSt=10)
 _pool("pooli", _I, ia=10, ib=10)
 _pool("poolf", _F, e1=10, e2=10, e3=10, e4=10, e5=10, x1=1, tot=1, L2a=11, in2=1, jl=16, pb=16)
 _add("bfloat16", xt=4 * BA, wt=3072)
-for _n, _w in (("x", BA), ("w", 768), ("sl1", REM), ("A", BL), ("sl2", 2 * REM), ("B", BW), ("p0", M), ("p1", M), ("p2", M)):
+for _n, _w in (("x", BA), ("w", 768), ("sl1", REM), ("A", BL), ("sl2", 2 * REM), ("B", BW), ("p0", M), ("p1", M)):
     SCRATCH[_n + "q"] = ("sbuf", [128, _w], _C)
     SCRATCH[_n + "s"] = ("sbuf", [128, _w], _S)
-_add(_S, hsl1=REM, hsl2=2 * REM)
-SCRATCH["ps_0"] = ("psum", [128, 512], _F)
-SCRATCH["ps_1"] = ("psum", [128, 512], _F)
+_add(_S, hsl1s=REM, hsl2s=2 * REM)
+_add(_C, hsl1q=REM, hsl2q=2 * REM)
+_add(_F, R20=BA, R21=BA, r20=M, r21=M)
+for _n in range(4):
+    SCRATCH["ps_%d" % _n] = ("psum", [128, 512], _F)
 
-SEMAPHORES = ["qv", "qs", "qp", "qk", "dst0", "dbt0", "dnx", "dnxA", "dx", "dw", "left", "dAB", "dL1",
-              "did", "dy0", "dy1", "am1", "Aq", "As", "am2", "Bq", "Bs", "hsl1", "hsl2", "loc"]
+SEMAPHORES = ["qv", "qs", "qp", "qk", "dst0", "dbt0", "dnx", "dnxA", "dx", "dw0", "dw1", "left", "dxA", "dAB", "dL1",
+              "did", "dy0", "dy1", "am1", "Aq", "As", "am2", "am3", "Bq", "Bs", "hsl1q", "hsl1s", "hsl2q", "hsl2s", "loc"]
 
 add, sub, mul, mx, mn = AluOpType.add, AluOpType.subtract, AluOpType.mult, AluOpType.max, AluOpType.min
 eq, ge, gt, le = AluOpType.is_equal, AluOpType.is_ge, AluOpType.is_gt, AluOpType.is_le
@@ -62,53 +64,76 @@ Copy, Ident = ActivationFunctionType.Copy, ActivationFunctionType.Identity
 STAGES = (("sl1", "A", BA, CAPP), ("sl2", "B", BL, 2 * CAPP))
 
 
-HANDED = [0]
+OPT = dict(s0=0, pre=0, late=0, mvA=1, mvB=0, o1="qs", one=1, early=0, at=0, split=1, sat=2)
+WAYS = {(0, "q"): (((0, 1), None), ((2, 3, 4), None)), (0, "s"): (((0, 1, 2, 3, 4), 0),),
+        (1, "q"): (((0, 1), None), ((2, 3), None), ((4,), None)), (1, "s"): (((0, 1, 2, 3, 4), None),)}
+
+
+def calls(places):
+    k = 4 if len(places) > 3 else 2 if len(places) > 1 else 1
+    return [places[:k]] + (calls(places[k:]) if places[k:] else [])
+
+
+def raw(ap, kind):
+    return ap.bitcast(dt.uint8) if kind == "q" else ap
 
 
 def pos(a, q):
     return (q - a - 1) % N
 
 
-def pieces(T, me, name, land, at, w):
-    return (lambda q: T[name][:, w * pos(me, q):w * pos(me, q) + w]), (lambda q: T[land][:, at + w * pos(q, me):at + w * pos(q, me) + w])
+def pieces(T, me, name, stage, kind):
+    _, land, at, w = STAGES[stage]
+    return ((lambda q: raw(T[name + kind][:, w * pos(me, q):w * pos(me, q) + w], kind)),
+            (lambda q: raw(T[land + kind][:, at + w * pos(q, me):at + w * pos(q, me) + w], kind)))
 
 
-def neighbour(T, topo, r):
+def neighbours(T, topo, r):
     c = T.cores[r]
     able = [h for h in topo.cores_of(c) if h != c and all(topo.may_write(h, d) for d in T.cores if d != c)]
-    return min(able, key=lambda h: topo.die(h) != topo.die(c))
+    return sorted(able, key=lambda h: topo.die(h) != topo.die(c))
+
+
+def inner(T, topo, r):
+    c = T.cores[r]
+    return [e for e in topo.engines(c, neighbours(T, topo, r)[0]) if e not in topo.engines(c, T.cores[(r + 1) % N])]
+
+
+def send(g, core, me, T, topo, places, src, dst, rsem, lsem):
+    trs = []
+    for k, d in enumerate(places):
+        q = (me + 1 + d) % N
+        c = T.cores[q]
+        rid, pid, _ = topo.addr(c)
+        m = sum(1 << e for e in topo.engines(core, c)[k::len(places)])
+        trs.append(RemoteDMATransfer(dst_ids=[DstId(rid=rid, pnc=pid)], dma_engine_mask=m, remote_sem=T.sem[rsem], src=src(q), dst=dst(q)))
+    g.remote_dma_fused(trs, local_sem=T.sem[lsem])
 
 
 def send_five(g, core, me, T, topo, src, dst, rsem, lsem):
-    others = [(me + 1 + k) % N for k in range(N - 1)]
-    trs = []
-    for k, q in enumerate(others[:4]):
-        c = T.cores[q]
-        rid, pid, _ = topo.addr(c)
-        m = sum(1 << e for e in topo.engines(core, c)[k::4])
-        trs.append(RemoteDMATransfer(dst_ids=[DstId(rid=rid, pnc=pid)], dma_engine_mask=m, remote_sem=T.sem[rsem], src=src(q), dst=dst(q)))
-    g.remote_dma_fused(trs, local_sem=T.sem[lsem])
-    c = T.cores[others[4]]
-    rid, pid, _ = topo.addr(c)
-    g.remote_dma(dst(others[4]), src(others[4]), T.sem[rsem], T.sem[lsem], pid, rid, topo.mask(core, c))
+    for places in ((0, 1, 2, 3), (4,)):
+        send(g, core, me, T, topo, places, src, dst, rsem, lsem)
 
 
 def hand_on(g, core, r, T, topo):
-    c = T.cores[r]
-    inner = [e for e in topo.engines(c, core) if e not in topo.engines(c, T.cores[(r + 1) % N])]
-    for stage in HANDED:
-        name, land, at, w = STAGES[stage]
-        g.wait_ge(T.sem["h" + name], len(inner))
-        src, dst = pieces(T, r, "h" + name, land + "s", at, w)
-        send_five(g, core, r, T, topo, src, dst, land + "s", "loc")
-    g.wait_ge(T.sem.loc, 16 * len(HANDED))
+    left = 0
+    for (stage, kind), ways in sorted(WAYS.items()):
+        name, land = "h" + STAGES[stage][0], STAGES[stage][1]
+        for places, via in ways:
+            if via is not None and neighbours(T, topo, r)[via] == core:
+                g.wait_ge(T.sem[name + kind], len(inner(T, topo, r)))
+                for part in calls(places):
+                    send(g, core, r, T, topo, part, *pieces(T, r, name, stage, kind), land + kind, "loc")
+                    left += len(topo.engines(core, T.cores[(r + 1) % N]))
+    if left:
+        g.wait_ge(T.sem.loc, left)
 
 
 def rank_program(g, core, T, topo):
     me = T.rank_of(core)
     if me is None:
         for r in range(N):
-            if HANDED and neighbour(T, topo, r) == core:
+            if core in neighbours(T, topo, r):
                 hand_on(g, core, r, T, topo)
         return
     others = [(me + 1 + k) % N for k in range(N - 1)]
@@ -246,45 +271,64 @@ def rank_program(g, core, T, topo):
         ks = (key + "q", key + "s")
         jobs.append((ks, lambda: op("v", lambda: g.vector.quantize_mx(T[outn + "q"][:, lo:hi], T[outn + "s"][:, lo:hi], T[src][:, 4 * lo:4 * hi]), skeys, ks), 3))
 
-    def move(outn, srcn, lo, hi, rkeys, key, sem):
+    def move(outn, srcn, lo, hi, rkeys, key, sem, behind=()):
         op("y", lambda: g.sync.dma_start(T[outn + "q"][:, lo:hi].bitcast(dt.uint8), T[srcn + "q"][:, lo:hi].bitcast(dt.uint8)),
-           tuple(k + "q" for k in rkeys), (key + "q",), sem=sem, inc=16, total=32)
+           tuple(k + "q" for k in rkeys) + behind, (key + "q",), sem=sem, inc=16, total=32)
         op("y", lambda: g.sync.dma_start(T[outn + "s"][:, lo:hi], T[srcn + "s"][:, lo:hi]), tuple(k + "s" for k in rkeys), (key + "s",), sem=sem, inc=16, total=32)
 
-    def fan(reads, src, dst, rsem, lsem="loc"):
-        op("p", lambda: send_five(g, core, me, T, topo, src, dst, rsem, lsem), reads, (), sem=None)
-        count[lsem] = count.get(lsem, 0) + 16
+    def everyone(reads, src, dst, rsem, lsem="loc"):
+        if OPT["one"]:
+            ids = [DstId(rid=topo.addr(T.cores[q])[0], pnc=topo.addr(T.cores[q])[1]) for q in others]
+            tf = RemoteDMATransfer(dst_ids=ids, dma_engine_mask=topo.mask(core, T.cores[others[0]]), remote_sem=T.sem[rsem], srcs=[src], dsts=[dst] * len(ids))
+            op("p", lambda: g.remote_dma_fused([tf], local_sem=T.sem[lsem]), reads, (), sem=None)
+        else:
+            op("p", lambda: send_five(g, core, me, T, topo, lambda q: src, lambda q: dst, rsem, lsem), reads, (), sem=None)
+        count[lsem] = count.get(lsem, 0) + (8 if OPT["one"] else 16)
         wr[lsem] = [(lsem, count[lsem], {})]
 
-    def columns(stage, keys):
+    def columns(stage, keys, kind, which=None):
         name, land, at, w = STAGES[stage]
-        src, dst = pieces(T, me, name + "q", land + "q", at, w)
-        h = neighbour(T, topo, me)
-        rid, pid, _ = topo.addr(h)
-        inner = [e for e in topo.engines(core, h) if e not in topo.engines(core, T.cores[others[0]])]
-        for kind in ("sq", "qs")[stage]:
-            if kind == "q":
-                fan(tuple(k + "q" for k in keys), lambda q: src(q).bitcast(dt.uint8), lambda q: dst(q).bitcast(dt.uint8), land + "q")
-            elif stage not in HANDED:
-                fan(tuple(k + "s" for k in keys), *pieces(T, me, name + "s", land + "s", at, w), land + "s")
+        reads = tuple(k + kind for k in keys)
+        for places, via in WAYS[stage, kind]:
+            if which is not None and places[0] not in which:
+                continue
+            if via is None:
+                for part in calls(places):
+                    op("p", lambda: send(g, core, me, T, topo, part, *pieces(T, me, name, stage, kind), land + kind, "loc"), reads, (), sem=None)
+                    count["loc"] += 8
             else:
-                op("p", lambda: g.remote_dma(T["h" + name][:], T[name + "s"][:], T.sem["h" + name], T.sem.loc, pid, rid, sum(1 << e for e in inner)),
-                   tuple(k + "s" for k in keys), (), sem=None)
-                count["loc"] = count.get("loc", 0) + len(inner)
+                rid, pid, _ = topo.addr(neighbours(T, topo, me)[via])
+                a, b = w * places[0], w * places[-1] + w
+                op("p", lambda: g.remote_dma(raw(T["h" + name + kind][:, a:b], kind), raw(T[name + kind][:, a:b], kind), T.sem["h" + name + kind], T.sem.loc,
+                                             pid, rid, sum(1 << e for e in inner(T, topo, me))), reads, (), sem=None)
+                count["loc"] += len(inner(T, topo, me))
 
-    for s_, k in (("am1", "L1i"), ("Aq", "Alq"), ("As", "Als"), ("am2", "L2i"), ("Bq", "Blq"), ("Bs", "Bls")):
-        count[s_] = 16
-        wr[k] = [(s_, 16, {})]
+    for s_, k in (("am1", "L1i"), ("am2", "L2i")):
+        count[s_] = 40 if OPT["one"] else 16
+        wr[k] = [(s_, count[s_], {})]
+    for (stage, kind), ways in WAYS.items():
+        land = STAGES[stage][1]
+        count[land + kind] = 8 * sum(len(calls(places)) for places, _ in ways)
+        wr[land + "l" + kind] = [(land + kind, count[land + kind], {})]
 
     def dma(q, out, in_, sem, total=None):
         op(q, lambda: eng[q].dma_start(out[1], in_[1]), in_[0], out[0], sem=sem, inc=16, total=total)
 
-    Tz = (("Tze", "Tzo"), T.Tz[:])
+    Tz = (("Tz0", "Tz1", "Tz2", "Tz3"), T.Tz[:])
     Ts = (("Tse", "Tso"), T.Ts[:])
+    HALF = ((0, 80), (80, V))
+    TURNS = ((0, 0, 96, "pa"), (192, 16, 64, "a"), (96, 96, 96, "br"), (256, 80, 96, "ab"))
 
-    def turn(zp):
-        tr(o("Tz", 0, 192, k="Tze"), o(zp, 0, 192, k=(zp, zp + "p", zp + "r")))
-        tr(o("Tz", 192, 352, k="Tzo"), o(zp, 16, 176))
+    def halves(f, zp, cuts=HALF):
+        for h, (a, b) in enumerate(cuts):
+            f(o(zp, 16 + a, 16 + b, k=zp + "ab"[h]), a, b)
+
+    def row(zp):
+        return o(zp, 16, 176, k=(zp + "a", zp + "b"))
+
+    def turn(zp, parts=TURNS):
+        for k, (to, at, n, ks) in enumerate(parts):
+            tr(o("Tz", to, to + n, k="Tz%d" % k), o(zp, at, at + n, k=tuple(zp + c for c in ks)))
 
     def turn_slots(win, even, at=0):
         tr(o("Ts", 256, 256 + 32 * even, k="Tse"), o(win, at, at + 32 * even))
@@ -295,23 +339,19 @@ def rank_program(g, core, T, topo):
         side(ms, o(zp, 176, 192, k=zp + "r"), 0.0)
 
     def sums():
-        scan(o("SS"), o("rs", k=("rs", "rs0", "rs1")), Tz, 0.0, mul, add)
+        for k, (to, _, n, _) in enumerate(TURNS):
+            scan(o("SS", to, to + n, k="SS%d" % k), o("rs", 0, n, k=("rs", "rs0", "rs1")), o("Tz", to, to + n, k="Tz%d" % k), 0.0, mul, add)
+    SS = o("SS", k=("SS0", "SS1", "SS2", "SS3"))
 
-    def gather_lists(off, row, rows):
-        n = 16 * rows
-        cp(o("Ha", 0, n), ind(Ts, o("selA", row, row + rows)))
-        tt(o("Hb", 0, n), ind(Ts, o("selA", 16 + row, 16 + row + rows)), o("Ha", 0, n), add)
-        if rows == 2:
-            n = 30
-            for k in range(2):
-                tt((("tq%d" % k,), T.tq1[0:64, :, k, :]), o("Hb", 16 * k, 16 * k + 15, p=(0, 64)), o("Hb", 16 * k, 16 * k + 15, p=(64, 128)), add)
-            tq = [(("tq0", "tq1"), T.tq1[32 * h:32 * h + 32]) for h in range(2)]
-        else:
-            tt(o("tq", 0, n, p=(0, 64)), o("Hb", 0, n, p=(0, 64)), o("Hb", 0, n, p=(64, 128)), add)
-            tq = [o("tq", 0, n, p=(32 * h, 32 * h + 32)) for h in range(2)]
+    def gather_lists(off):
+        cp(o("Ha", 0, 32, k="Ha0"), ind(Ts, o("selA", R_C0, R_C0 + 2)))
+        tt(o("Hb", 0, 32, k="Hb0"), ind(Ts, o("selA", 16 + R_C0, 18 + R_C0)), o("Ha", 0, 32, k="Ha0"), add)
+        for k in range(2):
+            tt((("tp%d" % k,), T.tq1[0:64, :, k, :]), o("Hb", 16 * k, 16 * k + 15, k="Hb0", p=(0, 64)), o("Hb", 16 * k, 16 * k + 15, k="Hb0", p=(64, 128)), add)
+        tq = [(("tp0", "tp1"), T.tq1[32 * h:32 * h + 32]) for h in range(2)]
         across.update((count["qv"], count["qv"] + 4))
         for h in range(4):
-            tt(o(off, 0, n, k=off + "%d" % h, p=(32 * h, 32 * h + 32)), tq[0], tq[1], add)
+            tt(o(off, 0, 30, k=off + "%d" % h, p=(32 * h, 32 * h + 32)), tq[0], tq[1], add)
         return tuple(off + "%d" % h for h in range(4))
 
     Q = 32 * (me // 2)
@@ -327,6 +367,7 @@ def rank_program(g, core, T, topo):
     for k in range(8):
         dma("y", o("nxA", p=(16 * k, 16 * k + 16), k="nxA%d" % k), ((), T.nx[:]), "dnxA", 128)
     nxA = (tuple("nxA%d" % k for k in range(8)), T.nxA[:])
+    dma("y", o("wt", 1536, 3072, k="wt1"), ((), T.w[:, 1536:3072]), "dw1")
 
     def rows(first, *pieces):
         ks, at = (), first
@@ -353,7 +394,7 @@ def rank_program(g, core, T, topo):
     ms(o("xt", 0, 4 * ZC, k="xtz"), 0.0)
     ms(o("L1", 60, 88, k="L1z"), 0.0)
     tr(o("KT", 0, 96, k="KTa"), Ka)
-    pads("zp1")
+    ms(o("rs"), 1.0)
     Fm = o("Fm", 0, N, k=("Fm0", "Fm1"))
     selZ = o("selB", 0, 1)
 
@@ -390,17 +431,20 @@ def rank_program(g, core, T, topo):
     ts(o("Fb", 0, N), o("Fc", 0, N), cc("b2"), add)
     ts(cc("wrap"), G16, 16.0 * me, le, float(CAPP * N), mul)
     ts(cc("pr"), J, float(R_OUT - 1), le, cc("pr0"), mul)
-    ts(o("zp0", 16, 176), ind(o("nxr"), o("offe")), 2.0, mul, 1.0, add)
-    side(ts, o("selP", 0, 1), B0b, float(R_LAND + me), add, 32.0 * NB - 1, mn)
-    side(ts, o("jl"), r16, 16.0, mul, J, add)
+    halves(lambda z, a, b: ts(z, ind(o("nxr"), o("offe", a // 16, b // 16)), 2.0, mul, 1.0, add), "zp0", ((0, 96), (96, V)))
     side(ts, o("mD", 0, 32, k="mD0"), o("Kt", 0, 32, k="Kt0"), J, eq, cc("pr"), mul)
-    pads("zp2")
-    turn("zp0")
+    side(tr, o("KT", 96, 192, k="KTb"), Kb)
+    side(ts, cc("c1"), G16, CAPP / 16.0, mul, cc("wrap"), add)
+    turn("zp0", ((0, 0, 96, "pa"), (192, 16, 96, "a"), (96, 96, 96, "abr"), (288, 112, 64, "b")))
     tt(o("L1o"), ind(Tz, selZ), o("b1t"), add)
-    fan(("L1o",), lambda q: T.L1o[:, 0:10], lambda q: T.L1[:, 10 * me:10 * me + 10], "am1", "left")
+    everyone(("L1o",), T.L1o[:, 0:10], T.L1[:, 10 * me:10 * me + 10], "am1", "left")
     dma("y", o("L1", 10 * me, 10 * me + 10, k="L1m"), o("L1o", 0, 10), "dL1")
-    dma("y", o("wt"), (("left",), T.w[:]), "dw")
+    dma("y", o("wt", 0, 1536, k="wt0"), (("left",), T.w[:, 0:1536]), "dw0")
 
+    iota(o("S0", 0, 288), [[0, 288]])
+    for zp in ("zp1", "zp2"):
+        iota(o(zp, 0, 16, k=zp + "p"), [[0, 16]])
+        iota(o(zp, 176, 192, k=zp + "r"), [[0, 16]])
     iota(o("S1", 0, 272), [[0, 272]])
     iota(o("idtab", 0, 1, k="idz"), [[0, 1]], -1)
 
@@ -409,77 +453,143 @@ def rank_program(g, core, T, topo):
     for k in range(N):
         Fk(k)
     ts(o("offr"), ind(Tz, selZ), -float(TN), add, 0.5 / TN, mul)
-    side(cp, o("nxo"), nxA)
-    side(tr, o("KT", 96, 192, k="KTb"), Kb)
-    side(tr, o("KU"), (K2, T.K2[:]))
-    jobs.append((("rs",), lambda: ms(o("rs"), 1.0), 3))
-    side(ts, o("selA"), o("ramp", 0, 32), B0, add)
     side(ms, o("rs", 0, None, 16, k=("rs0",)), 0.0)
     side(ms, o("rs", R_SLOT, None, 16, k=("rs1",)), 0.0)
-    jobs.append((("S0",), lambda: ms(o("S0", 0, 288), 0.0), 3))
+    side(tr, o("KU"), (K2, T.K2[:]))
+    side(cp, o("nxo"), nxA)
+    side(ts, cc("c2"), cc("c1"), float(BA - 1 - CAPP * (me + 1) - 15 - CAPP * (R_C0 - R_SLOT)), add, oh(R_C0), mul)
     side(ts, o("selL", 0, 1), SL, 0.125, mul)
-    side(ts, o("mD", 32, 64, k="mD1"), o("ramp", 0, 32), P16, eq, cc("pr"), mul)
+
     def own_codes(buf):
         for a_, b_ in ((0, 136), (136, 268), (268, BA)):
             quant(buf, a_, b_, "xt", ("xtx", "xtz"), "%s%d" % (buf, a_))
         return (buf + "0", buf + "136", buf + "268")
     xk = own_codes("x")
+    side(ts, o("DT", 64, 65, k="DTb"), o("KU", 0, 1), -LIFT, add, cc("pr"), mul)
+    side(tt, cc("KUc"), cc("c2"), o("KU", 0, 1), add)
+    side(ts, o("selA"), o("ramp", 0, 32), B0, add)
     cp(o("G0"), ind(Fm, o("offr", 0, 10)))
+    for _ in range(3):
+        jobs.pop(0)[1]()
     act(cc("k3"), oh(R_C1), scale=ZC / K - BIG, bias=cc("k2"))
     act(o("strow"), ind(o("ramp"), o("offSt")))
     act(o("TAB", 1, 769, k="TABa"), ind(o("F", k=tuple("F%d" % k for k in range(N))), o("nxo")))
-    act(cc("c1"), G16, scale=CAPP / 16.0, bias=cc("wrap"))
-    act(o("TAB", 0, 770, 769, k="TABz"), o("ramp", 0, 2), scale=0.0, bias=oh(R_OUT))
-    act(cc("prn"), cc("pr"), scale=-LIFT)
     for b in range(2):
         act(o("capT", 1 + b, 769, 2, k="capT%d" % b), o("ramp", 0, TN), scale=cc("cs"), bias=cc("k3"))
-    act(cc("c2"), cc("c1"), bias=float(BA - 1 - CAPP * (me + 1) - 15 - CAPP * (R_C0 - R_SLOT)))
     act(o("capT", 0, 770, 769, k="capT2"), o("ramp", 0, 2), scale=0.0, bias=cc("k3"))
     act(o("Mt"), o("strow"), scale=cc("ms"), bias=cc("mb"))
+    act(o("TAB", 0, 770, 769, k="TABz"), o("ramp", 0, 2), scale=0.0, bias=oh(R_OUT))
+    offE, G1 = o("offE", 0, 10), o("G1")
+
+    def entries():
+        ts(o("offE"), ind(o("L1", k=("L1i", "L1m", "L1z")), o("selL", 0, 1)), float(-2 * TN * me), add, float(2 * TN + 1), mn)
+        act(G1, ind(o("TAB", k=("TABa", "TABz")), offE), acc=o("x1"))
 
     scan(o("cn0"), o("G0"), o("G0"), cc("base0"), add, mx)
-    tt(o("zp0", 16, 176), o("G0"), o("cn0"), mul)
+    halves(lambda z, a, b: tt(z, o("G0", a, b), o("cn0", a, b), mul), "zp0")
     turn("zp0")
     sums()
-    cp(o("off0"), ind(o("SS"), o("selB", R_OUT, R_OUT + 1)))
-    act(o("DT", 64, 65, k="DTb"), o("KU", 0, 1), scale=cc("pr"), bias=cc("prn"))
-    act(cc("KUc"), cc("c2"), scale=oh(R_C0), bias=o("KU", 0, 1))
-    act(cc("in1"), o("DT", 64, 65, k="DTb"), scale=-1.0, bias=cc("KUc"))
+    cp(o("off0"), ind(SS, o("selB", R_OUT, R_OUT + 1)))
     scatter(o("S0"), o("off0", 0, 10), o("strow"))
     turn_slots("S0", 9)
+    side(ts, o("mD", 32, 64, k="mD1"), o("ramp", 0, 32), P16, eq, cc("pr"), mul)
+    side(tt, cc("in1"), cc("KUc"), o("DT", 64, 65, k="DTb"), sub)
 
-    ts(o("offE"), ind(o("L1", k=("L1i", "L1m", "L1z")), o("selL", 0, 1)), float(-2 * TN * me), add, float(2 * TN + 1), mn)
-    offE = o("offE", 0, 10)
-    cp(o("offi", k="offi"), ind(Ts, o("selA", 16 * (me % 2), 16 * (me % 2) + 1)))
-    act(o("G1"), ind(o("TAB", k=("TABa", "TABz")), offE), acc=o("x1"))
-    tt(o("cap1"), ind(o("capT", k=("capT0", "capT1", "capT2")), offE), o("Mt"), mul)
-    ki = ("offi",)
-    for q in range(4):
-        if 32 * q != Q:
-            ki += ("offi%d" % q,)
-            op("v", lambda: g.vector.tensor_copy(T.offi[32 * q:32 * q + 32, 0:16], T.offi[Q:Q + 32, 0:16]), ("offi",), ki[-1:])
-    ts(o("D"), o("mD", k=("mD0", "mD1")), o("x1"), mul)
-    pick("sl1", "x", (ki, T.offi[:, 0:15]), xk)
-    columns(0, ("sl1",))
-    tr(o("DT", 0, 64), o("D"))
-    scan(o("cn1"), o("G1"), o("cap1"), cc("in1"), add, mn)
-    Ak = own_codes("A")
-    Bx = own_codes("B")
-    for k in range(2 * 3):
-        quant("w", 128 * k, 128 * k + 128, "wt", ("wt",), "w%d" % k)
-    red(o("tot"), o("DT", 0, 32))
-    pre = (("pre",), T.L2[:, me, 0:1])
-    red(pre, o("DT", 32, 65, k=("DT", "DTb")))
-    tt(o("zl"), o("G1"), o("cn1"), mul)
-    ts((("pre1",), T.L2[32:64, me, 0:1]), (("pre",), T.L2[32:64, me, 0:1]), o("tot", p=(0, 32)), add)
-    ts((("pre2",), T.L2[64:96, me, 0:1]), (("pre",), T.L2[64:96, me, 0:1]), o("tot", p=(0, 32)), add, o("tot", p=(32, 64)), add)
-    pre = (("pre", "pre1", "pre2"), pre[1])
-    ts(o("zp1", 16, 176), o("zl"), pre, add, 0.0, mx)
+    ki = ("offi",) + tuple("offi%d" % q for q in range(4) if 32 * q != Q)
+
+    def caps():
+        tt(o("cap1"), ind(o("capT", k=("capT0", "capT1", "capT2")), offE), o("Mt"), mul)
+
+    def spread():
+        for q in range(4):
+            if 32 * q != Q:
+                cp(o("offi", k="offi%d" % q, p=(32 * q, 32 * q + 32)), o("offi", p=PQ))
+
+    def half(k, kind):
+        a, b = ((0, 6), (6, 15))[k]
+        pick("sl1", "x", (ki, T.offi[:, a:b]), xk, part=(16 * a, 16 * b), kinds=kind)
+
+    def rest():
+        columns(0, ("sl196",), "q", (2, 3, 4))
+
+    def first():
+        for kind in OPT["o1"]:
+            if kind == "q" and OPT["early"]:
+                columns(0, ("sl1", "sl196"), "q")
+            elif kind == "q":
+                columns(0, ("sl1",), "q", (0, 1))
+            else:
+                columns(0, ("sl1", "sl196"), "s")
+    s0 = OPT["s0"]
+    if OPT["pre"]:
+        ts(o("D"), o("mD", k=("mD0", "mD1")), o("x1"), mul)
+        cp(o("offi", k="offi"), ind(Ts, o("selA", 16 * (me % 2), 16 * (me % 2) + 1)))
+        tr(o("DT", 0, 64), o("D"))
+        spread()
+        caps()
+        pre = (("pre",), T.L2[:, me, 0:1])
+        red(o("tot"), o("DT", 0, 32))
+        red(pre, o("DT", 32, 65, k=("DT", "DTb")))
+        half(0, "s")
+        half(1, "s")
+        scan(o("cn1"), G1, o("cap1"), cc("in1"), add, mn)
+        ts((("pre1",), T.L2[32:64, me, 0:1]), (("pre",), T.L2[32:64, me, 0:1]), o("tot", p=(0, 32)), add)
+        ts((("pre2",), T.L2[64:96, me, 0:1]), (("pre",), T.L2[64:96, me, 0:1]), o("tot", p=(0, 32)), add, o("tot", p=(32, 64)), add)
+        pre = (("pre", "pre1", "pre2"), pre[1])
+        tt(o("zl"), G1, o("cn1"), mul)
+        half(0, "q")
+        first()
+        ts(o("zp1", 16, 176), o("zl"), pre, add, 0.0, mx)
+        half(1, "q")
+        rest()
+        Ak = own_codes("A")
+        s0 = None
+    if s0 == 0:
+        entries()
+        while jobs:
+            jobs.pop(0)[1]()
+    if s0 is not None:
+        cp(o("offi", k="offi"), ind(Ts, o("selA", 16 * (me % 2), 16 * (me % 2) + 1)))
+    if s0 == 0:
+        caps()
+        if OPT["mvA"]:
+            move("A", "x", 0, BA, xk, "Ax", "dxA")
+            Ak = ("Ax",)
+        else:
+            Ak = own_codes("A")
+        spread()
+    if s0 == 0:
+        ts(o("D"), o("mD", k=("mD0", "mD1")), o("x1"), mul)
+        scan(o("cn1"), G1, o("cap1"), cc("in1"), add, mn)
+        half(0, "s")
+        half(1, "s")
+        tr(o("DT", 0, 64), o("D"))
+        half(0, "q")
+        first()
+        red(o("tot"), o("DT", 0, 32))
+        pre = (("pre",), T.L2[:, me, 0:1])
+        red(pre, o("DT", 32, 65, k=("DT", "DTb")))
+        tt(o("zl"), G1, o("cn1"), mul)
+        ts((("pre1",), T.L2[32:64, me, 0:1]), (("pre",), T.L2[32:64, me, 0:1]), o("tot", p=(0, 32)), add)
+        ts((("pre2",), T.L2[64:96, me, 0:1]), (("pre",), T.L2[64:96, me, 0:1]), o("tot", p=(0, 32)), add, o("tot", p=(32, 64)), add)
+        pre = (("pre", "pre1", "pre2"), pre[1])
+        if not OPT["late"]:
+            half(1, "q")
+            rest()
+        halves(lambda z, a, b: ts(z, o("zl", a, b), pre, add, 0.0, mx), "zp1")
+        if OPT["late"]:
+            half(1, "q")
+            rest()
+    side(ts, o("selP", 0, 1), B0b, float(R_LAND + me), add, 32.0 * NB - 1, mn)
+    side(ts, o("jl"), r16, 16.0, mul, J, add)
+    Bx = () if OPT["mvB"] else own_codes("B")
+    for k in (4, 5, 3, 0, 1, 2):
+        quant("w", 128 * k, 128 * k + 128, "wt", ("wt%d" % (k // 3),), "w%d" % k)
     turn("zp1")
     sums()
-    cp((("L2o",), T.L2[:, me, 1:17]), ind(o("SS"), o("selB", R_SLOT - 1, R_SLOT)))
-    cp(o("off1"), ind(o("SS"), o("selB", R_OUT, R_OUT + 1)))
-    fan(("L2o",) + pre[0], lambda q: T.L2[:, me, 0:11], lambda q: T.L2[:, me, 0:11], "am2")
+    cp((("L2o",), T.L2[:, me, 1:17]), ind(SS, o("selB", R_SLOT - 1, R_SLOT)))
+    cp(o("off1"), ind(SS, o("selB", R_OUT, R_OUT + 1)))
+    everyone(("L2o",) + pre[0], T.L2[:, me, 0:11], T.L2[:, me, 0:11], "am2")
     iota(o("idtab", 1, 961, k="idn"), [[0, N], [1, V]])
     act(cc("o34"), oh(R_C0), bias=oh(R_C1))
     act(cc("z1"), oh(R_LAND + me), bias=oh(R_ID))
@@ -506,63 +616,88 @@ def rank_program(g, core, T, topo):
             fill(o("ztab", a_, a_ + n_, k=zk[-1]), n_, oh(R_ID))
             a_ += n_
     fill(o("S2", V, V + 288), 288)
-    act(o("E"), o("zp1", 16, 176), scale=cc("es"), bias=cc("e2"))
+    act(o("E"), row("zp1"), scale=cc("es"), bias=cc("e2"))
 
-    scatter(o("S1"), o("off1", 0, 10), o("zp1", 16, 176))
+    def product(k, oo, bank, n, keys, cols, first, last):
+        a, wk = 128 * (k * NO + oo), "w%d" % (k * NO + oo)
+        op("k", lambda: g.tensor.matmul_mx(T[bank][:, 0:cols], T.wq[:, a:a + 128], T.ws[:, a:a + 128], T[n + "q"][:], T[n + "s"][:], first, last),
+           (wk + "q", wk + "s") + tuple(x + c for x in keys for c in "qs"), (bank,) if last else ())
+
+    scatter(o("S1"), o("off1", 0, 10), row("zp1"))
     turn_slots("S1", 8)
-    k2 = gather_lists("off2", R_C0, 2)
-    move("B", "A", BA, BL, ("Al",), "Ba", "dAB")
+    k2 = gather_lists("off2")
+    PARTS = ((0, 1), (2, 3), (4,))
+    sl2k = ("sl2", "sl2192", "sl2384")
+    steps = [0]
 
     def third(k, kind):
-        pick("sl2", "A", (k2, T.off2[:, 10 * k:10 * k + 10]), ("Al",) + Ak, part=(V * k, V * k + V), kinds=kind)
+        a, b = 6 * PARTS[k][0], 6 * PARTS[k][-1] + 6
+        pick("sl2", "A", (k2, T.off2[:, a:b]), ("Al",) + Ak, part=(16 * a, 16 * b), kinds=kind)
+
+    def step():
+        k = steps[0] - OPT["at"]
+        steps[0] += 1
+        if 0 <= k < 3:
+            third(k, "q")
+            columns(1, sl2k[0:k + 1], "q", PARTS[k] if OPT["split"] else range(N) if k == 2 else ())
+        if k == OPT["sat"]:
+            columns(1, sl2k, "s")
+    for k in range(3):
+        third(k, "s")
+    move("B", "A", 0 if OPT["mvB"] else BA, BL, ("Al",) + Ak, "Ba", "dAB")
     L2k = ("L2i", "L2o") + pre[0]
-    third(0, "q")
-    tt((("L2h",), T.L2h[:]), (L2k, T.L2[:, 0:3, 0:11]), (L2k, T.L2[:, 3:6, 0:11]), add)
-    third(1, "q")
+    step()
+    tt((("L2h",), T.L2h[:]), (L2k + k2, T.L2[:, 0:3, 0:11]), (L2k, T.L2[:, 3:6, 0:11]), add)
+    step()
     tt(o("L2a"), (("L2h",), T.L2h[:, 0, :]), (("L2h",), T.L2h[:, 1, :]), add)
-    third(2, "q")
+    step()
     tt(o("vi", 0, 11), o("L2a"), (("L2h",), T.L2h[:, 2, :]), add)
+    step()
     if low:
         ts(o("offN"), o("vi", 1, 11), 1.0 / K, mul, float(at + TN), mn)
     else:
         ts(o("offN"), o("vi", 1, 11), 1.0 / K, mul, float(-TN * me), add)
     ts(o("sli"), o("vi", 1, 11), int(K) - 1, band)
-    act(o("G2"), ind(o("ztab", k=zk), o("offN")))
-    for k in range(3):
-        third(k, "s")
-    columns(1, ("sl2", "sl2160", "sl2320"))
-    iota(o("idtab", 1, 961, k="idn", p=(0, 1)), [[1, N], [0, V]])
     ts(o("in2"), o("vi", 0, 1), oh(R_LAND + me), mul, cc("i3"), add)
+    iota(o("idtab", 1, 961, k="idn", p=(0, 1)), [[1, N], [0, V]])
+    cp(o("G2"), ind(o("ztab", k=zk), o("offN")))
     cp(o("offS"), o("sli"))
     scan(o("cn2"), o("G2"), o("E"), o("in2"), add, mn)
-    tt(o("zp2", 16, 176), o("G2"), o("cn2"), mul)
+    halves(lambda z, a, b: tt(z, o("G2", a, b), o("cn2", a, b), mul), "zp2")
     turn("zp2")
-    tt(o("cap2"), ind(o("ptab", k=("pt0", "pt1")), o("offS")), o("zp2", 16, 176), mx)
+    tt(o("cap2"), ind(o("ptab", k=("pt0", "pt1")), o("offS")), row("zp2"), mx)
     tt(o("off20"), ind(Tz, o("selP", 0, 1)), o("jl"), mx)
     scatter(o("S2"), o("off20", 0, 10), o("cap2"))
+    for oo in range(NO):
+        product(2, oo, "ps_%d" % (2 + oo), "x", xk, BA, True, True)
+        act(o("R2%d" % oo), o("ps_%d" % (2 + oo), 0, BA))
     turn_slots("S2", 9, V)
-    kF = gather_lists("offF", R_ID, 4)
-    off = [(kF, T.offF[:, 16 * k:16 * k + 16]) for k in range(4)]
-
-    def product(k, last):
-        n = "p%d" % k
-        for oo in range(NO):
-            a = 128 * (k * NO + oo)
-            wk = "w%d" % (k * NO + oo)
-            op("k", lambda: g.tensor.matmul_mx(T["ps_%d" % oo][:, 0:M], T.wq[:, a:a + 128], T.ws[:, a:a + 128], T[n + "q"][:], T[n + "s"][:], k == 2, last),
-               (wk + "q", wk + "s", n + "q", n + "s"), ("ps_%d" % oo,) if last else ())
-    pick("p2", "B", off[1], Bx, BA)
-    product(2, False)
+    for n, row in enumerate((R_C0, R_ID)):
+        cp(o("Ha", 32 * n, 32 * n + 32, k="Ha%d" % n), ind(Ts, o("selA", row, row + 2)))
+    for n, row in enumerate((R_C0, R_ID)):
+        tt(o("Hb", 32 * n, 32 * n + 32, k="Hb%d" % n), ind(Ts, o("selA", 16 + row, 18 + row)), o("Ha", 32 * n, 32 * n + 32, k="Ha%d" % n), add)
+    for n in range(2):
+        tt(o("tq", 32 * n, 32 * n + 32, k="tq%d" % n, p=(0, 64)), o("Hb", 32 * n, 32 * n + 32, k="Hb%d" % n, p=(0, 64)),
+           o("Hb", 32 * n, 32 * n + 32, k="Hb%d" % n, p=(64, 128)), add)
+    for h in range(4):
+        tt(o("offF", 0, 32, k="offF%d" % h, p=(32 * h, 32 * h + 32)), o("tq", 0, 32, k="tq0", p=(0, 32)), o("tq", 0, 32, k="tq0", p=(32, 64)), add)
+    tt(o("offF", 32, 64, k="offG0", p=(0, 32)), o("tq", 32, 64, k="tq1", p=(0, 32)), o("tq", 32, 64, k="tq1", p=(32, 64)), add)
+    kF, kG = tuple("offF%d" % h for h in range(4)) + ("offG0",), tuple("offG%d" % h for h in range(4))
     Bk = Bx + ("Ba", "Bl")
-    pick("p0", "B", off[2], Bk)
-    product(0, False)
-    pick("p1", "B", off[3], Bk)
-    product(1, True)
-    act(o("idt"), ind(o("idtab", k=("idz", "idn")), off[0]))
-    cp(o("yo0"), o("ps_0", 0, M))
-    act(o("yo1"), o("ps_1", 0, M))
-    dma("y", (("y0",), T.y[:, 0:M]), o("yo0"), "dy0")
-    dma("s", (("y1",), T.y[:, M:2 * M]), o("yo1"), "dy1")
+    pick("p0", "B", (kF, T.offF[:, 0:16]), Bk)
+    for oo in range(NO):
+        product(0, oo, "ps_%d" % oo, "p0", ("p0",), M, True, False)
+    for h in range(1, 4):
+        cp(o("offF", 32, 64, k="offG%d" % h, p=(32 * h, 32 * h + 32)), o("offF", 32, 64, k="offG0", p=(0, 32)))
+    pick("p1", "B", (kF, T.offF[:, 16:32]), Bk)
+    for oo in range(NO):
+        product(1, oo, "ps_%d" % oo, "p1", ("p1",), M, False, True)
+    cp(o("r20"), ind(o("R20"), (kG, T.offF[:, 48:64])))
+    act(o("r21"), ind(o("R21"), (kG, T.offF[:, 48:64])))
+    act(o("idt"), ind(o("idtab", k=("idz", "idn")), (kG, T.offF[:, 32:48])))
+    for oo in range(NO):
+        tt(o("yo%d" % oo), o("ps_%d" % oo, 0, M), o("r2%d" % oo), add)
+        dma("ys"[oo], (("y%d" % oo,), T.y[:, M * oo:M * oo + M]), o("yo%d" % oo), "dy%d" % oo)
     op("y", lambda: g.sync.dma_start(T["id"][:], T.idt[0:2, :]), ("idt",), ("ido",), sem="did", inc=16)
     for sem, c in count.items():
         if know["p"].get(sem, 0) < c:

from concourse.bass import DstId, RemoteDMATransfer
from concourse.mybir import dt, AluOpType, AxisListType, ActivationFunctionType

N, TN, V, M, CAPP, NO = 6, 384, 160, 256, 48, 2
REM = CAPP * (N - 1)
ZC = 16
BA = ZC + TN
BL = BA + REM
BW = BL + 2 * REM
K = 2048.0
LIFT = 4096.0
BIG = 8192.0
R_N2, R_LAND, R_SLOT, R_OUT, R_C0, R_C1 = 0, 1, 7, 12, 14, 15
R_ELSE, R_ID, R_C2 = 0, 12, 13
NB = 11

_F, _I, _U, _C, _S = "float32", "int32", "uint16", "float8_e4m3fn_x4", "uint8"
SCRATCH, POOL = {}, {}


def _add(dtype, **shapes):
    for name, shape in shapes.items():
        SCRATCH[name] = ("sbuf", [128] + (list(shape) if isinstance(shape, tuple) else [shape]), dtype)


def _pool(buf, dtype, **widths):
    at = 0
    for name, w in widths.items():
        POOL[name] = (buf, at, w)
        at += w
    _add(dtype, **{buf: at})


_add(_I, st0=10, bt0=10, b1t=16, nxr=768, nxA=48, r1i=16, vi=12, sli=10)
_add(_F, cc=48, oh=16, ramp=480, Kt=192, KT=192, K2=(2, 16), KU=32, tq1=(5, 2, 3), Fm=8, Fb=8, Fc=8, Ft=16, F=2304, TAB=776, capT=776,
     ztab=1160, ptab=736, rs=96, mD=64, D=64, DT=72, idtab=968, idt=M, yo0=M, yo1=M)
_add(_F, zp0=192, zp1=192, zp2=192, Tz=32 * NB, SS=32 * NB, Ts=544, S0=416, S1=416, S2=448,
     G0=V, G1=V, G2=V, cn0=V, cn1=V, cn2=V, strow=V, Mt=V, cap1=V, E=V, cap2=V, zl=V,
     L1o=16, L1=88, L2=(6, 20), L2h=(3, 11), Ha=64, Hb=64, tq=64)
_add(_U, selA=32, selB=16, selP=2, selL=2, same=16, offr=16, off0=16, offi=16, nxo=48, offE=16, off1=16, off2=32,
     offN=10, offS=10, off20=16, offF=64)
_pool("poolu", _U, offe=10, offSt=10)
_pool("pooli", _I, ia=10, ib=10)
_pool("poolf", _F, e1=10, e2=10, e3=10, e4=10, e5=10, x1=1, tot=1, L2a=11, in2=1, jl=16, pb=16)
_add("bfloat16", xt=4 * BA, wt=3072)
for _n, _w in (("x", BA), ("w", 768), ("sl1", REM), ("A", BL), ("sl2", 2 * REM), ("B", BW), ("p0", M), ("p1", M)):
    SCRATCH[_n + "q"] = ("sbuf", [128, _w], _C)
    SCRATCH[_n + "s"] = ("sbuf", [128, _w], _S)
_add(_S, hsl1s=REM, hsl2s=2 * REM)
_add(_C, hsl1q=REM, hsl2q=2 * REM)
_add(_F, R20=BA, R21=BA, r20=M, r21=M)
for _n in range(4):
    SCRATCH["ps_%d" % _n] = ("psum", [128, 512], _F)

SEMAPHORES = ["qv", "qs", "qp", "qk", "dst0", "dbt0", "dnx", "dnxA", "dx", "dw0", "dw1", "left", "dxA", "dAB", "dL1",
              "did", "dy0", "dy1", "am1", "Aq", "As", "am2", "am3", "Bq", "Bs", "hsl1q", "hsl1s", "hsl2q", "hsl2s", "loc"]

add, sub, mul, mx, mn = AluOpType.add, AluOpType.subtract, AluOpType.mult, AluOpType.max, AluOpType.min
eq, ge, gt, le = AluOpType.is_equal, AluOpType.is_ge, AluOpType.is_gt, AluOpType.is_le
shr, band = AluOpType.arith_shift_right, AluOpType.bitwise_and
Copy, Ident = ActivationFunctionType.Copy, ActivationFunctionType.Identity


STAGES = (("sl1", "A", BA, CAPP), ("sl2", "B", BL, 2 * CAPP))


OPT = dict(s0=0, pre=0, late=0, mvA=1, mvB=0, o1="qs", one=1, early=0, at=0, split=1, sat=2)
WAYS = {(0, "q"): (((0, 1), None), ((2, 3, 4), None)), (0, "s"): (((0, 1, 2, 3, 4), 0),),
        (1, "q"): (((0, 1), None), ((2, 3), None), ((4,), None)), (1, "s"): (((0, 1, 2, 3, 4), None),)}


def calls(places):
    k = 4 if len(places) > 3 else 2 if len(places) > 1 else 1
    return [places[:k]] + (calls(places[k:]) if places[k:] else [])


def raw(ap, kind):
    return ap.bitcast(dt.uint8) if kind == "q" else ap


def pos(a, q):
    return (q - a - 1) % N


def pieces(T, me, name, stage, kind):
    _, land, at, w = STAGES[stage]
    return ((lambda q: raw(T[name + kind][:, w * pos(me, q):w * pos(me, q) + w], kind)),
            (lambda q: raw(T[land + kind][:, at + w * pos(q, me):at + w * pos(q, me) + w], kind)))


def neighbours(T, topo, r):
    c = T.cores[r]
    able = [h for h in topo.cores_of(c) if h != c and all(topo.may_write(h, d) for d in T.cores if d != c)]
    return sorted(able, key=lambda h: topo.die(h) != topo.die(c))


def inner(T, topo, r):
    c = T.cores[r]
    return [e for e in topo.engines(c, neighbours(T, topo, r)[0]) if e not in topo.engines(c, T.cores[(r + 1) % N])]


def send(g, core, me, T, topo, places, src, dst, rsem, lsem):
    trs = []
    for k, d in enumerate(places):
        q = (me + 1 + d) % N
        c = T.cores[q]
        rid, pid, _ = topo.addr(c)
        m = sum(1 << e for e in topo.engines(core, c)[k::len(places)])
        trs.append(RemoteDMATransfer(dst_ids=[DstId(rid=rid, pnc=pid)], dma_engine_mask=m, remote_sem=T.sem[rsem], src=src(q), dst=dst(q)))
    g.remote_dma_fused(trs, local_sem=T.sem[lsem])


def send_five(g, core, me, T, topo, src, dst, rsem, lsem):
    for places in ((0, 1, 2, 3), (4,)):
        send(g, core, me, T, topo, places, src, dst, rsem, lsem)


def hand_on(g, core, r, T, topo):
    left = 0
    for (stage, kind), ways in sorted(WAYS.items()):
        name, land = "h" + STAGES[stage][0], STAGES[stage][1]
        for places, via in ways:
            if via is not None and neighbours(T, topo, r)[via] == core:
                g.wait_ge(T.sem[name + kind], len(inner(T, topo, r)))
                for part in calls(places):
                    send(g, core, r, T, topo, part, *pieces(T, r, name, stage, kind), land + kind, "loc")
                    left += len(topo.engines(core, T.cores[(r + 1) % N]))
    if left:
        g.wait_ge(T.sem.loc, left)


def rank_program(g, core, T, topo):
    me = T.rank_of(core)
    if me is None:
        for r in range(N):
            if core in neighbours(T, topo, r):
                hand_on(g, core, r, T, topo)
        return
    others = [(me + 1 + k) % N for k in range(N - 1)]

    eng = {"v": g.vector, "s": g.scalar, "p": g, "k": g.tensor, "y": g.sync}
    know = {q: {} for q in eng}
    count, wr, rd, jobs, room = {"loc": 0}, {}, {}, [], []
    across = set()

    def side(f, out, *args):
        jobs.append((out[0], lambda: f(out, *args), 1))

    def need(q, evs):
        for sem, val, snap in sorted(evs, key=lambda e: -len(e[2])):
            if know[q].get(sem, 0) < val:
                eng[q].wait_ge(T.sem[sem], val)
                for a, b in list(snap.items()) + [(sem, val)]:
                    if know[q].get(a, 0) < b:
                        know[q][a] = b

    def op(q, call, reads=(), writes=(), sem="", inc=1, total=None):
        while any(k in job[0] for job in jobs for k in tuple(reads) + tuple(writes)):
            jobs.pop(0)[1]()
        evs = []
        for k in reads:
            evs += wr.get(k, [])
        for k in writes:
            evs += wr.get(k, []) + rd.get(k, [])
        if q == "v" and jobs and not room and count["qv"] not in across and any(e[0] == "qv" and e[1] == count["qv"] for e in evs):
            room.append(3)
            while jobs and jobs[0][2] <= room[0]:
                room[0] -= jobs[0][2]
                jobs.pop(0)[1]()
            room.pop()
        best = {}
        for e in evs:
            if e[0] not in best or best[e[0]][1] < e[1]:
                best[e[0]] = e
        need(q, list(best.values()))
        ins = call()
        if sem is None:
            return
        sem = sem or "q" + q
        ins.then_inc(T.sem[sem], inc)
        count[sem] = count.get(sem, 0) + inc
        ev = (sem, total or count[sem], dict(know[q]))
        for k in writes:
            wr[k] = [ev]
            rd[k] = []
        for k in reads:
            rd.setdefault(k, []).append(ev)

    def o(name, lo=None, hi=None, st=None, k=None, p=None):
        ps = slice(None) if p is None else slice(p[0], p[1])
        keys = (k,) if isinstance(k, str) else k or (name,)
        if name in POOL:
            name, at, w = POOL[name]
            lo, hi = at + (lo or 0), at + (w if hi is None else hi)
        return (keys, T[name][ps, slice(lo, hi, st)])

    def blk(name, lo, hi, st, k):
        return ((k,) if isinstance(k, str) else k, T[name][:, lo:hi:st, :])

    names = {}

    def cc(n):
        j = names.setdefault(n, len(names))
        return o("cc", j, j + 1, k="cc" + n)

    def oh(j):
        return o("oh", j, j + 1)

    def ind(win, off):
        return (win[0] + off[0], win[1].indirect(off[1]))

    def cp(out, in_):
        op("v", lambda: g.vector.tensor_copy(out[1], in_[1]), in_[0], out[0])

    def ms(out, c):
        op("v", lambda: g.vector.memset(out[1], c), ("rs",) if out[0][0] in ("rs0", "rs1") else (), out[0])

    def tt(out, a, b, f):
        op("v", lambda: g.vector.tensor_tensor(out[1], a[1], b[1], f), a[0] + b[0], out[0])

    def ts(out, a, s1, f1, s2=None, f2=None):
        rk = a[0] + (s1[0] if isinstance(s1, tuple) else ()) + (s2[0] if isinstance(s2, tuple) else ())
        v1 = s1[1] if isinstance(s1, tuple) else s1
        v2 = s2[1] if isinstance(s2, tuple) else s2
        if f2 is None:
            op("v", lambda: g.vector.tensor_scalar(out[1], a[1], v1, None, f1), rk, out[0])
        else:
            op("v", lambda: g.vector.tensor_scalar(out[1], a[1], v1, v2, f1, f2), rk, out[0])

    def scan(out, d0, d1, init, f0, f1):
        ik, iv = init if isinstance(init, tuple) else ((), init)
        op("v", lambda: g.vector.tensor_tensor_scan(out[1], d0[1], d1[1], iv, f0, f1), d0[0] + d1[0] + ik, out[0])

    def red(out, in_):
        op("v", lambda: g.vector.tensor_reduce(out[1], in_[1], AxisListType.X, add), in_[0], out[0])

    def tr(out, in_):
        op("v", lambda: g.vector.transpose(out[1], in_[1]), in_[0], out[0])

    def act(out, in_, scale=None, bias=None, acc=None):
        kw, rk, wk = {}, (), out[0]
        for n, v in (("scale", scale), ("bias", bias)):
            if isinstance(v, tuple):
                rk, v = rk + v[0], v[1]
            if v is not None:
                kw[n] = v
        if acc:
            kw["accum_out"], wk = acc[1], wk + acc[0]
        op("s", lambda: g.scalar.activation(out[1], in_[1], Copy if bias is None else Ident, **kw), in_[0] + rk, wk)

    def fill(out, n, v=0.0):
        act(out, o("ramp", 0, n), scale=0.0, bias=v)

    def iota(out, pattern, base=0, mult=0):
        op("p", lambda: g.iota(out[1], pattern, base, mult, allow_small_or_imprecise_dtypes=True), (), out[0])

    def scatter(win, off, in_):
        op("v", lambda: g.vector.tensor_copy(win[1].indirect(off[1]), in_[1]), win[0] + off[0] + in_[0], win[0])

    def pick(outn, winn, off, wkeys, hi=None, part=(0, None), kinds="qs"):
        a, b = part
        key = outn + ("%d" % a if a else "")
        if "q" in kinds:
            op("v", lambda: g.vector.tensor_copy(T[outn + "q"][:, a:b].bitcast(dt.uint32), T[winn + "q"][:, 0:hi].bitcast(dt.uint32).indirect(off[1])),
               tuple(x + "q" for x in wkeys) + off[0], (key + "q",))
        if "s" in kinds:
            op("s", lambda: g.scalar.activation(T[outn + "s"][:, a:b], T[winn + "s"][:, 0:hi].indirect(off[1]), Copy),
               tuple(x + "s" for x in wkeys) + off[0], (key + "s",))

    def quant(outn, lo, hi, src, skeys, key):
        ks = (key + "q", key + "s")
        jobs.append((ks, lambda: op("v", lambda: g.vector.quantize_mx(T[outn + "q"][:, lo:hi], T[outn + "s"][:, lo:hi], T[src][:, 4 * lo:4 * hi]), skeys, ks), 3))

    def move(outn, srcn, lo, hi, rkeys, key, sem, behind=()):
        op("y", lambda: g.sync.dma_start(T[outn + "q"][:, lo:hi].bitcast(dt.uint8), T[srcn + "q"][:, lo:hi].bitcast(dt.uint8)),
           tuple(k + "q" for k in rkeys) + behind, (key + "q",), sem=sem, inc=16, total=32)
        op("y", lambda: g.sync.dma_start(T[outn + "s"][:, lo:hi], T[srcn + "s"][:, lo:hi]), tuple(k + "s" for k in rkeys), (key + "s",), sem=sem, inc=16, total=32)

    def everyone(reads, src, dst, rsem, lsem="loc"):
        if OPT["one"]:
            ids = [DstId(rid=topo.addr(T.cores[q])[0], pnc=topo.addr(T.cores[q])[1]) for q in others]
            tf = RemoteDMATransfer(dst_ids=ids, dma_engine_mask=topo.mask(core, T.cores[others[0]]), remote_sem=T.sem[rsem], srcs=[src], dsts=[dst] * len(ids))
            op("p", lambda: g.remote_dma_fused([tf], local_sem=T.sem[lsem]), reads, (), sem=None)
        else:
            op("p", lambda: send_five(g, core, me, T, topo, lambda q: src, lambda q: dst, rsem, lsem), reads, (), sem=None)
        count[lsem] = count.get(lsem, 0) + (8 if OPT["one"] else 16)
        wr[lsem] = [(lsem, count[lsem], {})]

    def columns(stage, keys, kind, which=None):
        name, land, at, w = STAGES[stage]
        reads = tuple(k + kind for k in keys)
        for places, via in WAYS[stage, kind]:
            if which is not None and places[0] not in which:
                continue
            if via is None:
                for part in calls(places):
                    op("p", lambda: send(g, core, me, T, topo, part, *pieces(T, me, name, stage, kind), land + kind, "loc"), reads, (), sem=None)
                    count["loc"] += 8
            else:
                rid, pid, _ = topo.addr(neighbours(T, topo, me)[via])
                a, b = w * places[0], w * places[-1] + w
                op("p", lambda: g.remote_dma(raw(T["h" + name + kind][:, a:b], kind), raw(T[name + kind][:, a:b], kind), T.sem["h" + name + kind], T.sem.loc,
                                             pid, rid, sum(1 << e for e in inner(T, topo, me))), reads, (), sem=None)
                count["loc"] += len(inner(T, topo, me))

    for s_, k in (("am1", "L1i"), ("am2", "L2i")):
        count[s_] = 40 if OPT["one"] else 16
        wr[k] = [(s_, count[s_], {})]
    for (stage, kind), ways in WAYS.items():
        land = STAGES[stage][1]
        count[land + kind] = 8 * sum(len(calls(places)) for places, _ in ways)
        wr[land + "l" + kind] = [(land + kind, count[land + kind], {})]

    def dma(q, out, in_, sem, total=None):
        op(q, lambda: eng[q].dma_start(out[1], in_[1]), in_[0], out[0], sem=sem, inc=16, total=total)

    Tz = (("Tz0", "Tz1", "Tz2", "Tz3"), T.Tz[:])
    Ts = (("Tse", "Tso"), T.Ts[:])
    HALF = ((0, 80), (80, V))
    TURNS = ((0, 0, 96, "pa"), (192, 16, 64, "a"), (96, 96, 96, "br"), (256, 80, 96, "ab"))

    def halves(f, zp, cuts=HALF):
        for h, (a, b) in enumerate(cuts):
            f(o(zp, 16 + a, 16 + b, k=zp + "ab"[h]), a, b)

    def row(zp):
        return o(zp, 16, 176, k=(zp + "a", zp + "b"))

    def turn(zp, parts=TURNS):
        for k, (to, at, n, ks) in enumerate(parts):
            tr(o("Tz", to, to + n, k="Tz%d" % k), o(zp, at, at + n, k=tuple(zp + c for c in ks)))

    def turn_slots(win, even, at=0):
        tr(o("Ts", 256, 256 + 32 * even, k="Tse"), o(win, at, at + 32 * even))
        tr(o("Ts", 0, 256, k="Tso"), o(win, at + 16, at + 272))

    def pads(zp):
        side(ms, o(zp, 0, 16, k=zp + "p"), 0.0)
        side(ms, o(zp, 176, 192, k=zp + "r"), 0.0)

    def sums():
        for k, (to, _, n, _) in enumerate(TURNS):
            scan(o("SS", to, to + n, k="SS%d" % k), o("rs", 0, n, k=("rs", "rs0", "rs1")), o("Tz", to, to + n, k="Tz%d" % k), 0.0, mul, add)
    SS = o("SS", k=("SS0", "SS1", "SS2", "SS3"))

    def gather_lists(off):
        cp(o("Ha", 0, 32, k="Ha0"), ind(Ts, o("selA", R_C0, R_C0 + 2)))
        tt(o("Hb", 0, 32, k="Hb0"), ind(Ts, o("selA", 16 + R_C0, 18 + R_C0)), o("Ha", 0, 32, k="Ha0"), add)
        for k in range(2):
            tt((("tp%d" % k,), T.tq1[0:64, :, k, :]), o("Hb", 16 * k, 16 * k + 15, k="Hb0", p=(0, 64)), o("Hb", 16 * k, 16 * k + 15, k="Hb0", p=(64, 128)), add)
        tq = [(("tp0", "tp1"), T.tq1[32 * h:32 * h + 32]) for h in range(2)]
        across.update((count["qv"], count["qv"] + 4))
        for h in range(4):
            tt(o(off, 0, 30, k=off + "%d" % h, p=(32 * h, 32 * h + 32)), tq[0], tq[1], add)
        return tuple(off + "%d" % h for h in range(4))

    Q = 32 * (me // 2)
    PQ = (Q, Q + 32)
    ms(o("nxr"), 0)
    for h in range(2):
        dma("y", o("st0", p=(Q + 16 * h, Q + 16 * h + 16), k="st%d" % h), ((), T.st[:]), "dst0", 32)
        dma("s", o("bt0", p=(Q + 16 * h, Q + 16 * h + 16), k="bt%d" % h), ((), T.bt[:]), "dbt0", 32)
    st = o("st0", p=PQ, k=("st0", "st1"))
    bt = o("bt0", p=PQ, k=("bt0", "bt1"))
    dma("y", o("nxr", p=(16 * me, 16 * me + 1)), ((), T.nx[:]), "dnx")
    dma("y", o("xt", 4 * ZC, 4 * BA, k="xtx"), ((), T.x[:]), "dx")
    for k in range(8):
        dma("y", o("nxA", p=(16 * k, 16 * k + 16), k="nxA%d" % k), ((), T.nx[:]), "dnxA", 128)
    nxA = (tuple("nxA%d" % k for k in range(8)), T.nxA[:])
    dma("y", o("wt", 1536, 3072, k="wt1"), ((), T.w[:, 1536:3072]), "dw1")

    def rows(first, *pieces):
        ks, at = (), first
        for pat, base, mult in pieces:
            n = pat[0][1] * pat[1][1]
            ks += ("Kt%d" % at,)
            iota(o("Kt", at, at + n, k=ks[-1]), pat, base, mult)
            at += n
        return o("Kt", first, at, k=ks)
    Ka = rows(0, ([[0, 2], [1, 16]], 0, 0), ([[16, 2], [0, 16]], 0, 1), ([[32, 8], [-160, 2]], 192, 0), ([[32, 8], [192, 2]], 16, 0))
    iota(o("ramp"), [[1, 480]])
    Kb = rows(96, ([[32, 8], [288, 2]], 0, 0), ([[32, 8], [-256, 2]], 256, 0), ([[80, 2], [8, 16]], 0, 5), ([[16, 2], [1, 16]], 16, 0))
    K2 = ()
    for a_, b_, s_, v_ in ((0, R_LAND + me, -96, 96 * me - 1), (R_LAND + me, R_SLOT, -96, 96 * (N - 1) - 1), (R_SLOT, 16, CAPP, 15)):
        K2 += ("K2%d" % a_,)
        iota((K2[-1:], T.K2[:, :, a_:b_]), [[0, 2], [s_, b_ - a_]], v_)
    J, G16, B0b = (o("KT", 32 * b, 32 * b + 1, k="KTa") for b in range(3))
    B0, SL, P16 = (o("KT", 32 * b, 32 * b + 1, k="KTb") for b in range(3, 6))
    r16 = o("Kt", 0, 16, k="Kt0")
    ms(o("poolu", k=("offe", "offSt")), 0)
    ms(o("b1t"), 0)
    ms(o("zp0", 0, 16, k="zp0p"), 0.0)
    ms(o("zp0", 176, 192, k="zp0r"), 0.0)
    ms(o("xt", 0, 4 * ZC, k="xtz"), 0.0)
    ms(o("L1", 60, 88, k="L1z"), 0.0)
    tr(o("KT", 0, 96, k="KTa"), Ka)
    ms(o("rs"), 1.0)
    Fm = o("Fm", 0, N, k=("Fm0", "Fm1"))
    selZ = o("selB", 0, 1)

    act(o("Ft", 8, 8 + N, k="Fa"), o("Kt", 0, N, k="Kt0"), scale=K * TN, bias=K)
    ts(o("oh"), r16, J, eq)
    ts(cc("GM"), G16, 16.0 * me, eq)
    ts(o("ia", p=PQ), st, 3, shr)
    ts(o("ib", p=PQ), bt, 1, band)
    ts(o("e1", p=PQ), st, 96.0, mul)
    act(o("Ft", 0, N), o("Ft", 8, 8 + N, k="Fa"), scale=oh(R_N2))
    act(cc("b0"), oh(R_C1), scale=K)
    act(cc("b1"), cc("GM"), scale=K - 1, bias=1.0)
    act(cc("FS"), oh(R_N2), scale=K)
    act(cc("base0"), J, scale=float(CAPP), bias=float(15 - CAPP * R_SLOT))
    act(cc("b2"), cc("b1"), scale=oh(R_C0), bias=cc("b0"))
    act(cc("own"), cc("GM"), scale=oh(R_C0))
    act(cc("k1"), oh(R_N2), scale=1.0 - BIG, bias=BIG)
    act(cc("cs"), oh(R_C1), scale=1.0 / K)
    act(cc("k2"), cc("own"), scale=1.0 - BIG, bias=cc("k1"))
    act(cc("ms"), cc("own"), scale=1.0 / K)
    act(cc("mb"), cc("own"), scale=-1.0, bias=1.0)
    if me < N - 1:
        tt(o("Fm", me + 1, N, k="Fm1"), o("oh", R_LAND + me + 1, R_LAND + N), o("oh", R_SLOT, R_OUT - me), add)
    tt(o("Fm", 0, me + 1, k="Fm0"), o("oh", R_LAND, R_LAND + me + 1), o("oh", R_OUT - me, R_OUT + 1), add)
    ts(o("e2", p=PQ), o("ia", p=PQ), -767.0, mul)
    ts(o("e3", p=PQ), o("ib", p=PQ), 48.0, mul)
    ts(o("b1t", 0, 10, p=PQ), bt, 1, shr)
    ts(o("selB"), r16, B0b, add, 32.0 * NB - 1, mn)
    tt(o("e4", p=PQ), o("e1", p=PQ), o("e2", p=PQ), add)
    tt(o("Fc", 0, N), Fm, o("Ft", 0, N), add)
    ts(o("offSt", p=PQ), st, float(ZC), add)
    ts(cc("pr0"), J, float(R_LAND), ge)
    tt(o("offe", p=PQ), o("e4", p=PQ), o("e3", p=PQ), add)
    ts(o("Fb", 0, N), o("Fc", 0, N), cc("b2"), add)
    ts(cc("wrap"), G16, 16.0 * me, le, float(CAPP * N), mul)
    ts(cc("pr"), J, float(R_OUT - 1), le, cc("pr0"), mul)
    halves(lambda z, a, b: ts(z, ind(o("nxr"), o("offe", a // 16, b // 16)), 2.0, mul, 1.0, add), "zp0", ((0, 96), (96, V)))
    side(ts, o("mD", 0, 32, k="mD0"), o("Kt", 0, 32, k="Kt0"), J, eq, cc("pr"), mul)
    side(tr, o("KT", 96, 192, k="KTb"), Kb)
    side(ts, cc("c1"), G16, CAPP / 16.0, mul, cc("wrap"), add)
    turn("zp0", ((0, 0, 96, "pa"), (192, 16, 96, "a"), (96, 96, 96, "abr"), (288, 112, 64, "b")))
    tt(o("L1o"), ind(Tz, selZ), o("b1t"), add)
    everyone(("L1o",), T.L1o[:, 0:10], T.L1[:, 10 * me:10 * me + 10], "am1", "left")
    dma("y", o("L1", 10 * me, 10 * me + 10, k="L1m"), o("L1o", 0, 10), "dL1")
    dma("y", o("wt", 0, 1536, k="wt0"), (("left",), T.w[:, 0:1536]), "dw0")

    iota(o("S0", 0, 288), [[0, 288]])
    for zp in ("zp1", "zp2"):
        iota(o(zp, 0, 16, k=zp + "p"), [[0, 16]])
        iota(o(zp, 176, 192, k=zp + "r"), [[0, 16]])
    iota(o("S1", 0, 272), [[0, 272]])
    iota(o("idtab", 0, 1, k="idz"), [[0, 1]], -1)

    def Fk(k):
        act(o("F", TN * k, TN * k + TN, k="F%d" % k), o("ramp", 0, TN), scale=cc("FS"), bias=o("Fb", k, k + 1))
    for k in range(N):
        Fk(k)
    ts(o("offr"), ind(Tz, selZ), -float(TN), add, 0.5 / TN, mul)
    side(ms, o("rs", 0, None, 16, k=("rs0",)), 0.0)
    side(ms, o("rs", R_SLOT, None, 16, k=("rs1",)), 0.0)
    side(tr, o("KU"), (K2, T.K2[:]))
    side(cp, o("nxo"), nxA)
    side(ts, cc("c2"), cc("c1"), float(BA - 1 - CAPP * (me + 1) - 15 - CAPP * (R_C0 - R_SLOT)), add, oh(R_C0), mul)
    side(ts, o("selL", 0, 1), SL, 0.125, mul)

    def own_codes(buf):
        for a_, b_ in ((0, 136), (136, 268), (268, BA)):
            quant(buf, a_, b_, "xt", ("xtx", "xtz"), "%s%d" % (buf, a_))
        return (buf + "0", buf + "136", buf + "268")
    xk = own_codes("x")
    side(ts, o("DT", 64, 65, k="DTb"), o("KU", 0, 1), -LIFT, add, cc("pr"), mul)
    side(tt, cc("KUc"), cc("c2"), o("KU", 0, 1), add)
    side(ts, o("selA"), o("ramp", 0, 32), B0, add)
    cp(o("G0"), ind(Fm, o("offr", 0, 10)))
    for _ in range(3):
        jobs.pop(0)[1]()
    act(cc("k3"), oh(R_C1), scale=ZC / K - BIG, bias=cc("k2"))
    act(o("strow"), ind(o("ramp"), o("offSt")))
    act(o("TAB", 1, 769, k="TABa"), ind(o("F", k=tuple("F%d" % k for k in range(N))), o("nxo")))
    for b in range(2):
        act(o("capT", 1 + b, 769, 2, k="capT%d" % b), o("ramp", 0, TN), scale=cc("cs"), bias=cc("k3"))
    act(o("capT", 0, 770, 769, k="capT2"), o("ramp", 0, 2), scale=0.0, bias=cc("k3"))
    act(o("Mt"), o("strow"), scale=cc("ms"), bias=cc("mb"))
    act(o("TAB", 0, 770, 769, k="TABz"), o("ramp", 0, 2), scale=0.0, bias=oh(R_OUT))
    offE, G1 = o("offE", 0, 10), o("G1")

    def entries():
        ts(o("offE"), ind(o("L1", k=("L1i", "L1m", "L1z")), o("selL", 0, 1)), float(-2 * TN * me), add, float(2 * TN + 1), mn)
        act(G1, ind(o("TAB", k=("TABa", "TABz")), offE), acc=o("x1"))

    scan(o("cn0"), o("G0"), o("G0"), cc("base0"), add, mx)
    halves(lambda z, a, b: tt(z, o("G0", a, b), o("cn0", a, b), mul), "zp0")
    turn("zp0")
    sums()
    cp(o("off0"), ind(SS, o("selB", R_OUT, R_OUT + 1)))
    scatter(o("S0"), o("off0", 0, 10), o("strow"))
    turn_slots("S0", 9)
    side(ts, o("mD", 32, 64, k="mD1"), o("ramp", 0, 32), P16, eq, cc("pr"), mul)
    side(tt, cc("in1"), cc("KUc"), o("DT", 64, 65, k="DTb"), sub)

    ki = ("offi",) + tuple("offi%d" % q for q in range(4) if 32 * q != Q)

    def caps():
        tt(o("cap1"), ind(o("capT", k=("capT0", "capT1", "capT2")), offE), o("Mt"), mul)

    def spread():
        for q in range(4):
            if 32 * q != Q:
                cp(o("offi", k="offi%d" % q, p=(32 * q, 32 * q + 32)), o("offi", p=PQ))

    def half(k, kind):
        a, b = ((0, 6), (6, 15))[k]
        pick("sl1", "x", (ki, T.offi[:, a:b]), xk, part=(16 * a, 16 * b), kinds=kind)

    def rest():
        columns(0, ("sl196",), "q", (2, 3, 4))

    def first():
        for kind in OPT["o1"]:
            if kind == "q" and OPT["early"]:
                columns(0, ("sl1", "sl196"), "q")
            elif kind == "q":
                columns(0, ("sl1",), "q", (0, 1))
            else:
                columns(0, ("sl1", "sl196"), "s")
    s0 = OPT["s0"]
    if OPT["pre"]:
        ts(o("D"), o("mD", k=("mD0", "mD1")), o("x1"), mul)
        cp(o("offi", k="offi"), ind(Ts, o("selA", 16 * (me % 2), 16 * (me % 2) + 1)))
        tr(o("DT", 0, 64), o("D"))
        spread()
        caps()
        pre = (("pre",), T.L2[:, me, 0:1])
        red(o("tot"), o("DT", 0, 32))
        red(pre, o("DT", 32, 65, k=("DT", "DTb")))
        half(0, "s")
        half(1, "s")
        scan(o("cn1"), G1, o("cap1"), cc("in1"), add, mn)
        ts((("pre1",), T.L2[32:64, me, 0:1]), (("pre",), T.L2[32:64, me, 0:1]), o("tot", p=(0, 32)), add)
        ts((("pre2",), T.L2[64:96, me, 0:1]), (("pre",), T.L2[64:96, me, 0:1]), o("tot", p=(0, 32)), add, o("tot", p=(32, 64)), add)
        pre = (("pre", "pre1", "pre2"), pre[1])
        tt(o("zl"), G1, o("cn1"), mul)
        half(0, "q")
        first()
        ts(o("zp1", 16, 176), o("zl"), pre, add, 0.0, mx)
        half(1, "q")
        rest()
        Ak = own_codes("A")
        s0 = None
    if s0 == 0:
        entries()
        while jobs:
            jobs.pop(0)[1]()
    if s0 is not None:
        cp(o("offi", k="offi"), ind(Ts, o("selA", 16 * (me % 2), 16 * (me % 2) + 1)))
    if s0 == 0:
        caps()
        if OPT["mvA"]:
            move("A", "x", 0, BA, xk, "Ax", "dxA")
            Ak = ("Ax",)
        else:
            Ak = own_codes("A")
        spread()
    if s0 == 0:
        ts(o("D"), o("mD", k=("mD0", "mD1")), o("x1"), mul)
        scan(o("cn1"), G1, o("cap1"), cc("in1"), add, mn)
        half(0, "s")
        half(1, "s")
        tr(o("DT", 0, 64), o("D"))
        half(0, "q")
        first()
        red(o("tot"), o("DT", 0, 32))
        pre = (("pre",), T.L2[:, me, 0:1])
        red(pre, o("DT", 32, 65, k=("DT", "DTb")))
        tt(o("zl"), G1, o("cn1"), mul)
        ts((("pre1",), T.L2[32:64, me, 0:1]), (("pre",), T.L2[32:64, me, 0:1]), o("tot", p=(0, 32)), add)
        ts((("pre2",), T.L2[64:96, me, 0:1]), (("pre",), T.L2[64:96, me, 0:1]), o("tot", p=(0, 32)), add, o("tot", p=(32, 64)), add)
        pre = (("pre", "pre1", "pre2"), pre[1])
        if not OPT["late"]:
            half(1, "q")
            rest()
        halves(lambda z, a, b: ts(z, o("zl", a, b), pre, add, 0.0, mx), "zp1")
        if OPT["late"]:
            half(1, "q")
            rest()
    side(ts, o("selP", 0, 1), B0b, float(R_LAND + me), add, 32.0 * NB - 1, mn)
    side(ts, o("jl"), r16, 16.0, mul, J, add)
    Bx = () if OPT["mvB"] else own_codes("B")
    for k in (4, 5, 3, 0, 1, 2):
        quant("w", 128 * k, 128 * k + 128, "wt", ("wt%d" % (k // 3),), "w%d" % k)
    turn("zp1")
    sums()
    cp((("L2o",), T.L2[:, me, 1:17]), ind(SS, o("selB", R_SLOT - 1, R_SLOT)))
    cp(o("off1"), ind(SS, o("selB", R_OUT, R_OUT + 1)))
    everyone(("L2o",) + pre[0], T.L2[:, me, 0:11], T.L2[:, me, 0:11], "am2")
    iota(o("idtab", 1, 961, k="idn"), [[0, N], [1, V]])
    act(cc("o34"), oh(R_C0), bias=oh(R_C1))
    act(cc("z1"), oh(R_LAND + me), bias=oh(R_ID))
    act(cc("es"), cc("o34"), scale=1.0 / K)
    act(cc("z2"), cc("o34"), scale=K, bias=cc("z1"))
    act(cc("p1"), cc("o34"), scale=float(BL))
    act(cc("z3"), oh(R_C2), scale=float(ZC), bias=cc("z2"))
    act(cc("p2"), oh(R_C1), scale=float(CAPP), bias=cc("p1"))
    act(cc("e1"), cc("o34"), scale=-BIG, bias=BIG)
    act(cc("i0"), G16, scale=V / 16.0)
    act(cc("e2"), oh(R_C2), scale=1.0 - BIG, bias=cc("e1"))
    act(cc("i2"), oh(R_LAND + me), scale=V + 15 + N * (1 + LIFT) - 96 * 15)
    act(o("ptab", 0, 480, k="pt0"), o("ramp"), scale=cc("o34"), bias=cc("p2"))
    act(cc("i3"), cc("i0"), scale=oh(R_ID), bias=cc("i2"))
    fill(o("ptab", 480, 736, k="pt1"), 256)
    low = me < N // 2
    at = TN * me + 1 if low else 1
    act(o("ztab", at, at + TN, k="zt0"), o("ramp", 0, TN), scale=oh(R_C2), bias=cc("z3"))
    zk = ("zt0",)
    for a_, b_ in ((0, at), (at + TN, at + TN + (1 if low else TN * (N - 1 - me)))):
        while a_ < b_:
            n_ = min(b_ - a_, 480)
            zk += ("zt%d" % (a_ + 1),)
            fill(o("ztab", a_, a_ + n_, k=zk[-1]), n_, oh(R_ID))
            a_ += n_
    fill(o("S2", V, V + 288), 288)
    act(o("E"), row("zp1"), scale=cc("es"), bias=cc("e2"))

    def product(k, oo, bank, n, keys, cols, first, last):
        a, wk = 128 * (k * NO + oo), "w%d" % (k * NO + oo)
        op("k", lambda: g.tensor.matmul_mx(T[bank][:, 0:cols], T.wq[:, a:a + 128], T.ws[:, a:a + 128], T[n + "q"][:], T[n + "s"][:], first, last),
           (wk + "q", wk + "s") + tuple(x + c for x in keys for c in "qs"), (bank,) if last else ())

    scatter(o("S1"), o("off1", 0, 10), row("zp1"))
    turn_slots("S1", 8)
    k2 = gather_lists("off2")
    PARTS = ((0, 1), (2, 3), (4,))
    sl2k = ("sl2", "sl2192", "sl2384")
    steps = [0]

    def third(k, kind):
        a, b = 6 * PARTS[k][0], 6 * PARTS[k][-1] + 6
        pick("sl2", "A", (k2, T.off2[:, a:b]), ("Al",) + Ak, part=(16 * a, 16 * b), kinds=kind)

    def step():
        k = steps[0] - OPT["at"]
        steps[0] += 1
        if 0 <= k < 3:
            third(k, "q")
            columns(1, sl2k[0:k + 1], "q", PARTS[k] if OPT["split"] else range(N) if k == 2 else ())
        if k == OPT["sat"]:
            columns(1, sl2k, "s")
    for k in range(3):
        third(k, "s")
    move("B", "A", 0 if OPT["mvB"] else BA, BL, ("Al",) + Ak, "Ba", "dAB")
    L2k = ("L2i", "L2o") + pre[0]
    step()
    tt((("L2h",), T.L2h[:]), (L2k + k2, T.L2[:, 0:3, 0:11]), (L2k, T.L2[:, 3:6, 0:11]), add)
    step()
    tt(o("L2a"), (("L2h",), T.L2h[:, 0, :]), (("L2h",), T.L2h[:, 1, :]), add)
    step()
    tt(o("vi", 0, 11), o("L2a"), (("L2h",), T.L2h[:, 2, :]), add)
    step()
    if low:
        ts(o("offN"), o("vi", 1, 11), 1.0 / K, mul, float(at + TN), mn)
    else:
        ts(o("offN"), o("vi", 1, 11), 1.0 / K, mul, float(-TN * me), add)
    ts(o("sli"), o("vi", 1, 11), int(K) - 1, band)
    ts(o("in2"), o("vi", 0, 1), oh(R_LAND + me), mul, cc("i3"), add)
    iota(o("idtab", 1, 961, k="idn", p=(0, 1)), [[1, N], [0, V]])
    cp(o("G2"), ind(o("ztab", k=zk), o("offN")))
    cp(o("offS"), o("sli"))
    scan(o("cn2"), o("G2"), o("E"), o("in2"), add, mn)
    halves(lambda z, a, b: tt(z, o("G2", a, b), o("cn2", a, b), mul), "zp2")
    turn("zp2")
    tt(o("cap2"), ind(o("ptab", k=("pt0", "pt1")), o("offS")), row("zp2"), mx)
    tt(o("off20"), ind(Tz, o("selP", 0, 1)), o("jl"), mx)
    scatter(o("S2"), o("off20", 0, 10), o("cap2"))
    for oo in range(NO):
        product(2, oo, "ps_%d" % (2 + oo), "x", xk, BA, True, True)
        act(o("R2%d" % oo), o("ps_%d" % (2 + oo), 0, BA))
    turn_slots("S2", 9, V)
    for n, row in enumerate((R_C0, R_ID)):
        cp(o("Ha", 32 * n, 32 * n + 32, k="Ha%d" % n), ind(Ts, o("selA", row, row + 2)))
    for n, row in enumerate((R_C0, R_ID)):
        tt(o("Hb", 32 * n, 32 * n + 32, k="Hb%d" % n), ind(Ts, o("selA", 16 + row, 18 + row)), o("Ha", 32 * n, 32 * n + 32, k="Ha%d" % n), add)
    for n in range(2):
        tt(o("tq", 32 * n, 32 * n + 32, k="tq%d" % n, p=(0, 64)), o("Hb", 32 * n, 32 * n + 32, k="Hb%d" % n, p=(0, 64)),
           o("Hb", 32 * n, 32 * n + 32, k="Hb%d" % n, p=(64, 128)), add)
    for h in range(4):
        tt(o("offF", 0, 32, k="offF%d" % h, p=(32 * h, 32 * h + 32)), o("tq", 0, 32, k="tq0", p=(0, 32)), o("tq", 0, 32, k="tq0", p=(32, 64)), add)
    tt(o("offF", 32, 64, k="offG0", p=(0, 32)), o("tq", 32, 64, k="tq1", p=(0, 32)), o("tq", 32, 64, k="tq1", p=(32, 64)), add)
    kF, kG = tuple("offF%d" % h for h in range(4)) + ("offG0",), tuple("offG%d" % h for h in range(4))
    Bk = Bx + ("Ba", "Bl")
    pick("p0", "B", (kF, T.offF[:, 0:16]), Bk)
    for oo in range(NO):
        product(0, oo, "ps_%d" % oo, "p0", ("p0",), M, True, False)
    for h in range(1, 4):
        cp(o("offF", 32, 64, k="offG%d" % h, p=(32 * h, 32 * h + 32)), o("offF", 32, 64, k="offG0", p=(0, 32)))
    pick("p1", "B", (kF, T.offF[:, 16:32]), Bk)
    for oo in range(NO):
        product(1, oo, "ps_%d" % oo, "p1", ("p1",), M, False, True)
    cp(o("r20"), ind(o("R20"), (kG, T.offF[:, 48:64])))
    act(o("r21"), ind(o("R21"), (kG, T.offF[:, 48:64])))
    act(o("idt"), ind(o("idtab", k=("idz", "idn")), (kG, T.offF[:, 32:48])))
    for oo in range(NO):
        tt(o("yo%d" % oo), o("ps_%d" % oo, 0, M), o("r2%d" % oo), add)
        dma("ys"[oo], (("y%d" % oo,), T.y[:, M * oo:M * oo + M]), o("yo%d" % oo), "dy%d" % oo)
    op("y", lambda: g.sync.dma_start(T["id"][:], T.idt[0:2, :]), ("idt",), ("ido",), sem="did", inc=16)
    for sem, c in count.items():
        if know["p"].get(sem, 0) < c:
            g.wait_ge(T.sem[sem], c)
